import numpy as np, ml_dtypes
CORES = [3,11,19,27,35,43,51,59]
N = 8
BF = ml_dtypes.bfloat16
def gentries(a):
    return np.ascontiguousarray(a.reshape(8, 16, -1).transpose(0, 2, 1)).reshape(8, -1)
def gtable(e):
    e = np.asarray(e); return np.ascontiguousarray(e.reshape(8, -1, 16).transpose(0, 2, 1)).reshape(128, -1).astype(np.int32)
V, U, S, C, RO = 256, 768, 10, 2, 3
X, M, NONE = V + U, N * V, N * V + U
def cut(p, c):
    return np.where(np.arange(S) < c[..., None], p, NONE)
def around(rng, o, j):
    j = np.minimum(j, o); m = np.maximum(S - 1 - j, 1)
    below = rng.integers(1, np.maximum(o // np.maximum(j, 1), 1) + 1); above = rng.integers(1, np.maximum((M - 1 - o) // m, 1) + 1)
    d = np.arange(S) - j[..., None]; x = o[..., None] + np.where(d < 0, below[..., None], above[..., None]) * d
    return np.where(x < M, x, NONE)
def hold(rng, o, lo, hi):
    n = hi - lo; d = np.sort(rng.integers(0, n - S + 1, o.shape + (S - 1,)), axis=-1) + np.arange(1, S)
    d = np.concatenate([np.zeros(o.shape + (1,), np.int64), d], axis=-1)
    return np.sort(lo + (o[..., None] - lo + d) % n, axis=-1)
def numbers_of():
    return np.arange(M).reshape(N, 1, V) + np.zeros((1, 8, 1), np.int64)
def parts(rng):
    size = rng.random((N, 8, X, 1)); low = rng.random((N, 8, X, 1)) * (1 - size)
    x = np.minimum((low + size * rng.random((N, 8, X, S))) * (M - S + 1), M - S).astype(np.int64)
    p = cut(np.sort(x, axis=-1) + np.arange(S), rng.integers(0, S + 1, (N, 8, X)))
    return p, rng.integers(0, NONE + 1, (N, 8, X)), rng.integers(0, NONE + 1, (N, 8, C, X)), rng.integers(0, NONE + 1, (N, 8, V)), rng.integers(0, NONE + 1, (N, 8, V))
def name(rng, p, xs):
    xs = np.array(xs)
    for r in range(N):
        for g in range(8):
            tab = np.concatenate([p[:, g, :V].reshape(M, S), p[r, g, V:]])
            place, slot = np.nonzero(tab // V == r); k = rng.permutation(len(place))
            new = np.array(xs[r, g]); new[tab[place[k], slot[k]] - r * V] = place[k]
            xs[r, g] = np.where(rng.random(V) < 0.65, new, xs[r, g])
    return xs
def pack(p, ld, cp, xs, ys):
    a = np.full((N, 8, 16, X), NONE, np.int32); a[:, :, :S] = p.transpose(0, 1, 3, 2)
    return {"pts": a.reshape(N, 128, X), "ld": np.stack([gtable(e) for e in ld]), "cp": np.stack([gtable(e.reshape(8, -1)) for e in cp]),
            "xs": np.stack([gtable(e) for e in xs]), "ys": np.stack([gtable(e) for e in ys])}
def setup_inputs(rng):
    p, ld, cp, xs, ys = parts(rng)
    return pack(p, ld, cp, name(rng, p, xs), ys)
def setup_inputs_alike(rng):
    p, ld, cp, xs, ys = parts(rng)
    own = np.stack([np.concatenate([r * V + np.arange(V), M + np.arange(U)]) for r in range(N)])
    p[:, 0, :V] = around(rng, numbers_of(), rng.integers(0, S, (N, 8, V)))[:, 0]
    ld[:, 0] = own; cp[:, 0] = own[:, None]; xs[:, 0] = own[:, :V]
    ld[:, 1] = rng.integers(0, M, (N, 1)); cp[:, 1] = rng.integers(0, M, (N, 1, 1)); xs[:, 1] = rng.integers(0, M, (N, 1)); ys[:, 1] = rng.integers(0, M, (N, 1))
    p[:, 2, :V] = around(rng, np.array([M // 3]), np.array([S // 2]))[0]
    ld[:, 3] = NONE; cp[:, 3] = NONE
    ld[:, 4] = rng.integers(M, M + U, (N, X))
    ld[:, 5] = rng.integers(0, V, (N, X)) + V * np.arange(N)[:, None]
    ld[:, 6] = rng.integers(0, V, (N, X)) + V * ((np.arange(N) + 1) % N)[:, None]
    cp[:, 7] = ld[:, 7][:, None]
    keep = name(rng, p, xs); xs[:, 2:] = keep[:, 2:]
    return pack(p, ld, cp, xs, ys)
def setup_inputs_chain(rng):
    p, ld, cp, xs, ys = parts(rng); p[:] = NONE; ld[:] = NONE; cp[:] = NONE; xs[:] = NONE
    h = M // 4; kind = rng.permutation(8)
    for g in kind[:4]:
        o = rng.permutation(M); hub, shelf, leaf, rest = o[:h], o[h:2 * h], np.sort(o[2 * h:3 * h]), o[3 * h:]
        p[leaf // V, g, leaf % V, 0] = np.sort(rng.permutation(M)[:h])
        pick = np.sort(rng.integers(0, h - S + 1, (h, S)), axis=1) + np.arange(S)
        p[shelf // V, g, shelf % V] = leaf[pick]
        p[hub // V, g, hub % V, 0] = leaf[pick[:, 0]]; cp[hub // V, g, C - 1, hub % V] = shelf
        ld[:, g, V:] = hub[rng.integers(0, h, (N, U))]; ld[rest // V, g, rest % V] = hub[rng.integers(0, h, len(rest))]
    for g in kind[4:6]:
        e = 2 * h; o = rng.permutation(e); hub, shelf = o[:h], o[h:]
        leaf = e + np.sort(rng.permutation(e - 1)[:h]); held = np.sort(rng.permutation(e)[:h])
        pick = np.sort(rng.integers(0, h - 2 * S + 2, (h, 2 * S - 1)), axis=1) + np.arange(2 * S - 1)
        i = rng.integers(0, h, (N, X)); ld[:, g] = hub[i]
        p[:, g, :, :S - 1] = held[pick[i][:, :, :S - 1]]
        p[leaf // V, g, leaf % V] = NONE; p[leaf // V, g, leaf % V, 0] = held; p[leaf // V, g, leaf % V, 1] = M - 1
        p[hub // V, g, hub % V] = leaf[pick[:, :S]]; cp[hub // V, g, C - 1, hub % V] = shelf
        p[shelf // V, g, shelf % V] = np.concatenate([leaf[pick[:, S:]], np.full((h, 1), M - 1)], axis=1)
    for g in kind[6:]:
        b = int(rng.integers(0, N)); b1 = (b + 1) % N; b2 = (b + 2) % N; half = U // 2
        p[b, g, V:] = np.sort(rng.integers(0, M - S + 1, (U, S)), axis=1) + np.arange(S)
        cp[b, g, C - 1, :V] = M + rng.integers(0, U, V)
        cp[b1, g, C - 1] = b * V + rng.integers(0, V, X)
        cp[b2, g, C - 1] = b1 * V + rng.integers(0, V, X)
        for d in range(3, N):
            q = (b + d) % N
            p[q, g, V:V + half, 0] = rng.integers(0, M, half)
            cp[q, g, C - 1, :V] = M + rng.integers(0, half, V)
            cp[q, g, C - 1, V + half:] = b1 * V + rng.integers(0, V, U - half)
    return pack(p, ld, cp, xs, ys)
def setup_inputs_ends(rng):
    p, ld, cp, xs, ys = parts(rng)
    e = np.full((8, S), NONE); e[1, 0] = 0; e[2, 0] = M - 1; e[3, :2] = (0, M - 1); e[4] = np.arange(S); e[5] = M - S + np.arange(S); e[6, :2] = (V - 1, V); e[7, 0] = 1
    p = np.where((rng.random((N, 8, X)) < 0.7)[..., None], e[rng.integers(0, 8, (N, 8, X))], p)
    ends = np.array([0, V - 1, V, M - 1, M, NONE - 1, NONE]); xs = name(rng, p, xs)
    ld, cp, ys = [np.where(rng.random(a.shape) < 0.4, ends[rng.integers(0, 7, a.shape)], a) for a in (ld, cp, ys)]
    xs = np.where(rng.random(xs.shape) < 0.3, ends[rng.integers(0, 7, xs.shape)], xs)
    return pack(p, ld, cp, xs, ys)
def full_stores(rng, g, p, ld, cp, xs, ys):
    b = N - 1; low = M - V; to = rng.permutation(V)
    hr = (np.arange(b)[:, None] + rng.integers(1, b)) % b
    ld[:, g, :2 * V] = NONE; cp[:, g, :, :2 * V] = NONE
    p[hr, g, to] = hold(rng, np.arange(low).reshape(b, V), 0, low); xs[:b, g] = hr * V + to
    p[b, g, :V] = hold(rng, low + np.arange(V), low, M); ys[:b, g] = low + rng.integers(0, V, (b, V))
    xs[b, g] = rng.integers(0, low, V); ys[b, g] = rng.integers(0, low, V)
    nx = np.append((np.arange(b) + 1) % b, 0)
    p[:, g, V:2 * V] = p[nx, g, :V]; cp[:, g, C - 1, V:2 * V] = nx[:, None] * V + np.arange(V)
def late_names(rng, g, p, ld, cp, xs, ys):
    H = V // 3; Q = (V - 2 * H) // 2; ra = np.arange(N)[:, None]; k = np.arange(H)
    pm = np.concatenate([1 + np.argsort(rng.random((N, V - 1)), axis=1), np.zeros((N, 1), np.int64)], axis=1)
    namer, quiet, source = pm[:, :H], pm[:, 2 * H:2 * H + Q], pm[:, 2 * H + Q:]
    ld[:, g, :V + H] = NONE; cp[:, g, :, :V + H] = NONE; ld[:, g, X - 1] = NONE; cp[:, g, :, X - 1] = NONE; xs[:, g] = NONE
    far = (ra + np.where(k // (RO - 1) % 2 == 1, rng.integers(1, N, H), 0)) % N
    feed = around(rng, ra * V + namer, k % (RO - 1)); hv = pm[far, H + k]; low = feed[..., 0]
    p[far, g, V + k] = feed; cp[far, g, C - 1, hv] = M + k + np.zeros((N, 1), np.int64)
    p[far, g, hv] = NONE; p[far, g, hv, 0] = np.where((low > 0) & (rng.random(low.shape) < 0.5), low - 1, NONE)
    xs[ra, g, namer] = far * V + hv
    p[ra, g, source] = hold(rng, ra * V + source, 0, M)
    p[0, g, 0] = np.sort(rng.permutation((ra * V + quiet).reshape(-1))[:S])
    p[:, g, X - 1] = np.sort(ra * V + quiet[:, :S], axis=1)
    ask = np.concatenate([namer, quiet], axis=1); away = (ra + rng.integers(1, N, ask.shape)) % N
    sv = source[away, rng.integers(0, source.shape[1], ask.shape)]
    ys[ra, g, ask] = away * V + sv
    p[ra, g, ask] = cut(p[away, g, sv], rng.integers(0, S, ask.shape))
def setup_inputs_stores(rng):
    p, ld, cp, xs, ys = parts(rng); o = numbers_of(); sh = (N, 8, V)
    case = rng.integers(0, 4, sh); mid = np.where(case == 2, np.where(o + 1 < M, o + 1, 0), o)
    x = around(rng, mid, np.where(case == 1, S - 1, 0))
    p[:, :, V:2 * V] = np.where((case == 3)[..., None], NONE, x)
    ld[:, :, V:2 * V] = np.where(case == 3, NONE, ld[:, :, V:2 * V]); cp[:, :, :, V:2 * V] = NONE
    cp[:, :, 0, V:2 * V] = np.where(case == 3, (o + V) % M, NONE)
    j = rng.integers(0, RO, sh); k = around(rng, o, j)
    k = cut(k, np.where(rng.random(sh) < 0.5, np.minimum(j, o) + 1, S)); p[:, :, :V] = np.roll(k, 1, axis=0)
    quiet = rng.random(sh) < 0.5
    ld[:, :, :V] = np.where(quiet, NONE, ld[:, :, :V]); cp[..., :V] = np.where(quiet[:, :, None], NONE, cp[..., :V])
    xs = M + np.arange(V) + np.zeros(sh, np.int64)
    kind = [int(g) for g in rng.permutation(8)]
    for g in kind[:2]: full_stores(rng, g, p, ld, cp, xs, ys)
    for g in kind[2:4]: late_names(rng, g, p, ld, cp, xs, ys)
    return pack(p, ld, cp, xs, ys)
def setup_inputs_spread(rng):
    p, ld, cp, xs, ys = parts(rng)
    x = np.minimum(np.exp2(np.log2(M - S + 1) * rng.random((N, 8, X, S))).astype(np.int64) - 1, M - S)
    x = np.sort(x, axis=-1) + np.arange(S); x = np.where(rng.random((N, 8, X, 1)) < 0.35, (M - 1 - x)[..., ::-1], x)
    p = cut(x, np.minimum((rng.random((N, 8, X)) ** 2 * (S + 1)).astype(np.int64), S))
    ld, cp, xs, ys = [np.minimum((rng.random(a.shape) ** 3 * (NONE + 1)).astype(np.int64), NONE) for a in (ld, cp, xs, ys)]
    return pack(p, ld, cp, name(rng, p, xs), ys)
def check_inputs(d):
    bad = []
    a = np.asarray(d["pts"]).reshape(N, 8, 16, X); h = a[:, :, :S]
    if not np.all(((h >= 0) & (h < M)) | (h == NONE)): bad.append("range of pts")
    if not np.all((h[:, :, 1:] > h[:, :, :-1]) | (h[:, :, 1:] == NONE)): bad.append("pts rises")
    if not np.all(a[:, :, S:] == NONE): bad.append("later slots of pts")
    for k in ("ld", "cp", "xs", "ys"):
        if np.min(d[k]) < 0 or np.max(d[k]) > NONE: bad.append("range of " + k)
    return bad
def reference(pts, ld, cp, xs, ys):
    p = pts.astype(np.int64).reshape(N, 8, 16, X)
    lds, cps, xss, yss = [np.stack([gentries(a) for a in b]).astype(np.int64) for b in (ld, cp, xs, ys)]
    cps = cps.reshape(N, 8, C, X)
    def take(w, ix):
        return np.take_along_axis(w, ix[:, None, :], 2)
    for t in range(RO):
        objects = np.concatenate([p[q, :, :, :V] for q in range(N)], axis=2); gain = []
        for a in range(N):
            w = np.concatenate([objects, p[a, :, :, V:], np.full((8, 16, 1), NONE)], axis=2)
            top = np.max(np.where(p[a] == NONE, -1, p[a]), axis=1)[:, None, :]
            best = np.full((8, X), NONE)
            edge = take(w, lds[a])
            for i in range(S + t):
                s = take(w, edge[:, i]); best = np.minimum(best, np.min(np.where(s > top, s, NONE), axis=1))
            for c in range(C):
                s = take(w, cps[a, :, c]); best = np.minimum(best, np.min(np.where(s > top, s, NONE), axis=1))
            named = np.any(take(w, xss[a]) == a * V + np.arange(V), axis=1)[:, None, :]
            s = take(w, yss[a]); s = np.min(np.where(named & (s > top[:, :, :V]), s, NONE), axis=1)
            best[:, :V] = np.minimum(best[:, :V], s); gain.append(best)
        p[:, :, S + t] = np.stack(gain)
    return {"yp": p.reshape(N, 128, X).astype(np.float32)}

@@ -1,0 +1,520 @@
+from concourse.bass import DstId, RemoteDMATransfer
+from concourse.mybir import AluOpType as ALU, ActivationFunctionType as ACT
+
+N, V, X, M, NONE = 8, 256, 1024, 2048, 2816
+TMP = M + 16
+WIN = TMP + (X - V) + 1
+EWIN = M + 1
+BIG = 1.0e6
+HALF = 0.4375
+KK = 65536.0
+NBANK = 8
+
+
+def _sb(n, d): return ("sbuf", [128, n], d)
+
+
+SCRATCH = {}
+for _d, _l in (
+    ("int32", dict(PI=X, LI=224, LM=224, HI=X, GI=64, CI=4)),
+    ("uint16", dict(LU=224, O=640, ON1=64, ON2=64)),
+    ("float32", dict(OUT=X, SS=8448, SO=8448, U=384, SL=3200, SY=320, AX=160, SX=160, NM=16, NB=16, PY=16, T0=64, T1=64, T2=64, TOP=64,
+                     DT=80, DU=88, X128=128, X80=80, X88=88, CF=8, TB=12, OWN=2)),
+    ("bfloat16", dict(W0=2848, D1=2848, D2=2848, GE0=10240, GE1=10240, GE2=10240, GC0=2560, GC1=2560, GC2=2560, GN1=X, GN2=X,
+                      GD11=X, GD21=X, GD22=X, GL1=X, GL2=X, A=X, B=X, Z=512, ID=128, EH=128, EL=128, PK=1536, DEC=80, D88=88, K88=88,
+                      R88=88, DD=16, OT1=V, OT2=V, SEL1=2048, SEL2=2048, R60=480, R50=400, R30=240, RY1=160, RY2=160, P60=480, P50=400, P10=320)),
+):
+    for _k in _l: SCRATCH[_k] = _sb(_l[_k], _d)
+for _k in range(NBANK):
+    SCRATCH["MK%d" % _k] = _sb(400, "bfloat16")
+    SCRATCH["PS%d" % _k] = ("psum", [128, 512], "float32")
+
+NDMA = 20
+SEMAPHORES = ["cv", "cs", "cp", "cg"] + ["arr%d" % t for t in range(3)] + ["snt%d" % t for t in range(3)] + ["dm%d" % k for k in range(NDMA)]
+
+CYC, PCYC, GATH, LAT = 1.04, 0.55, 1.56, 180.0
+DMA_NS, NET_NS = 2300.0, 9000.0
+STATIC_GROUPS = [(0, 2), (2, 5), (5, 8)]
+ROUND_GROUPS = [(0, 2), (2, 8)]
+FINAL_GROUPS = [(0, 2), (2, 5), (5, 8)]
+URGENT, AHEAD = 4000.0, 0.5
+BIAS, SLACK = 500.0, 60.0
+BONUS = {'arr1': 18000, 'arr2': 33400, 'SS1': 3600, 'SO3': 3800, 'SY1': 7600, 'SO1.2.30.': 2600, 'NB1': 2000, 'SS1.5.35.': 5000, 'job1.14.': 400,
+         'T13.2.': -1400, 'SO3.5.20.': 8000, 'O1': 2000, 'E1.1.': 5000, 'GC3.2.0.': 3400, 'GI3.5.': -11000, 'job2.89.': 3000, 'GL3': 1400,
+         'GI3': 600, 'GC2': 9000, 'job2.60.': -4000, 'job3.110.': -8000, 'OT2.2.': 8000, 'T02.0.': 400, 'SO2.5.35.': -3000, 'SO1.5.10.': -3000,
+         'SO1.2.20.': -8000}
+
+
+def plan(T, topo, rank, core):
+    ops, lastw, readers = [], {}, {}
+    rnd, njob = [0], [0]
+
+    def op(eng, dur, fn, rd=(), wr=(), job=None, kind="c", lat=0.0):
+        deps = {}
+        rd = list(rd); wr = list(wr)
+        if job is not None:
+            wr.append(("job", job[0])); rd.append(("job", job[0]))
+        for k in rd:
+            if k in lastw: deps[lastw[k]] = True
+        for k in wr:
+            if k in lastw: deps[lastw[k]] = True
+            for r in readers.get(k, []): deps[r] = True
+        i = len(ops)
+        for k in rd: readers.setdefault(k, []).append(i)
+        for k in wr: lastw[k] = i; readers[k] = []
+        k = wr[0] if wr else "out"
+        cls = "%s%d" % (k if isinstance(k, str) else k[0], rnd[0])
+        ops.append({"eng": eng, "dur": dur, "fn": fn, "deps": deps, "job": job, "kind": kind, "lat": lat, "after": None, "f": 1.0,
+                    "cls": cls, "fine": cls if isinstance(k, str) else cls + "".join("." + str(x) for x in k[1:])})
+        if job is not None: job[1].append(i)
+
+    def alias(new, old):
+        for k in new:
+            readers[k] = readers.get(k, []) + [i for x in old for i in readers.get(x, []) + [lastw[x]]]
+
+    def newjob():
+        njob[0] += 1
+        return [njob[0], [], None]
+
+    def ps(job): return T["PS%d" % job[2]]
+    def mk(job): return T["MK%d" % job[2]]
+    def gt(n): return 200 + 2 * n * CYC
+
+    def vec(name, n, rd, wr, args, f=1.0, job=None):
+        calls = {"ts": lambda q, a: q.tensor_scalar(*a), "tt": lambda q, a: q.tensor_tensor(*a), "cp": lambda q, a: q.tensor_copy(*a),
+                 "ms": lambda q, a: q.memset(*a), "scan": lambda q, a: q.tensor_tensor_scan(*a)}
+        op("V", max(64, n * f) * CYC + 20, lambda e, q: [calls[name](q, args())], rd, wr, job)
+
+    def act(n, rd, wr, args, job=None):
+        def fn(e, q):
+            a = args()
+            return [q.activation(a[0], a[1], a[2], bias=a[3], scale=a[4])]
+        op("S", n * CYC + 70, fn, rd, wr, job)
+
+    def move(n, rd, wr, args, job=None, f=1.0, fix=0.0):
+        def fn(e, q):
+            o, i = args()
+            return [q.tensor_copy(o, i) if e == "V" else q.activation(o, i, ACT.Copy)]
+        op("VS", {"V": max(64, n * f) * CYC + 20 + fix, "S": n * f * CYC + 70}, fn, rd, wr, job)
+        ops[-1]["f"] = f
+
+    def gather(out, w, off, n, rd, wr):
+        move(n, rd, wr, lambda: (out, w.indirect(off)), f=GATH, fix=30)
+
+    def mm(items, rd, job):
+        dur = sum(max(64, x[5]) for x in items) * PCYC + 60
+        op("P", dur, lambda e, q: [q.matmul(ps(job)[:, c], l, r, a, b) for (c, l, r, a, b, _) in items], rd, [], job)
+
+    def sel(out, in_, pat, cmp, fill, base, cm, n, rd, wr):
+        op("G", gt(n), lambda e, q: [q.affine_select(out, in_, pat, cmp, fill, base, cm)], rd, wr)
+
+    def iota(out, pat, base, cm, n, wr, flag=True):
+        if flag: op("G", gt(n), lambda e, q: [q.iota(out, pat, base, cm, allow_small_or_imprecise_dtypes=True)], [], wr)
+        else: op("G", gt(n), lambda e, q: [q.iota(out, pat, base, cm)], [], wr)
+
+    def dma(eng, out, in_, rd, wr, extra=0.0):
+        op(eng, 80.0, lambda e, q: [q.dma_start(out, in_)], rd, wr, kind="dma", lat=DMA_NS + extra)
+
+    HB, LB, E, D0, SL = T.GL1, T.GL2, T.GN2, T.GD22, T.SL
+    own0 = rank * V
+    def wcol(b): return own0 + 128 * b if b < 2 else TMP + 128 * (b - 2)
+    def win(t): return [T.W0, T.D1, T.D2][t]
+    def wkey(t, b): return ("win", t, b)
+    def objkeys(t): return [wkey(t, 0), wkey(t, 1), ("arr", t), ("none", t)]
+    def allkeys(t): return objkeys(t) + [("pad", t)] + [wkey(t, b) for b in range(2, 8)]
+
+    def send(t):
+        src = win(t)[:, own0:own0 + V]
+        def fn(e, q):
+            trs = []
+            at = 0
+            for d in range(1, N):
+                dst = T.cores[(rank + d) % N]
+                eng = topo.engines(core, dst)
+                k = len(eng) - (N - 2) if d == 1 else 1
+                mask = sum(1 << x for x in eng[at:at + k]); at += k
+                rid, pid = topo.addr(dst)[:2]
+                trs.append(RemoteDMATransfer(dst_ids=[DstId(rid=rid, pnc=pid)], dma_engine_mask=mask, remote_sem=T.sem["arr%d" % t], src=src, dst=src))
+            q.remote_dma_fused(trs, local_sem=T.sem["snt%d" % t])
+            return []
+        op("G", 300.0, fn, [wkey(t, 0), wkey(t, 1)], [("arr", t)], kind=("net", t), lat=NET_NS)
+
+    dma("Y", T.PI[:, 0:V], T.pts[:, 0:V], [], ["PIo"])
+    dma("S", T.PI[:, V:X], T.pts[:, V:X], [], ["PIt"], 500)
+    dma("Y", T.LI[:, 0:16], T.xs[:, :], [], ["LI0"])
+    dma("Y", T.LI[:, 16:32], T.ys[:, :], [], ["LI1"])
+    dma("Y", T.LI[:, 32:160], T.cp[:, :], [], ["LI2"])
+    dma("Y", T.LI[:, 160:224], T.ld[:, :], [], ["LI3"])
+
+    vec("ms", 512, [], ["Z"], lambda: (T.Z[:, :], 0.0), 0.5)
+    ne, ge = ALU.not_equal, ALU.is_ge
+    sel(T.EL[:, :], T.Z[:, 0:128], [[16, 8], [2, 16]], ne, 1.0, -20, -1, 128, ["Z"], ["EL"])
+    sel(T.EL[:, :], T.EL[:, :], [[16, 8], [2, 16]], ne, 8.0, -19, -1, 128, ["EL"], ["EL"])
+    sel(T.EL[:, :], T.EL[:, :], [[0, 8], [1, 16]], ge, 0.0, -10, 0, 128, ["EL"], ["EL"])
+    sel(T.EL[:, :], T.EL[:, :], [[16, 8], [2, 8], [1000, 2]], ne, -8.0, 1, -1, 128, ["EL"], ["EL"])
+    sel(T.ID[:, :], T.Z[:, 0:128], [[1, 128]], ne, 1.0, 0, -1, 128, ["Z"], ["ID"])
+    sel(T.EH[:, :], T.ID[:, :], [[0, 8], [-1, 16]], ge, 0.0, 9, 0, 128, ["ID"], ["EH"])
+    iota(T.CI[:, 0:1], [[0, 1]], 0, 1, 1, ["CI0"], False)
+    iota(T.X128[:, :], [[64, 8], [1, 16]], 0, 0, 128, ["X128"])
+    iota(T.X80[:, :], [[64, 8], [1, 10]], 0, 0, 80, ["X80"])
+    iota(T.TB[:, :], [[-2, 12]], 8, 0, 12, ["TB"])
+    later = len(ops)
+    iota(T.X88[:, :], [[64, 8], [1, 11]], -1, 0, 88, ["X88"])
+    sel(T.R88[:, :], T.Z[:, 0:88], [[16, 8], [0, 11]], ne, KK, 5, -1, 88, ["Z"], ["R88"])
+    sel(T.R88[:, :], T.R88[:, :], [[16, 8], [0, 11]], ne, KK, 6, -1, 88, ["R88"], ["R88"])
+    sel(T.R88[:, :], T.R88[:, :], [[16, 8], [0, 11]], ne, 0.9375 * KK, 7, -1, 88, ["R88"], ["R88"])
+    sel(T.R88[:, :], T.R88[:, :], [[16, 8], [1000, 11]], ne, 2.0 * KK, 7, -1, 88, ["R88"], ["R88"])
+    iota(T.OWN[:, :], [[-128, 2]], -own0, -1, 2, ["OWN"])
+    for (buf, L) in ((T.R60, 60), (T.R50, 50)):
+        key = "R%d" % L
+        sel(buf[:, :], T.Z[:, 0:8 * L], [[16, 8], [0, L]], ne, -1.0, 5, -1, 8 * L, ["Z"], [key])
+        sel(buf[:, :], buf[:, :], [[16, 8], [0, L]], ne, -1.0, 6, -1, 8 * L, [key], [key])
+    sel(T.DD[:, :], T.Z[:, 0:16], [[16, 8], [1, 2]], ne, 1.0, 10, -1, 16, ["Z"], ["DD"])
+    sel(T.DD[:, :], T.DD[:, :], [[16, 8], [1, 2]], ne, 1.0, 2, -1, 16, ["DD"], ["DD"])
+    for t in (1, 2):
+        for j in range(4):
+            part = T["SEL%d" % t][:, 512 * j:512 * j + 512]; key = ("SEL", t, j)
+            sel(part, T.Z[:, :], [[-200, 4], [16, 8], [200, 16]], ne, 1.0, 9 + t - 800 * j, -1, 512, ["Z"], [key])
+            sel(part, part, [[-200, 4], [16, 8], [200, 16]], ne, 1.0, 1 + t - 800 * j, -1, 512, [key], [key])
+    sel(T.R50[:, :], T.R50[:, :], [[0, 16], [-1, 25]], ge, 0.0, 23, 0, 400, ["R50"], ["R50"])
+    sel(T.R30[:, :], T.R60[:, 0:480:2], [[0, 8], [-1, 10], [-10, 3]], ge, 0.0, 22, 0, 240, ["R60"], ["R30"])
+    sel(T.RY1[:, :], T.R60[:, 0:480:3], [[0, 8], [-1, 10], [-10, 2]], ge, 0.0, 10, 0, 160, ["R60"], ["RY1"])
+    sel(T.RY2[:, :], T.R60[:, 0:480:3], [[0, 16], [-1, 5], [-10, 2]], ge, 0.0, 10, 0, 160, ["R60"], ["RY2"])
+    for (buf, L, n) in ((T.P60, 60, 480), (T.P50, 50, 400), (T.P10, 10, 320)):
+        sel(buf[:, :], T.Z[:, 0:n], [[0, n // L], [1, L]], ne, BIG, 0, 0, n, ["Z"], ["P%d" % L])
+    for h in range(2):
+        bl = range(4 * h, 4 * h + 4)
+        sel(T.A[:, 512 * h:512 * h + 512], T.Z[:, :], [[0, 32], [1, 16]], ne, 1.0, -7, 0, 512, ["Z"], [("A", b) for b in bl])
+        iota(T.B[:, 512 * h:512 * h + 512], [[0, 512]], 0, 0, 512, [("B", b) for b in bl])
+    for t in range(3): iota(win(t)[:, M + 1:TMP], [[0, 15]], 0, 0, 15, [("pad", t)])
+    late = range(later, len(ops))
+    CI, CF = T.CI, T.CF
+    vec("ts", 1, ["CI0"], ["CI1"], lambda: (CI[:, 1:2], CI[:, 0:1], 15, None, ALU.bitwise_and))
+    vec("ts", 1, ["CI0"], ["CI2"], lambda: (CI[:, 2:3], CI[:, 0:1], 4, None, ALU.arith_shift_right))
+    vec("cp", 2, ["CI1", "CI2"], ["CF0"], lambda: (CF[:, 0:2], CI[:, 1:3]))
+    vec("ts", 1, ["CF0"], ["CF2"], lambda: (CF[:, 2:3], CF[:, 0:1], 10.0, None, ge))
+    vec("ts", 1, ["CF0", "CF2"], ["CF3"], lambda: (CF[:, 3:4], CF[:, 0:1], -19.9375, CF[:, 2:3], ALU.add, ALU.mult))
+    vec("ts", 1, ["CF0"], ["CF4"], lambda: (CF[:, 4:5], CF[:, 1:2], 64.0, CF[:, 0:1], ALU.mult, ALU.add))
+    vec("ts", 12, ["TB", "CF3", "CF4"], ["TB"], lambda: (T.TB[:, :], T.TB[:, :], CF[:, 3:4], CF[:, 4:5], ALU.subtract, ALU.subtract))
+    vec("ts", 1, ["CF2"], ["CF5"], lambda: (CF[:, 5:6], CF[:, 2:3], 0.0625, 1.0, ALU.mult, ALU.add))
+    vec("ts", 2, ["OWN"], ["OWN"], lambda: (T.OWN[:, :], T.OWN[:, :], -HALF, None, ALU.add))
+    for j in range(12):
+        act(128, ["X128", "TB"], [("PT", j)], lambda j=j: (SL[:, 128 * j:128 * j + 128], T.X128[:, :], ACT.Abs, T.TB[:, j:j + 1], 1.0))
+    for j in range(3):
+        act(512, [("PT", 4 * j + i) for i in range(4)] + ["CF5"], [("PK", 4 * j + i) for i in range(4)],
+            lambda j=j: (T.PK[:, 512 * j:512 * j + 512], SL[:, 512 * j:512 * j + 512], ACT.Relu, CF[:, 5:6], -1.0))
+    act(80, ["X80", "TB"], ["DT"], lambda: (T.DT[:, :], T.X80[:, :], ACT.Abs, T.TB[:, 4:5], 1.0))
+    act(80, ["DT", "CF5"], ["DEC"], lambda: (T.DEC[:, :], T.DT[:, :], ACT.Relu, CF[:, 5:6], -1.0))
+    act(88, ["X88", "TB"], ["DU"], lambda: (T.DU[:, :], T.X88[:, :], ACT.Abs, T.TB[:, 4:5], 1.0))
+    act(88, ["DU", "CF5"], ["D88"], lambda: (T.D88[:, :], T.DU[:, :], ACT.Relu, CF[:, 5:6], -1.0))
+    act(88, ["D88"], ["K88"], lambda: (T.K88[:, :], T.D88[:, :], ACT.Identity, 0.0, -KK))
+    vec("ts", 1, ["CF2"], ["CF6"], lambda: (CF[:, 6:7], CF[:, 2:3], -float(NONE), float(NONE), ALU.mult, ALU.add))
+    vec("ts", 1, ["CF2"], ["CF7"], lambda: (CF[:, 7:8], CF[:, 2:3], float(NONE), None, ALU.mult))
+    for t in range(3):
+        k = 7 if t else 6
+        vec("ts", 2, ["Z", "CF%d" % k], [("none", t)], lambda t=t, k=k: (win(t)[:, M:WIN:WIN - 1 - M], T.Z[:, 0:2], CF[:, k:k + 1], None, ALU.add))
+    off1 = [3 * a + 1 for a in range(10)] + [2, 5, 8]
+    off2 = [o for o in range(25) if o % 5 >= 2]
+
+    for (c0, c1, pk) in ((0, V, "PIo"), (V, 640, "PIt"), (640, X, "PIt")):
+        n = c1 - c0; bl = range(c0 // 128, c1 // 128)
+        vec("ts", n, [pk], [("HI", c0)], lambda c0=c0, c1=c1: (T.HI[:, c0:c1], T.PI[:, c0:c1], 4088, None, ALU.bitwise_and))
+        vec("cp", n, [("HI", c0)], [("HB", c0)], lambda c0=c0, c1=c1: (HB[:, c0:c1], T.HI[:, c0:c1]))
+        vec("tt", n, [("HI", c0), pk], [("LB", c0)], lambda c0=c0, c1=c1: (LB[:, c0:c1], T.PI[:, c0:c1], T.HI[:, c0:c1], ALU.subtract), 2.0)
+        job = newjob()
+        mm([(slice(0, n), T.EH[:, :], HB[:, c0:c1], True, False, n), (slice(0, n), T.EL[:, :], LB[:, c0:c1], False, True, n)],
+           ["EH", "EL", ("HB", c0), ("LB", c0)], job)
+        w = wcol(c0 // 128)
+        move(n, [], [wkey(0, b) for b in bl], lambda job=job, w=w, n=n: (T.W0[:, w:w + n], ps(job)[:, 0:n]), job)
+        if c0 == 0:
+            send(0)
+            for i in late: ops[i]["after"] = len(ops) - 1
+    vec("cp", X, ["PIo", "PIt"], ["OUT"], lambda: (T.OUT[:, :], T.PI[:, :]))
+    dma("Y", T.yp[:, :], T.OUT[:, :], ["OUT"], ["yp"], 1500)
+
+    lk = ["LI0", "LI1", "LI2", "LI3"]
+    vec("ts", 224, lk, ["LM"], lambda: (T.LM[:, :], T.LI[:, :], float(M), 16.0, ge, ALU.mult))
+    vec("tt", 224, lk + ["LM"], ["LM"], lambda: (T.LM[:, :], T.LM[:, :], T.LI[:, :], ALU.add), 2.0)
+    for (d, s, n) in ((0, 0, 48), (48, 96, 16), (64, 48, 48), (112, 112, 112)):
+        vec("cp", n, ["LM"], [("LU", d)], lambda d=d, s=s, n=n: (T.LU[:, d:d + n], T.LM[:, s:s + n]))
+    luk = [("LU", d) for d in (0, 48, 64, 112)]
+    def cpcol(c, b): return (512 + 256 * c + 128 * b) if b < 2 else (1024 + 768 * c + 128 * (b - 2))
+    def cpkey(t, c, b): return ("GC", t, 0 if b < 2 else 1 + c)
+
+    def finish_top(b0, b1):
+        n = 8 * (b1 - b0); c = slice(8 * b0, 8 * b1); ak = [("A", b) for b in range(b0, b1)]; tk = [("TOP", b) for b in range(b0, b1)]
+        hi = T.A[:, 128 * b0 + 5:128 * b1:16]
+        vec("cp", n, tk, ak, lambda: (hi, T.TOP[:, c]))
+        vec("tt", n, tk + ak, ak, lambda: (T.A[:, 128 * b0 + 6:128 * b1:16], T.TOP[:, c], hi, ALU.subtract), 2.0)
+
+    def turn_back(t, b0, b1, tops=False):
+        parts = [(b0, b1)] if b1 - b0 <= 4 else [(b0, (b0 + b1) // 2), ((b0 + b1) // 2, b1)]
+        for (p0, p1) in parts:
+            job = newjob(); items = []; rd = ["ID"]
+            for b in range(p0, p1):
+                c = slice(128 * (b - p0), 128 * (b - p0 + 1)); rd.append(("A", b))
+                items.append((c, T.A[:, 128 * b:128 * b + 128], T.ID[:, :], True, t < 3, 128))
+                if t == 3:
+                    items.append((c, T.B[:, 128 * b:128 * b + 128], T.ID[:, :], False, True, 128)); rd.append(("B", b))
+            mm(items, rd, job)
+            n = 128 * (p1 - p0)
+            if t == 0: dst = D0[:, 128 * p0:128 * p1]; wr = [("D0", b) for b in range(p0, p1)]
+            elif tops: dst = T["OT%d" % t][:, :]; wr = [("OT", t)]
+            elif t < 3: dst = win(t)[:, wcol(p0):wcol(p0) + n]; wr = [wkey(t, b) for b in range(p0, p1)]
+            else: dst = T.OUT[:, 128 * p0:128 * p1]; wr = [("OUT2", b) for b in range(p0, p1)]; alias(wr, ["yp"])
+            move(n, [], wr, lambda job=job, dst=dst, n=n: (dst, ps(job)[:, 0:n]), job)
+        if t == 3:
+            for k in range(3):
+                dma("YGS"[k], T.yp[10 + k:128:16, 128 * b0:128 * b1], T.OUT[10 + k:128:16, 128 * b0:128 * b1],
+                    [("OUT2", b) for b in range(b0, b1)] + ["yp"], [])
+
+    for h in range(2):
+        job = newjob(); bl = range(4 * h, 4 * h + 4)
+        mm([(slice(80 * i, 80 * i + 80), T.W0[:, wcol(b):wcol(b) + 128], T.DEC[:, :], True, True, 80) for i, b in enumerate(bl)],
+           ["DEC"] + [wkey(0, b) for b in bl], job)
+        a = SL[:, 1536 + 320 * h:1856 + 320 * h]; s = SL[:, 2176 + 320 * h:2496 + 320 * h]
+        ka = [("TA", h)]; kb = [("TS", h)]; tk = [("TOP", b) for b in bl]; gk = [("GI", b) for b in bl]
+        c = slice(32 * h, 32 * h + 32)
+        vec("ts", 320, [], ka, lambda job=job, a=a: (a, ps(job)[:, 0:320], 2500.0, 4000.0, ge, ALU.mult), job=job)
+        vec("tt", 320, ka, ka, lambda job=job, a=a: (a, a, ps(job)[:, 0:320], ALU.subtract), job=job)
+        vec("scan", 320, ka + ["P10"], kb, lambda a=a, s=s: (s, T.P10[:, :], a, 0.0, ALU.add, ALU.min))
+        vec("ts", 32, kb, gk, lambda h=h, c=c: (T.GI[:, c], SL[:, 2185 + 320 * h:2496 + 320 * h:10], -1.0, -HALF, ALU.mult, ALU.add))
+        vec("ts", 32, gk, tk, lambda c=c: (T.TOP[:, c], T.GI[:, c], -1.0, None, ALU.max))
+        finish_top(4 * h, 4 * h + 4)
+        turn_back(0, 4 * h, 4 * h + 4)
+
+    def topl(t, b):
+        if t and b < 2: return T["OT%d" % t][:, 128 * b:128 * b + 128], ("OT", t)
+        return (D0[:, 128 * b:128 * b + 128], ("D0", b)) if t == 0 else (win(t)[:, wcol(b):wcol(b) + 128], wkey(t, b))
+
+    def least(t, b, n, rtop, rkey, items, rd, pat, pkey, out, okey):
+        job = newjob(); l, lk_ = topl(t, b)
+        its = [(slice(0, n), l, rtop, True, False, n)] + [(c, a, r, False, x == len(items) - 1, k) for x, (c, a, r, k) in enumerate(items)]
+        mm(its, rd + [lk_, rkey], job)
+        act(n, [], [], lambda: (mk(job)[:, 0:n], ps(job)[:, 0:n], ACT.Relu, 122880.0, -131072.0), job)
+        vec("tt", n, [], [], lambda: (ps(job)[:, 0:n], ps(job)[:, 0:n], mk(job)[:, 0:n], ALU.add), job=job)
+        vec("scan", n, [pkey], [okey], lambda: (out, pat, ps(job)[:, 0:n], 0.0, ALU.add, ALU.min), job=job)
+
+    def pair(t, b, i):
+        if i < 10:
+            cb, r = divmod(10 * b + i, 16)
+            return T["GE%d" % t][:, 2048 * cb + r:2048 * (cb + 1):16], [("GE", t, cb, 0), ("GE", t, cb, 1)]
+        c = cpcol(i - 10, b)
+        return T["GC%d" % t][:, c:c + 128], [cpkey(t, i - 10, b)]
+
+    for t in range(3):
+        rnd[0] = t + 1
+        w = win(t); GC = T["GC%d" % t]; GE = T["GE%d" % t]
+        if t == 0:
+            for h in range(2):
+                gather(E[:, 512 * h:512 * h + 512], w[:, 0:WIN], T.LU[:, 160 + 32 * h:192 + 32 * h], 512, allkeys(0) + luk, [("E", h)])
+            for cbs in ((0,), (1,), (2, 3, 4)):
+                job = newjob(); items = []; rd = []
+                for x, cb in enumerate(cbs):
+                    bs = sorted(set(i // 10 for i in range(16 * cb, 16 * cb + 16)))
+                    for b in bs:
+                        j = (10 * b - 16 * cb + 8) // 2
+                        items.append((slice(128 * x, 128 * x + 128), T.PK[:, 128 * j:128 * j + 128], E[:, 128 * b:128 * b + 128], b == bs[0], b == bs[-1], 128))
+                        rd += [("PK", j), ("E", b // 4)]
+                mm(items, rd, job)
+                n = 128 * len(cbs)
+                vec("ts", n, [], [("O", cb) for cb in cbs],
+                    lambda job=job, n=n, c=128 * cbs[0]: (T.O[:, c:c + n], ps(job)[:, 0:n], -HALF, float(M), ALU.add, ALU.min), job=job)
+        else:
+            hs = range(2)
+            alias([("GL", t, h) for h in hs], [("HB" if t == 1 else "LB", c0) for c0 in (0, V, 640)])
+            if t == 1: alias([("SL", b) for b in range(8)], [("PT", j) for j in range(12)] + [(x, h) for x in ("TA", "TS") for h in hs])
+            else:
+                alias([("SL2", b) for b in range(8)], [("SL", b) for b in range(8)])
+                alias([("GN", 2, h) for h in hs], [("E", h) for h in hs])
+                alias([("GD", 2, 2, h) for h in hs], [("D0", b) for b in range(8)])
+            GL = T["GL%d" % t]; ON = T["ON%d" % t]; SEL = T["SEL%d" % t]
+            for h, (v0, v1) in enumerate(((0, V), (V, X))):
+                n = (v1 - v0) // 16; o0 = v0 // 16
+                gather(GL[:, v0:v1], w[:, 0:WIN], T.LU[:, 160 + o0:160 + o0 + n], v1 - v0, allkeys(t) + luk, [("GL", t, h)])
+                job = newjob()
+                mm([(slice(0, n), SEL[:, 128 * r:128 * r + 128], GL[:, v0 + r:v1:16], r == 0, r == 15, n) for r in range(16)],
+                   [("GL", t, h)] + [("SEL", t, j) for j in range(4)], job)
+                vec("ts", n, [], [("ON", t, h)], lambda job=job, n=n, o0=o0, ON=ON: (ON[:, o0:o0 + n], ps(job)[:, 0:n], float(M), None, ALU.min), job=job)
+                gather(T["GN%d" % t][:, v0:v1], T.W0[:, 0:EWIN], ON[:, o0:o0 + n], v1 - v0, objkeys(0) + [("ON", t, h)], [("GN", t, h)])
+                for u in range(1, t + 1):
+                    gather(T["GD%d%d" % (t, u)][:, v0:v1], w[:, 0:EWIN], T["ON%d" % u][:, o0:o0 + n], v1 - v0, objkeys(t) + [("ON", u, h)], [("GD", t, u, h)])
+        for x, (o0, n) in enumerate(((0, 64), (64, 48), (112, 48))):
+            gather(GC[:, 16 * o0:16 * (o0 + n)], w[:, 0:WIN], T.LU[:, o0:o0 + n], 16 * n, allkeys(t) + luk, [("GC", t, x)])
+        for cb in range(5):
+            for h in range(2):
+                o0 = 128 * cb + 64 * h
+                gather(GE[:, 16 * o0:16 * o0 + 1024], w[:, 0:EWIN], T.O[:, o0:o0 + 64], 1024, objkeys(t) + [("O", cb)], [("GE", t, cb, h)])
+
+        job = newjob(); n = 80 if t == 0 else 8
+        rhs = T.DEC[:, :] if t == 0 else T.DD[:, t - 1:16:2]
+        mm([(slice(n * b, n * b + n), GC[:, 128 * b:128 * b + 128], rhs, True, True, n) for b in range(2)], ["DEC", "DD", ("GC", t, 0)], job)
+        for b in range(2):
+            act(n, ["OWN"], ["AX"], lambda job=job, n=n, b=b: (T.AX[:, n * b:n * b + n], ps(job)[:, n * b:n * b + n], ACT.Abs, T.OWN[:, b:b + 1], 1.0), job)
+        if t == 0:
+            vec("scan", 160, ["AX", "P10"], ["SX"], lambda: (T.SX[:, :], T.P10[:, 0:160], T.AX[:, :], 0.0, ALU.add, ALU.min))
+            vec("cp", 16, ["SX"], ["NM"], lambda: (T.NM[:, :], T.SX[:, 9:160:10]))
+        else:
+            vec("tt", 16, ["AX", "NM"], ["NM"], lambda: (T.NM[:, :], T.NM[:, :], T.AX[:, 0:16], ALU.min), 2.0)
+        vec("ts", 16, ["NM"], ["NB"], lambda: (T.NB[:, :], T.NM[:, :], 0.5, BIG, ALU.is_gt, ALU.mult))
+        Ly = 10 if t == 0 else 20
+        for b in range(2):
+            n = 8 * Ly
+            items = [(slice(0, n, Ly // 10), T.GC0[:, 256 + 128 * b:384 + 128 * b], T.DEC[:, :], 80)]
+            if t: items.append((slice(1, n, 20 // t), GC[:, 256 + 128 * b:384 + 128 * b], T.DD[:, 0:16:2 // t], 8 * t))
+            least(t, b, n, T.R60[:, 0:480:6] if t == 0 else T["RY%d" % t][:, :], "R60" if t == 0 else "RY%d" % t, items,
+                  ["DEC", "DD", ("GC", 0, 0), ("GC", t, 0)], T.P60[:, 0:480:60 // Ly], "P60", T.SY[:, n * b:n * b + n], ("SY", b))
+        vec("tt", 16, [("SY", 0), ("SY", 1), "NB"], ["PY"], lambda Ly=Ly: (T.PY[:, :], T.SY[:, Ly - 1:16 * Ly:Ly], T.NB[:, :], ALU.add), 2.0)
+
+        for (b0, b1) in STATIC_GROUPS:
+            nb = b1 - b0; prs = [(i, b) for i in range(12) for b in range(b0, b1)]; base = 1056 * b0; oks = []
+            for x in range(0, len(prs), 5):
+                chunk = prs[x:x + 5]; n = 88 * len(chunk); c = slice(base + 88 * x, base + 88 * x + n); sk = ("SS", b0, x); ok = ("SO", b0, x); oks.append(ok)
+                rd = []; its = []; itm = []
+                for y, (i, b) in enumerate(chunk):
+                    a, k = pair(0, b, i); rd += k; cc = slice(88 * y, 88 * y + 88)
+                    its.append((cc, a, T.D88[:, :], True, True, 88))
+                    itm += [(cc, topl(t, b)[0], T.R88[:, :], True, False, 88), (cc, a, T.K88[:, :], False, True, 88)]
+                if t == 0:
+                    job = newjob(); mm(its, rd + ["D88"], job)
+                    move(n, [], [sk], lambda job=job, c=c, n=n: (T.SS[:, c], ps(job)[:, 0:n]), job)
+                job = newjob(); mm(itm, rd + ["K88", "R88"] + [topl(t, b)[1] for b in range(b0, b1)], job)
+                vec("scan", n, [sk], [ok], lambda job=job, c=c, n=n: (T.SO[:, c], T.SS[:, c], ps(job)[:, 0:n], 0.0, ALU.min, ALU.max), job=job)
+            m = 8 * nb; u = 48 * b0; uk = ("U", b0); hf = base + 528 * nb
+            vec("tt", 6 * m, oks, [uk], lambda u=u, m=m, base=base, hf=hf, nb=nb: (T.U[:, u:u + 6 * m], T.SO[:, base + 10:hf:11], T.SO[:, hf + 10:hf + 528 * nb:11], ALU.min), 2.0)
+            vec("tt", 3 * m, [uk], [uk], lambda u=u, m=m: (T.U[:, u:u + 3 * m], T.U[:, u:u + 3 * m], T.U[:, u + 3 * m:u + 6 * m], ALU.min), 2.0)
+            vec("tt", m, [uk], [uk], lambda u=u, m=m: (T.U[:, u:u + m], T.U[:, u:u + m], T.U[:, u + m:u + 2 * m], ALU.min), 2.0)
+            vec("tt", m, [uk], [("T0", b) for b in range(b0, b1)], lambda u=u, m=m, b0=b0: (T.T0[:, 8 * b0:8 * b0 + m], T.U[:, u:u + m], T.U[:, u + 2 * m:u + 3 * m], ALU.min), 2.0)
+
+        L = [0, 30, 50][t]
+        for b in range(8 if t else 0):
+            n = 8 * L; items = []; rd = ["DEC", "DD"]; offs = [None, off1, off2][t]; hb = 0 if b < 2 else 1
+            dd = T.DD[:, 0:16:2 // t]
+            for i in range(12):
+                a, k = pair(t, b, i); rd += k
+                items.append((slice(offs[i], n, L // t), a, dd, 8 * t))
+            for u in range(1, t + 1):
+                items.append((slice(offs[11 + u], n, L // t), T["GD%d%d" % (t, u)][:, 128 * b:128 * b + 128], dd, 8 * t))
+                items.append((slice(u - 1, n, L // 10), T["GN%d" % u][:, 128 * b:128 * b + 128], T.DEC[:, :], 80))
+                rd += [("GD", t, u, hb), ("GN", u, hb)]
+            least(t, b, n, T["R%d" % L][:, :], "R%d" % L, items, rd, T.P60[:, 0:480:2] if t == 1 else T.P50[:, :],
+                  "P60" if t == 1 else "P50", SL[:, n * b:n * b + n], ("SL", b) if t == 1 else ("SL2", b))
+
+        for (b0, b1) in (FINAL_GROUPS if t == 2 else ROUND_GROUPS):
+            bl = range(b0, b1); n = 8 * (b1 - b0); c = slice(8 * b0, 8 * b1)
+            def keys(s, bl=bl): return [(s, b) for b in bl]
+            t0 = T.T0[:, c]; t1 = T.T1[:, c]; t2 = T.T2[:, c]; gi = T.GI[:, c]; top = T.TOP[:, c]
+            if b0 == 0:
+                ko = [("T0", 0), ("T0", 1)]
+                vec("tt", 16, ["PY", ("TOP", 0), ("TOP", 1)], ["PY"], lambda: (T.PY[:, :], T.PY[:, :], T.TOP[:, 0:16], ALU.add), 2.0)
+                vec("tt", 16, ["PY"] + ko, ko, lambda: (T.T0[:, 0:16], T.T0[:, 0:16], T.PY[:, :], ALU.min), 2.0)
+            if t:
+                vec("tt", n, keys("SL" if t == 1 else "SL2") + keys("TOP"), keys("T1"),
+                    lambda t1=t1, top=top, b0=b0, b1=b1, L=L: (t1, top, SL[:, 8 * L * b0 + L - 1:8 * L * b1:L], ALU.add), 2.0)
+                vec("tt", n, keys("T1") + keys("T0"), keys("T0"), lambda t1=t1, t0=t0: (t0, t0, t1, ALU.min), 2.0)
+            vec("ts", n, keys("T0"), keys("GI"), lambda t0=t0, gi=gi: (gi, t0, -HALF, float(NONE), ALU.add, ALU.min))
+            hi = T.A[:, 128 * b0 + 10 + t:128 * b1:16]; lob = T.B[:, 128 * b0 + 10 + t:128 * b1:16]
+            vec("cp", n, keys("GI"), keys("A"), lambda hi=hi, gi=gi: (hi, gi))
+            if t < 2:
+                lo = T.A[:, 128 * b0 + 2 + t:128 * b1:16]
+                vec("tt", n, keys("GI") + keys("A"), keys("A"), lambda lo=lo, hi=hi, gi=gi: (lo, gi, hi, ALU.subtract), 2.0)
+                if b0 == 0:
+                    turn_back(t + 1, b0, b1); send(t + 1)
+                vec("ts", n, keys("GI"), keys("T2"), lambda t2=t2, gi=gi: (t2, gi, float(NONE), -4000.0, ge, ALU.mult))
+                vec("tt", n, keys("GI") + keys("T2"), keys("T2"), lambda t2=t2, gi=gi: (t2, t2, gi, ALU.add), 2.0)
+                vec("tt", n, keys("TOP") + keys("T2"), keys("TOP"), lambda t2=t2, top=top: (top, top, t2, ALU.max), 2.0)
+                finish_top(b0, b1)
+                turn_back(t + 1, b0, b1, b0 == 0)
+                vec("cp", n, keys("A"), keys("B"), lambda lo=lo, lob=lob: (lob, lo))
+            else:
+                vec("tt", n, keys("GI") + keys("A"), keys("B"), lambda lob=lob, hi=hi, gi=gi: (lob, gi, hi, ALU.subtract), 2.0)
+                turn_back(3, b0, b1)
+    return ops
+
+
+def order(ops, bias=BIAS, slack=SLACK, bonus=BONUS):
+    n = len(ops)
+    succ = [[] for _ in range(n)]
+    for i, o in enumerate(ops):
+        for d in o["deps"]: succ[d].append(i)
+    level = [0.0] * n
+    for i in range(n - 1, -1, -1):
+        o = ops[i]; d = o["dur"]["V"] if o["eng"] == "VS" else o["dur"]
+        level[i] = d + o["lat"] + LAT + bonus.get(o["cls"], 0.0) + bonus.get(o["fine"] + ".", 0.0) + max([level[s] for s in succ[i]] + [0.0])
+    left = [len(o["deps"]) for o in ops]
+    ready = [i for i in range(n) if left[i] == 0]
+    free = {e: 0.0 for e in "VSPGY"}
+    done = [0.0] * n
+    bank = [[0.0, None, True] for _ in range(NBANK)]
+    seq = []
+    while ready:
+        cand = []
+        for i in ready:
+            o = ops[i]
+            if o["after"] is not None and "on" not in ops[o["after"]]: continue
+            t0 = max([done[d] + LAT for d in o["deps"]] + [0.0])
+            bk = None
+            if o["job"] is not None and o["job"][1][0] == i:
+                fr = [k for k in range(NBANK) if bank[k][2]]
+                if not fr: continue
+                bk = min(fr, key=lambda k: bank[k][0]); t0 = max(t0, bank[bk][0] + LAT)
+            if o["eng"] == "VS":
+                e = bonus.get(o["fine"] + "@") or min("VS", key=lambda x: max(t0, free[x]) + o["dur"][x] + (bias if x == "V" else 0.0)); d = o["dur"][e]
+            else:
+                e = o["eng"]; d = o["dur"]
+            cand.append((max(t0, free[e]), i, e, d, bk))
+        cand = [c for c in cand if c[3] < 700.0 or not any(x[2] == c[2] and level[x[1]] > level[c[1]] + URGENT and x[0] < c[0] + AHEAD * c[3] for x in cand)]
+        tmin = min(c[0] for c in cand)
+        s, i, e, d, bk = max([c for c in cand if c[0] <= tmin + slack], key=lambda c: level[c[1]])
+        o = ops[i]; o["on"] = e
+        if bk is not None:
+            o["job"][2] = bk
+            if bank[bk][1] is not None: o["deps"][bank[bk][1]] = True
+            bank[bk][2] = False
+        free[e] = s + d; done[i] = s + d + o["lat"]; o["at"] = s
+        if o["job"] is not None and o["job"][1][-1] == i:
+            bank[o["job"][2]] = [done[i], i, True]
+        seq.append(i); ready.remove(i)
+        for x in succ[i]:
+            left[x] -= 1
+            if left[x] == 0: ready.append(x)
+    return seq, max(done)
+
+
+def rank_program(g, core, T, topo):
+    rank = T.rank_of(core)
+    if rank is None:
+        return
+    ops = plan(T, topo, rank, core)
+    seq, _ = order(ops)
+    queue = {"V": g.vector, "S": g.scalar, "P": g.tensor, "G": g, "Y": g.sync}
+    csem = {"V": "cv", "S": "cs", "P": "cp", "G": "cg"}
+    count = {}
+    waited = {e: {} for e in queue}
+    ndma = 0
+    nin = len(topo.engines(core, T.cores[(rank + 1) % N]))
+    for i in seq:
+        o = ops[i]; e = o["on"]; q = queue[e]
+        need = {}
+        for d in o["deps"]:
+            p = ops[d]
+            if e == "P" and p["on"] == "P": continue
+            s, v = p["sig"]
+            need[s] = max(need.get(s, 0), v)
+        for s, v in need.items():
+            if waited[e].get(s, 0) < v:
+                q.wait_ge(T.sem[s], v); waited[e][s] = v
+        ins = o["fn"](e, q)
+        if o["kind"] == "c":
+            s = csem[e]
+            for x in ins:
+                x.then_inc(T.sem[s], 1); count[s] = count.get(s, 0) + 1
+            o["sig"] = (s, count[s])
+        elif o["kind"] == "dma":
+            s = "dm%d" % ndma; ndma += 1
+            ins[0].then_inc(T.sem[s], 16); count[s] = 16; o["sig"] = (s, 16)
+        else:
+            t = o["kind"][1]
+            o["sig"] = ("arr%d" % t, nin); count["arr%d" % t] = nin; count["snt%d" % t] = nin
+    for s, v in count.items():
+        if waited["G"].get(s, 0) < v: g.wait_ge(T.sem[s], v)

@@ -1,3 +1,4 @@
+import math
 from concourse.bass import DstId, RemoteDMATransfer
 from concourse.mybir import AluOpType as ALU, ActivationFunctionType as ACT
 
@@ -5,44 +6,41 @@ N, V, X, M, NONE = 8, 256, 1024, 2048, 2816
 TMP = M + 16
 WIN = TMP + (X - V) + 1
 EWIN = M + 1
-BIG = 1.0e6
-HALF = 0.4375
-KK = 65536.0
-NBANK = 8
+STEP, ZERO = 64.0, 2880.0
+UP = math.exp(ZERO / STEP)
+THR = math.exp(-5.0)
+MAGIC = 12582912.0
+R0, RN, R2, L = 13, 157, 169, 182
+NB16, NF32 = 4, 4
+EARLY = 6
 
 
-def _sb(n, d): return ("sbuf", [128, n], d)
+def _sb(n, d): return ("sbuf", [128] + (n if isinstance(n, list) else [n]), d)
 
 
 SCRATCH = {}
 for _d, _l in (
-    ("int32", dict(PI=X, LI=224, LM=224, HI=X, GI=64, CI=4)),
+    ("int32", dict(PI=X, LI=[14, 16], LM=[14, 16], CI=2)),
     ("uint16", dict(LU=224, O=640, ON1=64, ON2=64)),
-    ("float32", dict(OUT=X, SS=8448, SO=8448, U=384, SL=3200, SY=320, AX=160, SX=160, NM=16, NB=16, PY=16, T0=64, T1=64, T2=64, TOP=64,
-                     DT=80, DU=88, X128=128, X80=80, X88=88, CF=8, TB=12, OWN=2)),
-    ("bfloat16", dict(W0=2848, D1=2848, D2=2848, GE0=10240, GE1=10240, GE2=10240, GC0=2560, GC1=2560, GC2=2560, GN1=X, GN2=X,
-                      GD11=X, GD21=X, GD22=X, GL1=X, GL2=X, A=X, B=X, Z=512, ID=128, EH=128, EL=128, PK=1536, DEC=80, D88=88, K88=88,
-                      R88=88, DD=16, OT1=V, OT2=V, SEL1=2048, SEL2=2048, R60=480, R50=400, R30=240, RY1=160, RY2=160, P60=480, P50=400, P10=320)),
+    ("float32", dict(OUT=X, IDF=128, CF=8, OWF=4, LN=640, LO1=64, LO2=64, LG=192, GF=192, FO=1024)),
+    ("bfloat16", dict(W0=2848, W1=2848, W2=2848, GE0=10240, GE1=1280 * EARLY, GE2=10240, GC0=2560, GC1=2560, GC2=2560,
+                      GL0=X, GL1=X, GL2=X, GA=X, GB=X, GN=X, SS=[8, 8, L], MK=[8, 8, L], SO=12288, A=[8, 8, 16], AT=[16, 8, 16], GX=128,
+                      Z=160, ID=160, PM0=160, PM1=160, PM2=160, PM3=160, PM4=160, OWN=4, P10=320, P12=304, P13=336, P14=352, P15=256, P16=272,
+                      TS=1024, AX=192, SX=192, PY=16, Y0=640, Y1=640, Y2=640, T1=64, T2=64, TOP=64)),
 ):
     for _k in _l: SCRATCH[_k] = _sb(_l[_k], _d)
-for _k in range(NBANK):
-    SCRATCH["MK%d" % _k] = _sb(400, "bfloat16")
-    SCRATCH["PS%d" % _k] = ("psum", [128, 512], "float32")
+for _k in range(NB16): SCRATCH["PB%d" % _k] = ("psum", [128, 8, 8, 16], "bfloat16")
+for _k in range(NF32): SCRATCH["PF%d" % _k] = ("psum", [128, 16, 32], "float32")
 
-NDMA = 20
-SEMAPHORES = ["cv", "cs", "cp", "cg"] + ["arr%d" % t for t in range(3)] + ["snt%d" % t for t in range(3)] + ["dm%d" % k for k in range(NDMA)]
+NDMA = 12
+SEMAPHORES = ["cv", "cs", "cp", "cg", "fin"] + ["arr%d" % t for t in range(3)] + ["snt%d" % t for t in range(3)] + ["dm%d" % k for k in range(NDMA)]
 
-CYC, PCYC, GATH, LAT = 1.04, 0.55, 1.56, 180.0
-DMA_NS, NET_NS = 2300.0, 9000.0
-STATIC_GROUPS = [(0, 2), (2, 5), (5, 8)]
-ROUND_GROUPS = [(0, 2), (2, 8)]
-FINAL_GROUPS = [(0, 2), (2, 5), (5, 8)]
-URGENT, AHEAD = 4000.0, 0.5
-BIAS, SLACK = 500.0, 60.0
-BONUS = {'arr1': 18000, 'arr2': 33400, 'SS1': 3600, 'SO3': 3800, 'SY1': 7600, 'SO1.2.30.': 2600, 'NB1': 2000, 'SS1.5.35.': 5000, 'job1.14.': 400,
-         'T13.2.': -1400, 'SO3.5.20.': 8000, 'O1': 2000, 'E1.1.': 5000, 'GC3.2.0.': 3400, 'GI3.5.': -11000, 'job2.89.': 3000, 'GL3': 1400,
-         'GI3': 600, 'GC2': 9000, 'job2.60.': -4000, 'job3.110.': -8000, 'OT2.2.': 8000, 'T02.0.': 400, 'SO2.5.35.': -3000, 'SO1.5.10.': -3000,
-         'SO1.2.20.': -8000}
+CYC, PCYC, GATH, LAT = 0.95, 0.55, 1.56, 150.0
+DMA_NS, NET_NS, NF2 = 2300.0, 7000.0, 0.6
+RANGES = [[(0, 2), (2, 4), (4, 6), (6, 8)], [(0, 2), (2, 4), (4, 6), (6, 8)], [(0, 2), (2, 4), (4, 6), (6, 8)]]
+LOADS = [None, [(0, 256), (256, 1024)], [(0, 256), (256, 512), (512, 768), (768, 1024)]]
+SIGNS = "0123456789abcdefghijklmnopqrstuvwxyzABCDEFGHIJKLMNOPQRSTUVWXYZ"
+ORDER = "12000m1a030e0W0g0k0p16140c0i0a0q040s1i1u1x0S1A0C06080O1G0w1I0u1D1W1s0Y1e1Z1g1c0y1M1Q0M101q1m281O0I1S0A0K1k1K2b0Q0G1U200E1y2l222o2c2426181o2e2g2m342C2u2r2s2i2F2Q2T1E2G4k372y2A4m2x3i0U4o3k3q382N4q3s2L3m3o4s3u3w4u4y3y4w2P3G4A3f2U2Z334C4E3I4G4I2I3C3A3F4K303K3M3O2X3W4U4Y4W3Q4M3d3Y3h4O444c3S40503b464f52483U54434b4g4Q5g564j595k5C5i5H8Y6N5m5E5I5o5K5q5M926P4S5a5S5w5s5c5u5O5Q6m6o6C6L906r7I6s5y5U6Q6W706H7K7r7M6Y5A7O5Z6S6U727Q7S6v6w7W7U7p6z7Y827A807t6A7E84617u5W885e757a957w7C8a7G7y8C8G8E8I8c7c7e8K8696989c79778M9e6J6E9a8O7g8e9g8Q9p9n7k9q9t7i9k9i8g7n9F8k9u9P9J8i9x9y9Ba4a08ma662a28oa88q64aa8w9Q8sac9Dag8u9V6c6eae9T8S9Zaibe6aak66bgaKaMan9Gc5bj8ybkcaap9M8U6gcecgaVaq68bn9Lasc6c8aPbpcc8Ab4aWaZb6bydAaQaTci8WbDdEdCdGb9buckbqau6ibAbsbxb0dIbI9XcmbMbab3bEcscwbGbRaAbWcuc0bLbPcycocWcTbdcAcUdLawbSc3cYbVbZaIdedjcqd0ay6kdgcCd3dkcEdNdOdQaGd5d6dmd8aCdacHdScIcKdpddcNcRdqcOdVaEdsdudwdz"
 
 
 def plan(T, topo, rank, core):
@@ -64,67 +62,67 @@ def plan(T, topo, rank, core):
         for k in wr: lastw[k] = i; readers[k] = []
         k = wr[0] if wr else "out"
         cls = "%s%d" % (k if isinstance(k, str) else k[0], rnd[0])
-        ops.append({"eng": eng, "dur": dur, "fn": fn, "deps": deps, "job": job, "kind": kind, "lat": lat, "after": None, "f": 1.0,
+        ops.append({"eng": eng, "dur": dur, "fn": fn, "deps": deps, "job": job, "kind": kind, "lat": lat, "g": 0,
                     "cls": cls, "fine": cls if isinstance(k, str) else cls + "".join("." + str(x) for x in k[1:])})
         if job is not None: job[1].append(i)
 
-    def alias(new, old):
-        for k in new:
-            readers[k] = readers.get(k, []) + [i for x in old for i in readers.get(x, []) + [lastw[x]]]
-
-    def newjob():
+    def newjob(kind):
         njob[0] += 1
-        return [njob[0], [], None]
+        return [njob[0], [], None, kind]
 
-    def ps(job): return T["PS%d" % job[2]]
-    def mk(job): return T["MK%d" % job[2]]
+    def ps(job): return T[("PB%d" if job[3] == "b" else "PF%d") % job[2]]
     def gt(n): return 200 + 2 * n * CYC
+    def vt(n): return max(64, n) * CYC + 10
+    def st(n): return max(64, n) * CYC + 60
 
-    def vec(name, n, rd, wr, args, f=1.0, job=None):
-        calls = {"ts": lambda q, a: q.tensor_scalar(*a), "tt": lambda q, a: q.tensor_tensor(*a), "cp": lambda q, a: q.tensor_copy(*a),
-                 "ms": lambda q, a: q.memset(*a), "scan": lambda q, a: q.tensor_tensor_scan(*a)}
-        op("V", max(64, n * f) * CYC + 20, lambda e, q: [calls[name](q, args())], rd, wr, job)
+    calls = {"ts": lambda q, a: q.tensor_scalar(*a), "tt": lambda q, a: q.tensor_tensor(*a), "cp": lambda q, a: q.tensor_copy(*a),
+             "ms": lambda q, a: q.memset(*a), "scan": lambda q, a: q.tensor_tensor_scan(*a)}
 
-    def act(n, rd, wr, args, job=None):
+    def vec(name, n, rd, wr, args, job=None):
+        op("V", vt(n), lambda e, q: [calls[name](q, args())], rd, wr, job)
+
+    def act(n, rd, wr, args, job=None, extra=0.0):
         def fn(e, q):
             a = args()
             return [q.activation(a[0], a[1], a[2], bias=a[3], scale=a[4])]
-        op("S", n * CYC + 70, fn, rd, wr, job)
+        op("S", st(n) + extra, fn, rd, wr, job)
 
-    def move(n, rd, wr, args, job=None, f=1.0, fix=0.0):
+    def move(n, rd, wr, args, job=None, f=1.0):
         def fn(e, q):
             o, i = args()
             return [q.tensor_copy(o, i) if e == "V" else q.activation(o, i, ACT.Copy)]
-        op("VS", {"V": max(64, n * f) * CYC + 20 + fix, "S": n * f * CYC + 70}, fn, rd, wr, job)
-        ops[-1]["f"] = f
+        op("VS", {"V": vt(n * f), "S": st(n)}, fn, rd, wr, job)
 
     def gather(out, w, off, n, rd, wr):
-        move(n, rd, wr, lambda: (out, w.indirect(off)), f=GATH, fix=30)
+        def fn(e, q):
+            i = w.indirect(off)
+            return [q.tensor_copy(out, i) if e == "V" else q.activation(out, i, ACT.Copy)]
+        op("VS", {"V": n * GATH * CYC + 50, "S": n * GATH * CYC + 65}, fn, rd, wr)
+        ops[-1]["g"] = 1
 
     def mm(items, rd, job):
         dur = sum(max(64, x[5]) for x in items) * PCYC + 60
-        op("P", dur, lambda e, q: [q.matmul(ps(job)[:, c], l, r, a, b) for (c, l, r, a, b, _) in items], rd, [], job)
+        op("P", dur, lambda e, q: [q.matmul(c(ps(job)), l, r, a, b) for (c, l, r, a, b, _) in items], rd, [], job)
 
-    def sel(out, in_, pat, cmp, fill, base, cm, n, rd, wr):
-        op("G", gt(n), lambda e, q: [q.affine_select(out, in_, pat, cmp, fill, base, cm)], rd, wr)
+    def turn(items, rd, job, ident, f=1):
+        op("P", 128 * f * len(items) * PCYC + 60, lambda e, q: [q.transpose(c(ps(job)), a, ident) for (c, a) in items], rd, [], job)
 
-    def iota(out, pat, base, cm, n, wr, flag=True):
-        if flag: op("G", gt(n), lambda e, q: [q.iota(out, pat, base, cm, allow_small_or_imprecise_dtypes=True)], [], wr)
-        else: op("G", gt(n), lambda e, q: [q.iota(out, pat, base, cm)], [], wr)
+    def dma(eng, out, in_, rd, wr, extra=0.0, kind="dma"):
+        op(eng, 60.0, lambda e, q: [q.dma_start(out, in_)], rd, wr, kind=kind, lat=DMA_NS + extra)
 
-    def dma(eng, out, in_, rd, wr, extra=0.0):
-        op(eng, 80.0, lambda e, q: [q.dma_start(out, in_)], rd, wr, kind="dma", lat=DMA_NS + extra)
-
-    HB, LB, E, D0, SL = T.GL1, T.GL2, T.GN2, T.GD22, T.SL
     own0 = rank * V
+    ID = T.ID[:, 16:144]
+    NN = T.OWN[:, 2:3]
+    GXO = T.GX[:, 16 * rank:16 * rank + 16]
     def wcol(b): return own0 + 128 * b if b < 2 else TMP + 128 * (b - 2)
-    def win(t): return [T.W0, T.D1, T.D2][t]
+    def win(t): return [T.W0, T.W1, T.W2][t]
     def wkey(t, b): return ("win", t, b)
-    def objkeys(t): return [wkey(t, 0), wkey(t, 1), ("arr", t), ("none", t)]
+    def objkeys(t): return [("obj", 0), ("obj", 1), ("none", t)] if t == 2 else [wkey(t, 0), wkey(t, 1), ("arr", t), ("none", t)]
     def allkeys(t): return objkeys(t) + [("pad", t)] + [wkey(t, b) for b in range(2, 8)]
+    def shift(k, d): return T["PM%d" % k][:, 16 - d:144 - d]
 
     def send(t):
-        src = win(t)[:, own0:own0 + V]
+        src = win(t)[:, own0:own0 + V] if t < 2 else GXO
         def fn(e, q):
             trs = []
             at = 0
@@ -137,348 +135,282 @@ def plan(T, topo, rank, core):
                 trs.append(RemoteDMATransfer(dst_ids=[DstId(rid=rid, pnc=pid)], dma_engine_mask=mask, remote_sem=T.sem["arr%d" % t], src=src, dst=src))
             q.remote_dma_fused(trs, local_sem=T.sem["snt%d" % t])
             return []
-        op("G", 300.0, fn, [wkey(t, 0), wkey(t, 1)], [("arr", t)], kind=("net", t), lat=NET_NS)
+        op("G", 300.0, fn, [wkey(t, 0), wkey(t, 1)] if t < 2 else ["GXO"], [("arr", t)], kind=("net", t), lat=NET_NS)
+        ops[-1]["nf"] = NF2 if t == 2 else 1.0
 
     dma("Y", T.PI[:, 0:V], T.pts[:, 0:V], [], ["PIo"])
     dma("S", T.PI[:, V:X], T.pts[:, V:X], [], ["PIt"], 500)
-    dma("Y", T.LI[:, 0:16], T.xs[:, :], [], ["LI0"])
-    dma("Y", T.LI[:, 16:32], T.ys[:, :], [], ["LI1"])
-    dma("Y", T.LI[:, 32:160], T.cp[:, :], [], ["LI2"])
-    dma("Y", T.LI[:, 160:224], T.ld[:, :], [], ["LI3"])
+    dma("Y", T.LI[:, 0:4, :], T.ld[:, :], [], ["LI0"])
+    dma("Y", T.LI[:, 4:12, :], T.cp[:, :], [], ["LI1"])
+    dma("Y", T.LI[:, 12, :], T.xs[:, :], [], ["LI2"])
+    dma("Y", T.LI[:, 13, :], T.ys[:, :], [], ["LI3"])
 
-    vec("ms", 512, [], ["Z"], lambda: (T.Z[:, :], 0.0), 0.5)
-    ne, ge = ALU.not_equal, ALU.is_ge
-    sel(T.EL[:, :], T.Z[:, 0:128], [[16, 8], [2, 16]], ne, 1.0, -20, -1, 128, ["Z"], ["EL"])
-    sel(T.EL[:, :], T.EL[:, :], [[16, 8], [2, 16]], ne, 8.0, -19, -1, 128, ["EL"], ["EL"])
-    sel(T.EL[:, :], T.EL[:, :], [[0, 8], [1, 16]], ge, 0.0, -10, 0, 128, ["EL"], ["EL"])
-    sel(T.EL[:, :], T.EL[:, :], [[16, 8], [2, 8], [1000, 2]], ne, -8.0, 1, -1, 128, ["EL"], ["EL"])
-    sel(T.ID[:, :], T.Z[:, 0:128], [[1, 128]], ne, 1.0, 0, -1, 128, ["Z"], ["ID"])
-    sel(T.EH[:, :], T.ID[:, :], [[0, 8], [-1, 16]], ge, 0.0, 9, 0, 128, ["ID"], ["EH"])
-    iota(T.CI[:, 0:1], [[0, 1]], 0, 1, 1, ["CI0"], False)
-    iota(T.X128[:, :], [[64, 8], [1, 16]], 0, 0, 128, ["X128"])
-    iota(T.X80[:, :], [[64, 8], [1, 10]], 0, 0, 80, ["X80"])
-    iota(T.TB[:, :], [[-2, 12]], 8, 0, 12, ["TB"])
-    later = len(ops)
-    iota(T.X88[:, :], [[64, 8], [1, 11]], -1, 0, 88, ["X88"])
-    sel(T.R88[:, :], T.Z[:, 0:88], [[16, 8], [0, 11]], ne, KK, 5, -1, 88, ["Z"], ["R88"])
-    sel(T.R88[:, :], T.R88[:, :], [[16, 8], [0, 11]], ne, KK, 6, -1, 88, ["R88"], ["R88"])
-    sel(T.R88[:, :], T.R88[:, :], [[16, 8], [0, 11]], ne, 0.9375 * KK, 7, -1, 88, ["R88"], ["R88"])
-    sel(T.R88[:, :], T.R88[:, :], [[16, 8], [1000, 11]], ne, 2.0 * KK, 7, -1, 88, ["R88"], ["R88"])
-    iota(T.OWN[:, :], [[-128, 2]], -own0, -1, 2, ["OWN"])
-    for (buf, L) in ((T.R60, 60), (T.R50, 50)):
-        key = "R%d" % L
-        sel(buf[:, :], T.Z[:, 0:8 * L], [[16, 8], [0, L]], ne, -1.0, 5, -1, 8 * L, ["Z"], [key])
-        sel(buf[:, :], buf[:, :], [[16, 8], [0, L]], ne, -1.0, 6, -1, 8 * L, [key], [key])
-    sel(T.DD[:, :], T.Z[:, 0:16], [[16, 8], [1, 2]], ne, 1.0, 10, -1, 16, ["Z"], ["DD"])
-    sel(T.DD[:, :], T.DD[:, :], [[16, 8], [1, 2]], ne, 1.0, 2, -1, 16, ["DD"], ["DD"])
-    for t in (1, 2):
-        for j in range(4):
-            part = T["SEL%d" % t][:, 512 * j:512 * j + 512]; key = ("SEL", t, j)
-            sel(part, T.Z[:, :], [[-200, 4], [16, 8], [200, 16]], ne, 1.0, 9 + t - 800 * j, -1, 512, ["Z"], [key])
-            sel(part, part, [[-200, 4], [16, 8], [200, 16]], ne, 1.0, 1 + t - 800 * j, -1, 512, [key], [key])
-    sel(T.R50[:, :], T.R50[:, :], [[0, 16], [-1, 25]], ge, 0.0, 23, 0, 400, ["R50"], ["R50"])
-    sel(T.R30[:, :], T.R60[:, 0:480:2], [[0, 8], [-1, 10], [-10, 3]], ge, 0.0, 22, 0, 240, ["R60"], ["R30"])
-    sel(T.RY1[:, :], T.R60[:, 0:480:3], [[0, 8], [-1, 10], [-10, 2]], ge, 0.0, 10, 0, 160, ["R60"], ["RY1"])
-    sel(T.RY2[:, :], T.R60[:, 0:480:3], [[0, 16], [-1, 5], [-10, 2]], ge, 0.0, 10, 0, 160, ["R60"], ["RY2"])
-    for (buf, L, n) in ((T.P60, 60, 480), (T.P50, 50, 400), (T.P10, 10, 320)):
-        sel(buf[:, :], T.Z[:, 0:n], [[0, n // L], [1, L]], ne, BIG, 0, 0, n, ["Z"], ["P%d" % L])
-    for h in range(2):
-        bl = range(4 * h, 4 * h + 4)
-        sel(T.A[:, 512 * h:512 * h + 512], T.Z[:, :], [[0, 32], [1, 16]], ne, 1.0, -7, 0, 512, ["Z"], [("A", b) for b in bl])
-        iota(T.B[:, 512 * h:512 * h + 512], [[0, 512]], 0, 0, 512, [("B", b) for b in bl])
-    for t in range(3): iota(win(t)[:, M + 1:TMP], [[0, 15]], 0, 0, 15, [("pad", t)])
-    late = range(later, len(ops))
+    ge, lt = ALU.is_ge, ALU.is_lt
     CI, CF = T.CI, T.CF
+    vec("ms", 80, [], ["Z"], lambda: (T.Z[:, :], 0.0))
+    op("G", gt(2), lambda e, q: [q.iota(T.OWF[:, 0:2], [[128, 2]], own0, 1, allow_small_or_imprecise_dtypes=True)], [], ["OWF0"])
+    op("G", gt(1), lambda e, q: [q.iota(CI[:, 0:1], [[0, 1]], 0, 1)], [], ["CI0"])
+    op("G", gt(160), lambda e, q: [q.affine_select(T.ID[:, :], T.Z[:, :], [[1, 160]], ALU.not_equal, 1.0, -16, -1)], ["Z"], ["ID"])
+    vec("ms", 1, [], ["OWF1"], lambda: (T.OWF[:, 2:3], float(NONE)))
+    vec("ms", 1, [], ["EB"], lambda: (T.OWF[:, 3:4], -ZERO / STEP))
+    EB = T.OWF[:, 3:4]
+    act(3, ["OWF0", "OWF1", "EB"], ["OWN"], lambda: (T.OWN[:, 0:3], T.OWF[:, 0:3], ACT.Exp, EB, 1.0 / STEP), extra=1300.0)
     vec("ts", 1, ["CI0"], ["CI1"], lambda: (CI[:, 1:2], CI[:, 0:1], 15, None, ALU.bitwise_and))
-    vec("ts", 1, ["CI0"], ["CI2"], lambda: (CI[:, 2:3], CI[:, 0:1], 4, None, ALU.arith_shift_right))
-    vec("cp", 2, ["CI1", "CI2"], ["CF0"], lambda: (CF[:, 0:2], CI[:, 1:3]))
-    vec("ts", 1, ["CF0"], ["CF2"], lambda: (CF[:, 2:3], CF[:, 0:1], 10.0, None, ge))
-    vec("ts", 1, ["CF0", "CF2"], ["CF3"], lambda: (CF[:, 3:4], CF[:, 0:1], -19.9375, CF[:, 2:3], ALU.add, ALU.mult))
-    vec("ts", 1, ["CF0"], ["CF4"], lambda: (CF[:, 4:5], CF[:, 1:2], 64.0, CF[:, 0:1], ALU.mult, ALU.add))
-    vec("ts", 12, ["TB", "CF3", "CF4"], ["TB"], lambda: (T.TB[:, :], T.TB[:, :], CF[:, 3:4], CF[:, 4:5], ALU.subtract, ALU.subtract))
-    vec("ts", 1, ["CF2"], ["CF5"], lambda: (CF[:, 5:6], CF[:, 2:3], 0.0625, 1.0, ALU.mult, ALU.add))
-    vec("ts", 2, ["OWN"], ["OWN"], lambda: (T.OWN[:, :], T.OWN[:, :], -HALF, None, ALU.add))
-    for j in range(12):
-        act(128, ["X128", "TB"], [("PT", j)], lambda j=j: (SL[:, 128 * j:128 * j + 128], T.X128[:, :], ACT.Abs, T.TB[:, j:j + 1], 1.0))
-    for j in range(3):
-        act(512, [("PT", 4 * j + i) for i in range(4)] + ["CF5"], [("PK", 4 * j + i) for i in range(4)],
-            lambda j=j: (T.PK[:, 512 * j:512 * j + 512], SL[:, 512 * j:512 * j + 512], ACT.Relu, CF[:, 5:6], -1.0))
-    act(80, ["X80", "TB"], ["DT"], lambda: (T.DT[:, :], T.X80[:, :], ACT.Abs, T.TB[:, 4:5], 1.0))
-    act(80, ["DT", "CF5"], ["DEC"], lambda: (T.DEC[:, :], T.DT[:, :], ACT.Relu, CF[:, 5:6], -1.0))
-    act(88, ["X88", "TB"], ["DU"], lambda: (T.DU[:, :], T.X88[:, :], ACT.Abs, T.TB[:, 4:5], 1.0))
-    act(88, ["DU", "CF5"], ["D88"], lambda: (T.D88[:, :], T.DU[:, :], ACT.Relu, CF[:, 5:6], -1.0))
-    act(88, ["D88"], ["K88"], lambda: (T.K88[:, :], T.D88[:, :], ACT.Identity, 0.0, -KK))
-    vec("ts", 1, ["CF2"], ["CF6"], lambda: (CF[:, 6:7], CF[:, 2:3], -float(NONE), float(NONE), ALU.mult, ALU.add))
-    vec("ts", 1, ["CF2"], ["CF7"], lambda: (CF[:, 7:8], CF[:, 2:3], float(NONE), None, ALU.mult))
+    vec("cp", 1, ["CI1"], ["CF5"], lambda: (CF[:, 5:6], CI[:, 1:2]))
+    row = CF[:, 5:6]
+    vec("ts", 1, ["CF5"], ["CF0"], lambda: (CF[:, 0:1], row, 10.0, None, lt))
+    vec("ts", 1, ["CF5"], ["CF1"], lambda: (CF[:, 1:2], row, 6.0, None, lt))
+    vec("ts", 1, ["CF5", "CF0"], ["CF2"], lambda: (CF[:, 2:3], row, 6.0, CF[:, 0:1], ge, ALU.mult))
+    vec("ts", 1, ["CF5"], ["CF3"], lambda: (CF[:, 3:4], row, 10.0, None, ALU.is_equal))
+    vec("ts", 1, ["CF5"], ["CF4"], lambda: (CF[:, 4:5], row, 11.0, None, ALU.is_equal))
+    for k in range(5):
+        vec("ts", 80, ["ID", "CF%d" % k], [("PM", k)], lambda k=k: (T["PM%d" % k][:, :], T.ID[:, :], CF[:, k:k + 1], None, ALU.mult))
+    vec("cp", 128, ["ID"], ["IDF"], lambda: (T.IDF[:, :], ID))
     for t in range(3):
-        k = 7 if t else 6
-        vec("ts", 2, ["Z", "CF%d" % k], [("none", t)], lambda t=t, k=k: (win(t)[:, M:WIN:WIN - 1 - M], T.Z[:, 0:2], CF[:, k:k + 1], None, ALU.add))
-    off1 = [3 * a + 1 for a in range(10)] + [2, 5, 8]
-    off2 = [o for o in range(25) if o % 5 >= 2]
+        vec("ts", 2, ["Z", "OWN"], [("none", t)], lambda t=t: (win(t)[:, M:WIN:WIN - 1 - M], T.Z[:, 0:2], NN, None, ALU.add))
+        vec("ms", 8, [], [("pad", t)], lambda t=t: (win(t)[:, M + 1:TMP], 0.0))
+    vec("ms", 160, [], ["P10"], lambda: (T.P10[:, :], 1.0))
+    vec("ms", 32, ["P10"], ["P10"], lambda: (T.P10[:, 0:320:10], 0.0))
+    for k in range(12, 17):
+        p = T["P%d" % k]; key = "P%d" % k; m = 25 if k < 15 else 17
+        vec("ms", m * k / 2, [], [key], lambda p=p: (p[:, :], 0.0))
+        vec("ts", m, ["Z", "OWN", key], [key], lambda p=p, k=k, m=m: (p[:, 0:m * k:k], T.Z[:, 0:m], NN, None, ALU.add))
+    vec("ts", 64, ["Z", "OWN"], ["late"], lambda: (T.SS[:, :, :, RN + 11], T.Z[:, 0:64], NN, None, ALU.add))
+    vec("ms", 8, [], ["reset"], lambda: (T.SS[:, 0:2, :, R0 - 1], -1.0))
 
-    for (c0, c1, pk) in ((0, V, "PIo"), (V, 640, "PIt"), (640, X, "PIt")):
-        n = c1 - c0; bl = range(c0 // 128, c1 // 128)
-        vec("ts", n, [pk], [("HI", c0)], lambda c0=c0, c1=c1: (T.HI[:, c0:c1], T.PI[:, c0:c1], 4088, None, ALU.bitwise_and))
-        vec("cp", n, [("HI", c0)], [("HB", c0)], lambda c0=c0, c1=c1: (HB[:, c0:c1], T.HI[:, c0:c1]))
-        vec("tt", n, [("HI", c0), pk], [("LB", c0)], lambda c0=c0, c1=c1: (LB[:, c0:c1], T.PI[:, c0:c1], T.HI[:, c0:c1], ALU.subtract), 2.0)
-        job = newjob()
-        mm([(slice(0, n), T.EH[:, :], HB[:, c0:c1], True, False, n), (slice(0, n), T.EL[:, :], LB[:, c0:c1], False, True, n)],
-           ["EH", "EL", ("HB", c0), ("LB", c0)], job)
-        w = wcol(c0 // 128)
-        move(n, [], [wkey(0, b) for b in bl], lambda job=job, w=w, n=n: (T.W0[:, w:w + n], ps(job)[:, 0:n]), job)
-        if c0 == 0:
-            send(0)
-            for i in late: ops[i]["after"] = len(ops) - 1
-    vec("cp", X, ["PIo", "PIt"], ["OUT"], lambda: (T.OUT[:, :], T.PI[:, :]))
-    dma("Y", T.yp[:, :], T.OUT[:, :], ["OUT"], ["yp"], 1500)
+    for (c0, c1, pk) in ((0, V, "PIo"), (V, X, "PIt")):
+        n = c1 - c0; w = wcol(c0 // 128)
+        vec("cp", n, [pk], [("OUT", c0)], lambda c0=c0, c1=c1: (T.OUT[:, c0:c1], T.PI[:, c0:c1]))
+        act(n, [("OUT", c0), "EB", "OWN"], [wkey(0, b) for b in range(c0 // 128, c1 // 128)],
+            lambda c0=c0, c1=c1, w=w, n=n: (T.W0[:, w:w + n], T.OUT[:, c0:c1], ACT.Exp, EB, 1.0 / STEP))
+        if c0 == 0: send(0)
+    dma("Y", T.yp[:, :], T.OUT[:, :], [("OUT", 0), ("OUT", V)], ["yp"], 1500)
 
     lk = ["LI0", "LI1", "LI2", "LI3"]
-    vec("ts", 224, lk, ["LM"], lambda: (T.LM[:, :], T.LI[:, :], float(M), 16.0, ge, ALU.mult))
-    vec("tt", 224, lk + ["LM"], ["LM"], lambda: (T.LM[:, :], T.LM[:, :], T.LI[:, :], ALU.add), 2.0)
-    for (d, s, n) in ((0, 0, 48), (48, 96, 16), (64, 48, 48), (112, 112, 112)):
-        vec("cp", n, ["LM"], [("LU", d)], lambda d=d, s=s, n=n: (T.LU[:, d:d + n], T.LM[:, s:s + n]))
-    luk = [("LU", d) for d in (0, 48, 64, 112)]
-    def cpcol(c, b): return (512 + 256 * c + 128 * b) if b < 2 else (1024 + 768 * c + 128 * (b - 2))
-    def cpkey(t, c, b): return ("GC", t, 0 if b < 2 else 1 + c)
-
-    def finish_top(b0, b1):
-        n = 8 * (b1 - b0); c = slice(8 * b0, 8 * b1); ak = [("A", b) for b in range(b0, b1)]; tk = [("TOP", b) for b in range(b0, b1)]
-        hi = T.A[:, 128 * b0 + 5:128 * b1:16]
-        vec("cp", n, tk, ak, lambda: (hi, T.TOP[:, c]))
-        vec("tt", n, tk + ak, ak, lambda: (T.A[:, 128 * b0 + 6:128 * b1:16], T.TOP[:, c], hi, ALU.subtract), 2.0)
-
-    def turn_back(t, b0, b1, tops=False):
-        parts = [(b0, b1)] if b1 - b0 <= 4 else [(b0, (b0 + b1) // 2), ((b0 + b1) // 2, b1)]
-        for (p0, p1) in parts:
-            job = newjob(); items = []; rd = ["ID"]
-            for b in range(p0, p1):
-                c = slice(128 * (b - p0), 128 * (b - p0 + 1)); rd.append(("A", b))
-                items.append((c, T.A[:, 128 * b:128 * b + 128], T.ID[:, :], True, t < 3, 128))
-                if t == 3:
-                    items.append((c, T.B[:, 128 * b:128 * b + 128], T.ID[:, :], False, True, 128)); rd.append(("B", b))
-            mm(items, rd, job)
-            n = 128 * (p1 - p0)
-            if t == 0: dst = D0[:, 128 * p0:128 * p1]; wr = [("D0", b) for b in range(p0, p1)]
-            elif tops: dst = T["OT%d" % t][:, :]; wr = [("OT", t)]
-            elif t < 3: dst = win(t)[:, wcol(p0):wcol(p0) + n]; wr = [wkey(t, b) for b in range(p0, p1)]
-            else: dst = T.OUT[:, 128 * p0:128 * p1]; wr = [("OUT2", b) for b in range(p0, p1)]; alias(wr, ["yp"])
-            move(n, [], wr, lambda job=job, dst=dst, n=n: (dst, ps(job)[:, 0:n]), job)
-        if t == 3:
-            for k in range(3):
-                dma("YGS"[k], T.yp[10 + k:128:16, 128 * b0:128 * b1], T.OUT[10 + k:128:16, 128 * b0:128 * b1],
-                    [("OUT2", b) for b in range(b0, b1)] + ["yp"], [])
+    vec("ts", 224, lk, ["LM"], lambda: (T.LM[:, :, :], T.LI[:, :, :], float(M), 16.0, ge, ALU.mult))
+    vec("tt", 448, lk + ["LM"], ["LM"], lambda: (T.LM[:, :, :], T.LM[:, :, :], T.LI[:, :, :], ALU.add))
+    vec("cp", 64, ["LM"], [("LU", 0)], lambda: (T.LU[:, 0:64], T.LM[:, 0:4, :]))
+    vec("cp", 32, ["LM"], [("LU", 1)], lambda: (T.LU[:, 96:128], T.LM[:, 12:14, :]))
+    def gb(P): return 512 + 512 * P if P else 0
+    for P in range(4):
+        o = 64 + gb(P) // 16
+        vec("cp", 32, ["LM"], [("LU", 2 + P)], lambda P=P, o=o: (T.LU[:, o:o + 32], T.LM[:, 4 + P:12:4, :]))
+    luk = [("LU", k) for k in range(6)]
 
     for h in range(2):
-        job = newjob(); bl = range(4 * h, 4 * h + 4)
-        mm([(slice(80 * i, 80 * i + 80), T.W0[:, wcol(b):wcol(b) + 128], T.DEC[:, :], True, True, 80) for i, b in enumerate(bl)],
-           ["DEC"] + [wkey(0, b) for b in bl], job)
-        a = SL[:, 1536 + 320 * h:1856 + 320 * h]; s = SL[:, 2176 + 320 * h:2496 + 320 * h]
-        ka = [("TA", h)]; kb = [("TS", h)]; tk = [("TOP", b) for b in bl]; gk = [("GI", b) for b in bl]
-        c = slice(32 * h, 32 * h + 32)
-        vec("ts", 320, [], ka, lambda job=job, a=a: (a, ps(job)[:, 0:320], 2500.0, 4000.0, ge, ALU.mult), job=job)
-        vec("tt", 320, ka, ka, lambda job=job, a=a: (a, a, ps(job)[:, 0:320], ALU.subtract), job=job)
-        vec("scan", 320, ka + ["P10"], kb, lambda a=a, s=s: (s, T.P10[:, :], a, 0.0, ALU.add, ALU.min))
-        vec("ts", 32, kb, gk, lambda h=h, c=c: (T.GI[:, c], SL[:, 2185 + 320 * h:2496 + 320 * h:10], -1.0, -HALF, ALU.mult, ALU.add))
-        vec("ts", 32, gk, tk, lambda c=c: (T.TOP[:, c], T.GI[:, c], -1.0, None, ALU.max))
-        finish_top(4 * h, 4 * h + 4)
-        turn_back(0, 4 * h, 4 * h + 4)
+        job = newjob("b"); bl = range(4 * h, 4 * h + 4); ak = [("A", b) for b in bl]; c = slice(320 * h, 320 * h + 320)
+        turn([(lambda p, i=i: p[:, i, :, :], T.W0[:, wcol(b):wcol(b) + 128]) for i, b in enumerate(bl)], ["ID"] + [wkey(0, b) for b in bl], job, ID)
+        move(512, [], ak, lambda job=job, h=h: (T.A[:, 4 * h:4 * h + 4, :, :], ps(job)[:, 0:4, :, :]), job, 0.5)
+        a = T.A[:, 4 * h:4 * h + 4, :, 0:10]
+        vec("ts", 160, ak, [("Y0", h)], lambda a=a, c=c: (T.Y0[:, c], a, THR, None, lt))
+        vec("tt", 640, ak + [("Y0", h)], [("Y1", h)], lambda a=a, c=c: (T.Y1[:, c], T.Y0[:, c], a, ALU.mult))
+        vec("scan", 160, [("Y1", h), "P10"], [("Y2", h)], lambda c=c: (T.Y2[:, c], T.P10[:, 0:320], T.Y1[:, c], 0.0, ALU.mult, ALU.max))
+        vec("cp", 32, [("Y2", h)], [("TOP", b) for b in bl], lambda h=h: (T.TOP[:, 32 * h:32 * h + 32], T.Y2[:, 320 * h + 9:320 * h + 320:10]))
 
-    def topl(t, b):
-        if t and b < 2: return T["OT%d" % t][:, 128 * b:128 * b + 128], ("OT", t)
-        return (D0[:, 128 * b:128 * b + 128], ("D0", b)) if t == 0 else (win(t)[:, wcol(b):wcol(b) + 128], wkey(t, b))
+    def source(t, b, i):
+        P, odd = divmod(b, 2); base = 2560 * P
+        if i >= 10:
+            c = gb(P) + 256 * (i - 10) + 128 * odd
+            return T["GC%d" % t][:, c:c + 128], [("GC", t, P)]
+        GE = T["GE%d" % t]
+        if odd and i >= 6: return GE[:, base + 2048 + i - 6:base + 2560:4], [("GE", t, P, 2)]
+        return GE[:, base + 10 * odd + i:base + 2048:16], [("GE", t, P, 0), ("GE", t, P, 1)]
 
-    def least(t, b, n, rtop, rkey, items, rd, pat, pkey, out, okey):
-        job = newjob(); l, lk_ = topl(t, b)
-        its = [(slice(0, n), l, rtop, True, False, n)] + [(c, a, r, False, x == len(items) - 1, k) for x, (c, a, r, k) in enumerate(items)]
-        mm(its, rd + [lk_, rkey], job)
-        act(n, [], [], lambda: (mk(job)[:, 0:n], ps(job)[:, 0:n], ACT.Relu, 122880.0, -131072.0), job)
-        vec("tt", n, [], [], lambda: (ps(job)[:, 0:n], ps(job)[:, 0:n], mk(job)[:, 0:n], ALU.add), job=job)
-        vec("scan", n, [pkey], [okey], lambda: (out, pat, ps(job)[:, 0:n], 0.0, ALU.add, ALU.min), job=job)
+    def members(t, P):
+        for x, (o, n) in enumerate(((0, 64), (64, 64), (128, 32))):
+            o += 160 * P
+            gather(T["GE%d" % t][:, 16 * o:16 * (o + n)], win(t)[:, 0:EWIN], T.O[:, o:o + n], 16 * n, objkeys(t) + [("O", P)], [("GE", t, P, x)])
 
-    def pair(t, b, i):
-        if i < 10:
-            cb, r = divmod(10 * b + i, 16)
-            return T["GE%d" % t][:, 2048 * cb + r:2048 * (cb + 1):16], [("GE", t, cb, 0), ("GE", t, cb, 1)]
-        c = cpcol(i - 10, b)
-        return T["GC%d" % t][:, c:c + 128], [cpkey(t, i - 10, b)]
+    def places(t, P):
+        n = 512 if P else 1024; c = gb(P)
+        gather(T["GC%d" % t][:, c:c + n], win(t)[:, 0:WIN], T.LU[:, 64 + c // 16:64 + (c + n) // 16], n, allkeys(t) + luk, [("GC", t, P)])
 
-    for t in range(3):
-        rnd[0] = t + 1
-        w = win(t); GC = T["GC%d" % t]; GE = T["GE%d" % t]
-        if t == 0:
-            for h in range(2):
-                gather(E[:, 512 * h:512 * h + 512], w[:, 0:WIN], T.LU[:, 160 + 32 * h:192 + 32 * h], 512, allkeys(0) + luk, [("E", h)])
-            for cbs in ((0,), (1,), (2, 3, 4)):
-                job = newjob(); items = []; rd = []
-                for x, cb in enumerate(cbs):
-                    bs = sorted(set(i // 10 for i in range(16 * cb, 16 * cb + 16)))
-                    for b in bs:
-                        j = (10 * b - 16 * cb + 8) // 2
-                        items.append((slice(128 * x, 128 * x + 128), T.PK[:, 128 * j:128 * j + 128], E[:, 128 * b:128 * b + 128], b == bs[0], b == bs[-1], 128))
-                        rd += [("PK", j), ("E", b // 4)]
-                mm(items, rd, job)
-                n = 128 * len(cbs)
-                vec("ts", n, [], [("O", cb) for cb in cbs],
-                    lambda job=job, n=n, c=128 * cbs[0]: (T.O[:, c:c + n], ps(job)[:, 0:n], -HALF, float(M), ALU.add, ALU.min), job=job)
-        else:
-            hs = range(2)
-            alias([("GL", t, h) for h in hs], [("HB" if t == 1 else "LB", c0) for c0 in (0, V, 640)])
-            if t == 1: alias([("SL", b) for b in range(8)], [("PT", j) for j in range(12)] + [(x, h) for x in ("TA", "TS") for h in hs])
-            else:
-                alias([("SL2", b) for b in range(8)], [("SL", b) for b in range(8)])
-                alias([("GN", 2, h) for h in hs], [("E", h) for h in hs])
-                alias([("GD", 2, 2, h) for h in hs], [("D0", b) for b in range(8)])
-            GL = T["GL%d" % t]; ON = T["ON%d" % t]; SEL = T["SEL%d" % t]
-            for h, (v0, v1) in enumerate(((0, V), (V, X))):
-                n = (v1 - v0) // 16; o0 = v0 // 16
-                gather(GL[:, v0:v1], w[:, 0:WIN], T.LU[:, 160 + o0:160 + o0 + n], v1 - v0, allkeys(t) + luk, [("GL", t, h)])
-                job = newjob()
-                mm([(slice(0, n), SEL[:, 128 * r:128 * r + 128], GL[:, v0 + r:v1:16], r == 0, r == 15, n) for r in range(16)],
-                   [("GL", t, h)] + [("SEL", t, j) for j in range(4)], job)
-                vec("ts", n, [], [("ON", t, h)], lambda job=job, n=n, o0=o0, ON=ON: (ON[:, o0:o0 + n], ps(job)[:, 0:n], float(M), None, ALU.min), job=job)
-                gather(T["GN%d" % t][:, v0:v1], T.W0[:, 0:EWIN], ON[:, o0:o0 + n], v1 - v0, objkeys(0) + [("ON", t, h)], [("GN", t, h)])
-                for u in range(1, t + 1):
-                    gather(T["GD%d%d" % (t, u)][:, v0:v1], w[:, 0:EWIN], T["ON%d" % u][:, o0:o0 + n], v1 - v0, objkeys(t) + [("ON", u, h)], [("GD", t, u, h)])
-        for x, (o0, n) in enumerate(((0, 64), (64, 48), (112, 48))):
-            gather(GC[:, 16 * o0:16 * (o0 + n)], w[:, 0:WIN], T.LU[:, o0:o0 + n], 16 * n, allkeys(t) + luk, [("GC", t, x)])
-        for cb in range(5):
-            for h in range(2):
-                o0 = 128 * cb + 64 * h
-                gather(GE[:, 16 * o0:16 * o0 + 1024], w[:, 0:EWIN], T.O[:, o0:o0 + 64], 1024, objkeys(t) + [("O", cb)], [("GE", t, cb, h)])
+    def loads(t, v0, v1):
+        gather(T["GL%d" % t][:, v0:v1], win(t)[:, 0:WIN], T.LU[:, v0 // 16:v1 // 16], v1 - v0, allkeys(t) + luk,
+               [("GL", t, P) for P in range(v0 // V, v1 // V)])
 
-        job = newjob(); n = 80 if t == 0 else 8
-        rhs = T.DEC[:, :] if t == 0 else T.DD[:, t - 1:16:2]
-        mm([(slice(n * b, n * b + n), GC[:, 128 * b:128 * b + 128], rhs, True, True, n) for b in range(2)], ["DEC", "DD", ("GC", t, 0)], job)
+    first_ln = [1500.0]
+    def ln(n, rd, wr, args, job=None):
+        act(n, rd, wr, lambda: args() + (ACT.Ln, 0.0, UP), job, first_ln[0]); first_ln[0] = 0.0
+
+    def gained(t, v0, v1):
+        n = (v1 - v0) // 16; o = v0 // 16; job = newjob("f"); pk = range(v0 // V, v1 // V)
+        GL = T["GL%d" % t]; LO = T["LO%d" % t]
+        mm([(lambda p: p[:, 0:n // 16, 0:16], shift(2 + t, r - 9 - t), GL[:, v0 + r:v1:16], r == 0, r == 15, n) for r in range(16)],
+           [("GL", t, P) for P in pk] + [("PM", 2 + t)], job)
+        ln(n, [], [("LO", t, v0)], lambda: (LO[:, o:o + n], ps(job)[:, 0:n // 16, 0:16]), job)
+        vec("ts", n, [("LO", t, v0)], [("ON", t, P) for P in pk], lambda: (T["ON%d" % t][:, o:o + n], LO[:, o:o + n], STEP, float(M), ALU.mult, ALU.min))
+
+    def named(buf, u, t, v0, v1):
+        pk = range(v0 // V, v1 // V)
+        gather(T[buf][:, v0:v1], win(t)[:, 0:EWIN], T["ON%d" % u][:, v0 // 16:v1 // 16], v1 - v0,
+               objkeys(t) + [("ON", u, P) for P in pk], [(buf, P) for P in pk])
+
+    def whole(buf, b0, b1, at, k, key):
+        job = newjob("b"); bl = range(b0, b1)
+        turn([(lambda p, i=b - b0: p[:, i, :, :], T[buf][:, 128 * b:128 * b + 128]) for b in bl], ["ID"] + [(buf, b // 2) for b in bl], job, ID)
+        move(8 * k * len(bl), [], [(key, b) for b in bl], lambda: (T.SS[:, b0:b1, :, at:at + k], ps(job)[:, 0:b1 - b0, :, 0:k]), job, 0.5)
+
+    def gains(u, b, items, rd):
+        job = newjob("f"); n = len(items)
+        mm([(lambda p, i=i: p[:, 0:8, i], a, T.ID[:, 26 + u:154:16], True, True, 8) for i, a in enumerate(items)], ["ID"] + rd, job)
+        out = T.SS[:, b, :, R0 + 10 + u:R0 + 12 * n:12]
+        move(8 * n, [], [("Sg1" if u else "Sg0", b)], lambda: (out, ps(job)[:, 0:8, 0:n]), job)
+
+    def stores(t):
+        job = newjob("b"); GC = T["GC%d" % t]
+        turn([(lambda p, i=i: p[:, i, :, :], GC[:, 512 + 128 * i:640 + 128 * i]) for i in range(4)], ["ID", ("GC", t, 0)], job, ID)
+        move(192, [], ["Sy"], lambda: (T.SS[:, 0:2, :, 0:12], ps(job)[:, 2:4, :, 0:12]), job, 0.5)
         for b in range(2):
-            act(n, ["OWN"], ["AX"], lambda job=job, n=n, b=b: (T.AX[:, n * b:n * b + n], ps(job)[:, n * b:n * b + n], ACT.Abs, T.OWN[:, b:b + 1], 1.0), job)
-        if t == 0:
-            vec("scan", 160, ["AX", "P10"], ["SX"], lambda: (T.SX[:, :], T.P10[:, 0:160], T.AX[:, :], 0.0, ALU.add, ALU.min))
-            vec("cp", 16, ["SX"], ["NM"], lambda: (T.NM[:, :], T.SX[:, 9:160:10]))
-        else:
-            vec("tt", 16, ["AX", "NM"], ["NM"], lambda: (T.NM[:, :], T.NM[:, :], T.AX[:, 0:16], ALU.min), 2.0)
-        vec("ts", 16, ["NM"], ["NB"], lambda: (T.NB[:, :], T.NM[:, :], 0.5, BIG, ALU.is_gt, ALU.mult))
-        Ly = 10 if t == 0 else 20
-        for b in range(2):
-            n = 8 * Ly
-            items = [(slice(0, n, Ly // 10), T.GC0[:, 256 + 128 * b:384 + 128 * b], T.DEC[:, :], 80)]
-            if t: items.append((slice(1, n, 20 // t), GC[:, 256 + 128 * b:384 + 128 * b], T.DD[:, 0:16:2 // t], 8 * t))
-            least(t, b, n, T.R60[:, 0:480:6] if t == 0 else T["RY%d" % t][:, :], "R60" if t == 0 else "RY%d" % t, items,
-                  ["DEC", "DD", ("GC", 0, 0), ("GC", t, 0)], T.P60[:, 0:480:60 // Ly], "P60", T.SY[:, n * b:n * b + n], ("SY", b))
-        vec("tt", 16, [("SY", 0), ("SY", 1), "NB"], ["PY"], lambda Ly=Ly: (T.PY[:, :], T.SY[:, Ly - 1:16 * Ly:Ly], T.NB[:, :], ALU.add), 2.0)
+            vec("ts", 48, ["OWN"], [("AX", b)], lambda b=b: (T.AX[:, 96 * b:96 * b + 96], ps(job)[:, b, :, 0:12], T.OWN[:, b:b + 1], None, ALU.not_equal), job)
+        vec("scan", 96, [("AX", 0), ("AX", 1), "P12"], ["SX"], lambda: (T.SX[:, :], T.P12[:, 0:192], T.AX[:, :], 0.0, ALU.max, ALU.min))
 
-        for (b0, b1) in STATIC_GROUPS:
-            nb = b1 - b0; prs = [(i, b) for i in range(12) for b in range(b0, b1)]; base = 1056 * b0; oks = []
-            for x in range(0, len(prs), 5):
-                chunk = prs[x:x + 5]; n = 88 * len(chunk); c = slice(base + 88 * x, base + 88 * x + n); sk = ("SS", b0, x); ok = ("SO", b0, x); oks.append(ok)
-                rd = []; its = []; itm = []
-                for y, (i, b) in enumerate(chunk):
-                    a, k = pair(0, b, i); rd += k; cc = slice(88 * y, 88 * y + 88)
-                    its.append((cc, a, T.D88[:, :], True, True, 88))
-                    itm += [(cc, topl(t, b)[0], T.R88[:, :], True, False, 88), (cc, a, T.K88[:, :], False, True, 88)]
-                if t == 0:
-                    job = newjob(); mm(its, rd + ["D88"], job)
-                    move(n, [], [sk], lambda job=job, c=c, n=n: (T.SS[:, c], ps(job)[:, 0:n]), job)
-                job = newjob(); mm(itm, rd + ["K88", "R88"] + [topl(t, b)[1] for b in range(b0, b1)], job)
-                vec("scan", n, [sk], [ok], lambda job=job, c=c, n=n: (T.SO[:, c], T.SS[:, c], ps(job)[:, 0:n], 0.0, ALU.min, ALU.max), job=job)
-            m = 8 * nb; u = 48 * b0; uk = ("U", b0); hf = base + 528 * nb
-            vec("tt", 6 * m, oks, [uk], lambda u=u, m=m, base=base, hf=hf, nb=nb: (T.U[:, u:u + 6 * m], T.SO[:, base + 10:hf:11], T.SO[:, hf + 10:hf + 528 * nb:11], ALU.min), 2.0)
-            vec("tt", 3 * m, [uk], [uk], lambda u=u, m=m: (T.U[:, u:u + 3 * m], T.U[:, u:u + 3 * m], T.U[:, u + 3 * m:u + 6 * m], ALU.min), 2.0)
-            vec("tt", m, [uk], [uk], lambda u=u, m=m: (T.U[:, u:u + m], T.U[:, u:u + m], T.U[:, u + m:u + 2 * m], ALU.min), 2.0)
-            vec("tt", m, [uk], [("T0", b) for b in range(b0, b1)], lambda u=u, m=m, b0=b0: (T.T0[:, 8 * b0:8 * b0 + m], T.U[:, u:u + m], T.U[:, u + 2 * m:u + 3 * m], ALU.min), 2.0)
+    nout = [0]
+    def finish(t, b0, b1):
+        bl = range(b0, b1); n = 8 * (b1 - b0); K = 12 + t; end = R0 + 12 * K
+        s = 0 if b0 == 0 else R0; w = end - s
+        K += 2 if b0 == 0 else 0
+        line = 12 * K; so = 1536 * b0
+        def keys(s): return [(s, b) for b in bl]
+        for b in bl:
+            rd = [("Sa", b), ("Sb", b)] + (["Sy", "reset"] if b < 2 else []) + ([("Sg0", b), ("Sn1", b), "late"] if t else []) + ([("Sg1", b), ("Sn2", b)] if t == 2 else [])
+            def marks(e, q, b=b):
+                if e == "V": return [q.tensor_scalar(T.MK[:, b, g, s:end], T.SS[:, b, g, s:end], T.TOP[:, 8 * b + g:8 * b + g + 1], None, ALU.is_le) for g in range(8)]
+                return [q.activation(T.MK[:, b, g, s:end], T.SS[:, b, g, s:end], ACT.Sign, bias=T.TOP[:, 8 * b + g:8 * b + g + 1], scale=-0.995) for g in range(8)]
+            def scans(e, q, b=b):
+                return [q.tensor_tensor_scan(T.SO[:, c - w:c], T.SS[:, b, g, s:end], T.MK[:, b, g, s:end], 1.0, ALU.min, ALU.max)
+                        for g in range(8) for c in [so + line * (8 * (b - b0) + g + 1)]]
+            op("VS", {"V": 8 * vt(w / 2), "S": 8 * st(w)}, marks, rd + [("TOP", b)], [("MK", b)]); ops[-1]["ni"] = 8
+            op("V", 8 * vt(w / 2), scans, rd + [("MK", b)], [("SO", b)]); ops[-1]["ni"] = 8
+        c0 = 128 * b0; ends = T.TS[:, c0 + K - 1:c0 + n * K:K]; p0 = K - 1 if b0 == 0 else 0
+        vec("scan", n * K / 2, keys("SO") + ["P%d" % K], keys("TS"),
+            lambda: (T.TS[:, c0:c0 + n * K], T["P%d" % K][:, p0:p0 + n * K], T.SO[:, so + 11:so + n * line:12], 0.0, ALU.max, ALU.min))
+        gain = T.A[:, b0:b1, :, 10 + t]; gk = keys("A")
+        if b0 == 0:
+            vec("tt", 32, keys("SO") + ["SX"], ["PY"], lambda: (T.PY[:, :], T.SO[:, 22:n * line:line], T.SX[:, 11:192:12], ALU.max))
+            if t == 1:
+                vec("tt", 32, keys("TS") + ["PY"], ["GXO"], lambda: (GXO, ends, T.PY[:, :], ALU.min))
+                send(2)
+                vec("cp", n, ["GXO"], gk, lambda: (gain, GXO))
+            else: vec("tt", 32, keys("TS") + ["PY"], gk, lambda: (gain, ends, T.PY[:, :], ALU.min))
+        elif t < 2: vec("cp", n, keys("TS"), gk, lambda: (gain, ends))
+        else: gain = ends; gk = keys("TS")
+        if t < 2:
+            if t == 0 or b0:
+                job = newjob("b"); wc = wcol(b0)
+                turn([(lambda p, i=b - b0: p[:, i, :, :], T.A[:, b, :, :]) for b in bl], ["ID"] + gk, job, ID)
+                move(16 * n, [], [wkey(t + 1, b) for b in bl], lambda: (win(t + 1)[:, wc:wc + 16 * n], ps(job)[:, 0:b1 - b0, :, :]), job, 0.5)
+                if b0 == 0: send(1)
+            c = slice(8 * b0, 8 * b1)
+            vec("ts", n, gk, keys("T1"), lambda: (T.T1[:, c], gain, THR, None, lt))
+            vec("tt", 2 * n, gk + keys("T1"), keys("T2"), lambda: (T.T2[:, c], T.T1[:, c], gain, ALU.mult))
+            vec("tt", 2 * n, keys("T2") + keys("TOP"), keys("TOP"), lambda: (T.TOP[:, c], T.TOP[:, c], T.T2[:, c], ALU.max))
+        if t == 2: output(2, b0, b1, gain, gk)
 
-        L = [0, 30, 50][t]
-        for b in range(8 if t else 0):
-            n = 8 * L; items = []; rd = ["DEC", "DD"]; offs = [None, off1, off2][t]; hb = 0 if b < 2 else 1
-            dd = T.DD[:, 0:16:2 // t]
+    def affine(n, rd, wr, args, scale, bias, job=None):
+        def fn(e, q):
+            o, i = args()
+            return [q.tensor_scalar(o, i, scale, bias, ALU.mult, ALU.add) if e == "V" else q.activation(o, i, ACT.Identity, bias=bias, scale=scale)]
+        op("VS", {"V": vt(n), "S": st(n)}, fn, rd, wr, job)
+
+    def output(t, b0, b1, gain, gk):
+        n = 8 * (b1 - b0); c = slice(64 * t + 8 * b0, 64 * t + 8 * b1); k = nout[0]; nout[0] += 1
+        ln(n, gk, [("LG", k)], lambda: (T.LG[:, c], gain))
+        affine(n, [("LG", k)], [("GF", k)], lambda: (T.GF[:, c], T.LG[:, c]), STEP, MAGIC)
+        job = newjob("f")
+        turn([(lambda p: p[0:n, 0:4, :], T.GF[:, c])], ["IDF", ("GF", k)], job, T.IDF[:, :], 4)
+        affine(128, [], [("FO", k)], lambda: (T.FO[0:n, 128 * k:128 * k + 128], ps(job)[0:n, 0:4, :]), 1.0, -MAGIC, job)
+        for b in range(b0, b1):
+            dma("YS"[b % 2] if t == 2 else "Y", T.yp[10 + t:128:16, 128 * b:128 * b + 128], T.FO[8 * (b - b0):8 * (b - b0) + 8, 128 * k:128 * k + 128],
+                [("FO", k), "yp"], [], kind="fin")
+
+    rnd[0] = 1
+    loads(0, 0, V); loads(0, V, X)
+    for P in range(4):
+        job = newjob("f"); E = T.GL0; e = V * P
+        mm([(lambda p: p[:, 0:4, :], shift(0, 0), E[:, e:e + 128], True, False, 128), (lambda p: p[:, 0:4, :], shift(1, 10), E[:, e + 128:e + 256], False, True, 128)]
+           + [(lambda p: p[:, 4, :], shift(2, 4 * x - 6), E[:, e + 128 + x:e + 256:4], x == 0, x == 3, 32) for x in range(4)],
+           [("GL", 0, P), ("PM", 0), ("PM", 1), ("PM", 2)], job)
+        c = slice(160 * P, 160 * P + 160)
+        ln(160, [], [("LN", P)], lambda job=job, c=c: (T.LN[:, c], ps(job)[:, 0:5, :]), job)
+        vec("ts", 160, [("LN", P)], [("O", P)], lambda c=c: (T.O[:, c], T.LN[:, c], STEP, float(M), ALU.mult, ALU.min))
+        places(0, P); members(0, P)
+    for b in range(8):
+        for (i0, i1, key) in ((0, 8, "Sa"), (8, 12, "Sb")):
+            job = newjob("b"); rd = ["ID"]; items = []
+            for i in range(i0, i1):
+                a, k = source(0, b, i); rd += k; items.append((lambda p, x=i - i0: p[:, :, x, :], a))
+            turn(items, rd, job, ID)
+            move(96 * (i1 - i0), [], [(key, b), ("Sg0", b)], lambda job=job, b=b, i0=i0, i1=i1: (T.SS[:, b, :, R0 + 12 * i0:R0 + 12 * i1], ps(job)[:, :, 0:i1 - i0, 0:12]), job, 0.5)
+    stores(0)
+    for r in RANGES[0]: finish(0, *r)
+    output(0, 0, 8, T.A[:, :, :, 10], [("A", b) for b in range(8)])
+
+    rnd[0] = 2
+    def first_gains(t, b):
+        items = []; rd = []
+        for i in range(12):
+            a, k = source(t if i < 10 else 1, b, i); items.append(a); rd += k
+        gains(0, b, items, rd)
+    for (v0, v1) in LOADS[1]:
+        loads(1, v0, v1); gained(1, v0, v1)
+    for P in range(4): places(1, P)
+    for P in range(EARLY // 2):
+        members(1, P); named("GA", 1, 1, V * P, V * P + V); whole("GA", 2 * P, 2 * P + 2, RN, 11, "Sn1")
+        for b in (2 * P, 2 * P + 1): first_gains(1, b)
+    stores(1)
+    for r in RANGES[1]:
+        if r[0] < EARLY: finish(1, *r)
+    for h in range(2):
+        job = newjob("b")
+        turn([(lambda p, i=i: p[:, i, :, :], T.W1[:, 1024 * h + 128 * i:1024 * h + 128 * i + 128]) for i in range(8)], ["ID"] + objkeys(1), job, ID)
+        move(1024, [], [("AT", h)], lambda job=job, h=h: (T.AT[:, 8 * h:8 * h + 8, :, :], ps(job)[:, :, :, :]), job, 0.5)
+    for h in range(2):
+        vec("cp", 64, [("arr", 2), "GXO"], [("AT", h)], lambda h=h: (T.AT[:, 8 * h:8 * h + 8, :, 11], T.GX[:, 64 * h:64 * h + 64]))
+        job = newjob("b")
+        turn([(lambda p, i=i: p[:, i, :, :], T.AT[:, 8 * h + i, :, :]) for i in range(8)], ["ID", ("AT", h)], job, ID)
+        move(1024, [], [("obj", h)], lambda job=job, h=h: (T.W2[:, 1024 * h:1024 * h + 1024], ps(job)[:, :, :, :]), job, 0.5)
+    for P in list(range(EARLY // 2, 4)) + list(range(EARLY // 2)):
+        members(2, P); named("GB", 1, 2, V * P, V * P + V)
+        if P >= EARLY // 2:
+            whole("GB", 2 * P, 2 * P + 2, RN, 11, "Sn1")
+            for b in (2 * P, 2 * P + 1): first_gains(2, b)
+    for r in RANGES[1]:
+        if r[0] >= EARLY: finish(1, *r)
+    output(1, 0, 8, T.A[:, :, :, 11], [("A", b) for b in range(8)])
+
+    rnd[0] = 3
+    for (v0, v1) in LOADS[2]:
+        loads(2, v0, v1); gained(2, v0, v1); named("GN", 2, 2, v0, v1)
+    for P in range(4):
+        places(2, P); whole("GN", 2 * P, 2 * P + 2, R2, 12, "Sn2")
+        for b in (2 * P, 2 * P + 1):
+            items = []; rd = [("GB", P)]
             for i in range(12):
-                a, k = pair(t, b, i); rd += k
-                items.append((slice(offs[i], n, L // t), a, dd, 8 * t))
-            for u in range(1, t + 1):
-                items.append((slice(offs[11 + u], n, L // t), T["GD%d%d" % (t, u)][:, 128 * b:128 * b + 128], dd, 8 * t))
-                items.append((slice(u - 1, n, L // 10), T["GN%d" % u][:, 128 * b:128 * b + 128], T.DEC[:, :], 80))
-                rd += [("GD", t, u, hb), ("GN", u, hb)]
-            least(t, b, n, T["R%d" % L][:, :], "R%d" % L, items, rd, T.P60[:, 0:480:2] if t == 1 else T.P50[:, :],
-                  "P60" if t == 1 else "P50", SL[:, n * b:n * b + n], ("SL", b) if t == 1 else ("SL2", b))
-
-        for (b0, b1) in (FINAL_GROUPS if t == 2 else ROUND_GROUPS):
-            bl = range(b0, b1); n = 8 * (b1 - b0); c = slice(8 * b0, 8 * b1)
-            def keys(s, bl=bl): return [(s, b) for b in bl]
-            t0 = T.T0[:, c]; t1 = T.T1[:, c]; t2 = T.T2[:, c]; gi = T.GI[:, c]; top = T.TOP[:, c]
-            if b0 == 0:
-                ko = [("T0", 0), ("T0", 1)]
-                vec("tt", 16, ["PY", ("TOP", 0), ("TOP", 1)], ["PY"], lambda: (T.PY[:, :], T.PY[:, :], T.TOP[:, 0:16], ALU.add), 2.0)
-                vec("tt", 16, ["PY"] + ko, ko, lambda: (T.T0[:, 0:16], T.T0[:, 0:16], T.PY[:, :], ALU.min), 2.0)
-            if t:
-                vec("tt", n, keys("SL" if t == 1 else "SL2") + keys("TOP"), keys("T1"),
-                    lambda t1=t1, top=top, b0=b0, b1=b1, L=L: (t1, top, SL[:, 8 * L * b0 + L - 1:8 * L * b1:L], ALU.add), 2.0)
-                vec("tt", n, keys("T1") + keys("T0"), keys("T0"), lambda t1=t1, t0=t0: (t0, t0, t1, ALU.min), 2.0)
-            vec("ts", n, keys("T0"), keys("GI"), lambda t0=t0, gi=gi: (gi, t0, -HALF, float(NONE), ALU.add, ALU.min))
-            hi = T.A[:, 128 * b0 + 10 + t:128 * b1:16]; lob = T.B[:, 128 * b0 + 10 + t:128 * b1:16]
-            vec("cp", n, keys("GI"), keys("A"), lambda hi=hi, gi=gi: (hi, gi))
-            if t < 2:
-                lo = T.A[:, 128 * b0 + 2 + t:128 * b1:16]
-                vec("tt", n, keys("GI") + keys("A"), keys("A"), lambda lo=lo, hi=hi, gi=gi: (lo, gi, hi, ALU.subtract), 2.0)
-                if b0 == 0:
-                    turn_back(t + 1, b0, b1); send(t + 1)
-                vec("ts", n, keys("GI"), keys("T2"), lambda t2=t2, gi=gi: (t2, gi, float(NONE), -4000.0, ge, ALU.mult))
-                vec("tt", n, keys("GI") + keys("T2"), keys("T2"), lambda t2=t2, gi=gi: (t2, t2, gi, ALU.add), 2.0)
-                vec("tt", n, keys("TOP") + keys("T2"), keys("TOP"), lambda t2=t2, top=top: (top, top, t2, ALU.max), 2.0)
-                finish_top(b0, b1)
-                turn_back(t + 1, b0, b1, b0 == 0)
-                vec("cp", n, keys("A"), keys("B"), lambda lo=lo, lob=lob: (lob, lo))
-            else:
-                vec("tt", n, keys("GI") + keys("A"), keys("B"), lambda lob=lob, hi=hi, gi=gi: (lob, gi, hi, ALU.subtract), 2.0)
-                turn_back(3, b0, b1)
+                a, k = source(2, b, i); items.append(a); rd += k
+            gains(1, b, items + [T.GB[:, 128 * b:128 * b + 128]], rd)
+    stores(2)
+    for r in RANGES[2]: finish(2, *r)
     return ops
 
 
-def order(ops, bias=BIAS, slack=SLACK, bonus=BONUS):
-    n = len(ops)
-    succ = [[] for _ in range(n)]
-    for i, o in enumerate(ops):
-        for d in o["deps"]: succ[d].append(i)
-    level = [0.0] * n
-    for i in range(n - 1, -1, -1):
-        o = ops[i]; d = o["dur"]["V"] if o["eng"] == "VS" else o["dur"]
-        level[i] = d + o["lat"] + LAT + bonus.get(o["cls"], 0.0) + bonus.get(o["fine"] + ".", 0.0) + max([level[s] for s in succ[i]] + [0.0])
-    left = [len(o["deps"]) for o in ops]
-    ready = [i for i in range(n) if left[i] == 0]
-    free = {e: 0.0 for e in "VSPGY"}
-    done = [0.0] * n
-    bank = [[0.0, None, True] for _ in range(NBANK)]
+def order(ops):
+    if ORDER:
+        v = [SIGNS.index(ORDER[k]) * 62 + SIGNS.index(ORDER[k + 1]) for k in range(0, len(ORDER), 2)]
+    else:
+        v = [2 * i for i in range(len(ops))]
+    free = {"b": [[k, None] for k in range(NB16)], "f": [[k, None] for k in range(NF32)]}
     seq = []
-    while ready:
-        cand = []
-        for i in ready:
-            o = ops[i]
-            if o["after"] is not None and "on" not in ops[o["after"]]: continue
-            t0 = max([done[d] + LAT for d in o["deps"]] + [0.0])
-            bk = None
-            if o["job"] is not None and o["job"][1][0] == i:
-                fr = [k for k in range(NBANK) if bank[k][2]]
-                if not fr: continue
-                bk = min(fr, key=lambda k: bank[k][0]); t0 = max(t0, bank[bk][0] + LAT)
-            if o["eng"] == "VS":
-                e = bonus.get(o["fine"] + "@") or min("VS", key=lambda x: max(t0, free[x]) + o["dur"][x] + (bias if x == "V" else 0.0)); d = o["dur"][e]
-            else:
-                e = o["eng"]; d = o["dur"]
-            cand.append((max(t0, free[e]), i, e, d, bk))
-        cand = [c for c in cand if c[3] < 700.0 or not any(x[2] == c[2] and level[x[1]] > level[c[1]] + URGENT and x[0] < c[0] + AHEAD * c[3] for x in cand)]
-        tmin = min(c[0] for c in cand)
-        s, i, e, d, bk = max([c for c in cand if c[0] <= tmin + slack], key=lambda c: level[c[1]])
-        o = ops[i]; o["on"] = e
-        if bk is not None:
-            o["job"][2] = bk
-            if bank[bk][1] is not None: o["deps"][bank[bk][1]] = True
-            bank[bk][2] = False
-        free[e] = s + d; done[i] = s + d + o["lat"]; o["at"] = s
-        if o["job"] is not None and o["job"][1][-1] == i:
-            bank[o["job"][2]] = [done[i], i, True]
-        seq.append(i); ready.remove(i)
-        for x in succ[i]:
-            left[x] -= 1
-            if left[x] == 0: ready.append(x)
-    return seq, max(done)
+    for x in v:
+        i = x // 2; o = ops[i]; job = o["job"]
+        o["on"] = "VS"[x % 2] if o["eng"] == "VS" else o["eng"]
+        if job is not None:
+            if job[1][0] == i:
+                job[2], last = free[job[3]].pop(0)
+                if last is not None: o["deps"][last] = True
+            if job[1][-1] == i: free[job[3]].append([job[2], i])
+        seq.append(i)
+    return seq
 
 
 def rank_program(g, core, T, topo):
@@ -486,7 +418,7 @@ def rank_program(g, core, T, topo):
     if rank is None:
         return
     ops = plan(T, topo, rank, core)
-    seq, _ = order(ops)
+    seq = order(ops)
     queue = {"V": g.vector, "S": g.scalar, "P": g.tensor, "G": g, "Y": g.sync}
     csem = {"V": "cv", "S": "cs", "P": "cp", "G": "cg"}
     count = {}
@@ -513,6 +445,8 @@ def rank_program(g, core, T, topo):
         elif o["kind"] == "dma":
             s = "dm%d" % ndma; ndma += 1
             ins[0].then_inc(T.sem[s], 16); count[s] = 16; o["sig"] = (s, 16)
+        elif o["kind"] == "fin":
+            ins[0].then_inc(T.sem.fin, 16); count["fin"] = count.get("fin", 0) + 16
         else:
             t = o["kind"][1]
             o["sig"] = ("arr%d" % t, nin); count["arr%d" % t] = nin; count["snt%d" % t] = nin

@@ -10,9 +10,9 @@ STEP, ZERO = 64.0, 2880.0
 UP = math.exp(ZERO / STEP)
 THR = math.exp(-5.0)
 MAGIC = 12582912.0
-R0, RN, R2, L = 13, 157, 169, 182
-NB16, NF32 = 4, 4
-EARLY = 6
+KB = 2.0 ** 71
+L1, L2, L3, LY = 27, 24, 30, 13
+BANKS = {"b": 3, "a": 2, "d": 3}
 
 
 def _sb(n, d): return ("sbuf", [128] + (n if isinstance(n, list) else [n]), d)
@@ -23,24 +23,27 @@ for _d, _l in (
     ("int32", dict(PI=X, LI=[14, 16], LM=[14, 16], CI=2)),
     ("uint16", dict(LU=224, O=640, ON1=64, ON2=64)),
     ("float32", dict(OUT=X, IDF=128, CF=8, OWF=4, LN=640, LO1=64, LO2=64, LG=192, GF=192, FO=1024)),
-    ("bfloat16", dict(W0=2848, W1=2848, W2=2848, GE0=10240, GE1=1280 * EARLY, GE2=10240, GC0=2560, GC1=2560, GC2=2560,
-                      GL0=X, GL1=X, GL2=X, GA=X, GB=X, GN=X, SS=[8, 8, L], MK=[8, 8, L], SO=12288, A=[8, 8, 16], AT=[16, 8, 16], GX=128,
-                      Z=160, ID=160, PM0=160, PM1=160, PM2=160, PM3=160, PM4=160, OWN=4, P10=320, P12=304, P13=336, P14=352, P15=256, P16=272,
-                      TS=1024, AX=192, SX=192, PY=16, Y0=640, Y1=640, Y2=640, T1=64, T2=64, TOP=64)),
+    ("bfloat16", dict(W0=2848, W1=2848, W2=2848, GE0=10240, GE1=2560, GE2=10240, GC0=2560, GC1=2560, GC2=2560,
+                      GL0=X, GL1=X, GL2=X, GA=V, GB=X, GN=X, SS=[8, 8, 120], MK=[8, 8, 120], SO=7680, TS=768, S3=[8, 8, 4], A=[8, 8, 16],
+                      DL1=64 * L1, DL2=64 * L2, DL3=64 * L3, DO=64 * L3, DT=64 * L1, T3=64, DY=16 * LY, DZ=16 * LY, TT=1536, TOP=64,
+                      R1=16 * L1, R2=16 * L2, R3=16 * L3, RY=16 * LY, NK=128, I3=[8, 16], C12=96, C11=88, C2=16, Z=16 * L3,
+                      ID=160, PM0=160, PM1=160, PM2=160, PM3=160, PM4=160, OWN=4, P10=320, P12=192, P15=240, P27=432,
+                      AX=192, SX=192, PY=16, Y0=640, Y1=640, Y2=640, T1=64, T2=64)),
 ):
     for _k in _l: SCRATCH[_k] = _sb(_l[_k], _d)
-for _k in range(NB16): SCRATCH["PB%d" % _k] = ("psum", [128, 8, 8, 16], "bfloat16")
-for _k in range(NF32): SCRATCH["PF%d" % _k] = ("psum", [128, 16, 32], "float32")
+for _k in range(BANKS["b"]): SCRATCH["Pb%d" % _k] = ("psum", [128, 8, 8, 16], "bfloat16")
+for _k in range(BANKS["a"]): SCRATCH["Pa%d" % _k] = ("psum", [128, 8, 64], "float32")
+for _k in range(BANKS["d"]): SCRATCH["Pd%d" % _k] = ("psum", [128, 512], "float32")
 
 NDMA = 12
-SEMAPHORES = ["cv", "cs", "cp", "cg", "fin"] + ["arr%d" % t for t in range(3)] + ["snt%d" % t for t in range(3)] + ["dm%d" % k for k in range(NDMA)]
+SEMAPHORES = ["cv", "cs", "cp", "cg", "fin"] + [s + str(t) for s in ("arr", "snt") for t in range(3)] + ["dm%d" % k for k in range(NDMA)]
 
-CYC, PCYC, GATH, LAT = 0.95, 0.55, 1.56, 150.0
-DMA_NS, NET_NS, NF2 = 2300.0, 7000.0, 0.6
-RANGES = [[(0, 2), (2, 4), (4, 6), (6, 8)], [(0, 2), (2, 4), (4, 6), (6, 8)], [(0, 2), (2, 4), (4, 6), (6, 8)]]
+CYC, PCYC, GATH, LAT = 0.95, 0.5, 1.56, 150.0
+DMA_NS, NET_NS = 2300.0, 7000.0
+PAIRS = [(0, 2), (2, 4), (4, 6), (6, 8)]
 LOADS = [None, [(0, 256), (256, 1024)], [(0, 256), (256, 512), (512, 768), (768, 1024)]]
 SIGNS = "0123456789abcdefghijklmnopqrstuvwxyzABCDEFGHIJKLMNOPQRSTUVWXYZ"
-ORDER = "12000m1a030e0W0g0k0p16140c0i0a0q040s1i1u1x0S1A0C06080O1G0w1I0u1D1W1s0Y1e1Z1g1c0y1M1Q0M101q1m281O0I1S0A0K1k1K2b0Q0G1U200E1y2l222o2c2426181o2e2g2m342C2u2r2s2i2F2Q2T1E2G4k372y2A4m2x3i0U4o3k3q382N4q3s2L3m3o4s3u3w4u4y3y4w2P3G4A3f2U2Z334C4E3I4G4I2I3C3A3F4K303K3M3O2X3W4U4Y4W3Q4M3d3Y3h4O444c3S40503b464f52483U54434b4g4Q5g564j595k5C5i5H8Y6N5m5E5I5o5K5q5M926P4S5a5S5w5s5c5u5O5Q6m6o6C6L906r7I6s5y5U6Q6W706H7K7r7M6Y5A7O5Z6S6U727Q7S6v6w7W7U7p6z7Y827A807t6A7E84617u5W885e757a957w7C8a7G7y8C8G8E8I8c7c7e8K8696989c79778M9e6J6E9a8O7g8e9g8Q9p9n7k9q9t7i9k9i8g7n9F8k9u9P9J8i9x9y9Ba4a08ma662a28oa88q64aa8w9Q8sac9Dag8u9V6c6eae9T8S9Zaibe6aak66bgaKaMan9Gc5bj8ybkcaap9M8U6gcecgaVaq68bn9Lasc6c8aPbpcc8Ab4aWaZb6bydAaQaTci8WbDdEdCdGb9buckbqau6ibAbsbxb0dIbI9XcmbMbab3bEcscwbGbRaAbWcuc0bLbPcycocWcTbdcAcUdLawbSc3cYbVbZaIdedjcqd0ay6kdgcCd3dkcEdNdOdQaGd5d6dmd8aCdacHdScIcKdpddcNcRdqcOdVaEdsdudwdz"
+ORDER = "0k0m0e0p0016120g0q1e140c1w0s1z0U181k06040a02080i1A1C0u1o1a0y1F2i260Q0W1Q1u0w101S291O0C2l1m1g2a0E0O1U222c202e1i0G0I2g1c0Y0A1s240S2m4u4x1W1q1Y0K2o2q2s2v2y2T2B2w302M2E1K1I1M1G2P334y2C2H4A2Q2I3e4G3h2X4C2K4J2V373w2Y3y4E3s3u343A3E3C3G393b3d4K4S4W4M3I4U3K4Y4O3Q3M3S4Q503U3O3i523W543Y5m5a560M5q5o4a4c425s5c4640585u445e485w3p3n3l5O5g5i5S5y5A3r4e4i4m5Q5U4h5k5M4k4q5W4o5Y4s6g607b776k6i6m64626o665C6q786s6u6G8I7c7K8E7e7H7j7k7z7n7o6e7W6w7Y7g7O7J7M8c808V6J8R8K7Q8G8e88828a8g6y8M6K7S68846a7U8O8i866c8k6A5E8m968o6C7r7D7F8q8s7s6M7vbt925G5I6E8S988W8u948Y8w9abo9cbu90bq7w8y8AbE5K7BbR6PbNbAbGbC9f9tbcbI9A9g9i9l9n9r9o9v9K9O9M9Qbwae9Saiah9z9D9w9U8CaIakbKby9Wbg9YamaoaMaLaPcCaQcGa0a4bOa6bS9Ha8aqaScFascIaUcWaaaucSaybUa29FaWaAacaYcKbWawaCb2cYb0bicVdzaEb4aGcMdIdcd8dAe7bZdDdTd0b6b8dKbec0c2dEe5d2dedGbkbabmd4dUf2dbdNdOc5c6eYdgf4dXdYf0dpdRc86W6Q6Ye8cOe0cqf6cmctcofudqfwdi9IcQe3fqfScueadtd6dkduftf8fWdmcwfyfVdxfZeufaecfAeecyfCexeyg0eieBeleCegcAfcfEfHffg2emg4eEeoeqeGfJfhfiflfKg6esg9eIeKeNgagcgffpgjeOfMfReQeSfmcicecc6S6U72cg70ca74ggckfOeUeX"
 
 
 def plan(T, topo, rank, core):
@@ -70,7 +73,7 @@ def plan(T, topo, rank, core):
         njob[0] += 1
         return [njob[0], [], None, kind]
 
-    def ps(job): return T[("PB%d" if job[3] == "b" else "PF%d") % job[2]]
+    def ps(job): return T["P%s%d" % (job[3], job[2])]
     def gt(n): return 200 + 2 * n * CYC
     def vt(n): return max(64, n) * CYC + 10
     def st(n): return max(64, n) * CYC + 60
@@ -113,16 +116,15 @@ def plan(T, topo, rank, core):
     own0 = rank * V
     ID = T.ID[:, 16:144]
     NN = T.OWN[:, 2:3]
-    GXO = T.GX[:, 16 * rank:16 * rank + 16]
     def wcol(b): return own0 + 128 * b if b < 2 else TMP + 128 * (b - 2)
     def win(t): return [T.W0, T.W1, T.W2][t]
     def wkey(t, b): return ("win", t, b)
-    def objkeys(t): return [("obj", 0), ("obj", 1), ("none", t)] if t == 2 else [wkey(t, 0), wkey(t, 1), ("arr", t), ("none", t)]
+    def objkeys(t): return [wkey(t, 0), wkey(t, 1), ("arr", t), ("none", t)]
     def allkeys(t): return objkeys(t) + [("pad", t)] + [wkey(t, b) for b in range(2, 8)]
     def shift(k, d): return T["PM%d" % k][:, 16 - d:144 - d]
 
     def send(t):
-        src = win(t)[:, own0:own0 + V] if t < 2 else GXO
+        src = win(t)[:, own0:own0 + V]
         def fn(e, q):
             trs = []
             at = 0
@@ -135,11 +137,10 @@ def plan(T, topo, rank, core):
                 trs.append(RemoteDMATransfer(dst_ids=[DstId(rid=rid, pnc=pid)], dma_engine_mask=mask, remote_sem=T.sem["arr%d" % t], src=src, dst=src))
             q.remote_dma_fused(trs, local_sem=T.sem["snt%d" % t])
             return []
-        op("G", 300.0, fn, [wkey(t, 0), wkey(t, 1)] if t < 2 else ["GXO"], [("arr", t)], kind=("net", t), lat=NET_NS)
-        ops[-1]["nf"] = NF2 if t == 2 else 1.0
+        op("G", 300.0, fn, [wkey(t, 0), wkey(t, 1)], [("arr", t)], kind=("net", t), lat=NET_NS)
 
     dma("Y", T.PI[:, 0:V], T.pts[:, 0:V], [], ["PIo"])
-    dma("S", T.PI[:, V:X], T.pts[:, V:X], [], ["PIt"], 500)
+    dma("Y", T.PI[:, V:X], T.pts[:, V:X], [], ["PIt"], 500)
     dma("Y", T.LI[:, 0:4, :], T.ld[:, :], [], ["LI0"])
     dma("Y", T.LI[:, 4:12, :], T.cp[:, :], [], ["LI1"])
     dma("Y", T.LI[:, 12, :], T.xs[:, :], [], ["LI2"])
@@ -147,10 +148,10 @@ def plan(T, topo, rank, core):
 
     ge, lt = ALU.is_ge, ALU.is_lt
     CI, CF = T.CI, T.CF
-    vec("ms", 80, [], ["Z"], lambda: (T.Z[:, :], 0.0))
+    vec("ms", 240, [], ["Z"], lambda: (T.Z[:, :], 0.0))
     op("G", gt(2), lambda e, q: [q.iota(T.OWF[:, 0:2], [[128, 2]], own0, 1, allow_small_or_imprecise_dtypes=True)], [], ["OWF0"])
     op("G", gt(1), lambda e, q: [q.iota(CI[:, 0:1], [[0, 1]], 0, 1)], [], ["CI0"])
-    op("G", gt(160), lambda e, q: [q.affine_select(T.ID[:, :], T.Z[:, :], [[1, 160]], ALU.not_equal, 1.0, -16, -1)], ["Z"], ["ID"])
+    op("G", gt(160), lambda e, q: [q.affine_select(T.ID[:, :], T.Z[:, 0:160], [[1, 160]], ALU.not_equal, 1.0, -16, -1)], ["Z"], ["ID"])
     vec("ms", 1, [], ["OWF1"], lambda: (T.OWF[:, 2:3], float(NONE)))
     vec("ms", 1, [], ["EB"], lambda: (T.OWF[:, 3:4], -ZERO / STEP))
     EB = T.OWF[:, 3:4]
@@ -171,12 +172,16 @@ def plan(T, topo, rank, core):
         vec("ms", 8, [], [("pad", t)], lambda t=t: (win(t)[:, M + 1:TMP], 0.0))
     vec("ms", 160, [], ["P10"], lambda: (T.P10[:, :], 1.0))
     vec("ms", 32, ["P10"], ["P10"], lambda: (T.P10[:, 0:320:10], 0.0))
-    for k in range(12, 17):
-        p = T["P%d" % k]; key = "P%d" % k; m = 25 if k < 15 else 17
-        vec("ms", m * k / 2, [], [key], lambda p=p: (p[:, :], 0.0))
-        vec("ts", m, ["Z", "OWN", key], [key], lambda p=p, k=k, m=m: (p[:, 0:m * k:k], T.Z[:, 0:m], NN, None, ALU.add))
-    vec("ts", 64, ["Z", "OWN"], ["late"], lambda: (T.SS[:, :, :, RN + 11], T.Z[:, 0:64], NN, None, ALU.add))
-    vec("ms", 8, [], ["reset"], lambda: (T.SS[:, 0:2, :, R0 - 1], -1.0))
+    for k in (12, 15, 27):
+        p = T["P%d" % k]; key = "P%d" % k
+        vec("ms", 8 * k, [], [key], lambda p=p: (p[:, :], 0.0))
+        vec("ts", 16, ["Z", "OWN", key], [key], lambda p=p, k=k: (p[:, 0:16 * k:k], T.Z[:, 0:16], NN, None, ALU.add))
+    vec("ms", 32, [], ["reset"], lambda: (T.S3[:, :, :, 0], -1.0))
+    vec("ts", 32, ["Z", "OWN"], [("S3", 2, b) for b in range(8)], lambda: (T.S3[:, :, :, 3], T.Z[:, 0:64], NN, None, ALU.add))
+    vec("ts", 64, ["ID"], ["NK"], lambda: (T.NK[:, :], ID, -KB, None, ALU.mult))
+    vec("cp", 64, ["ID"], ["I3"], lambda: (T.I3[:, :, :], ID))
+    for (k, r0, r1) in (("C12", 0, 12), ("C11", 0, 11), ("C2", 10, 12)):
+        vec("cp", 48, ["I3"], [k], lambda k=k, r0=r0, r1=r1: (T[k][:, :], T.I3[:, :, r0:r1]))
 
     for (c0, c1, pk) in ((0, V, "PIo"), (V, X, "PIt")):
         n = c1 - c0; w = wcol(c0 // 128)
@@ -184,7 +189,10 @@ def plan(T, topo, rank, core):
         act(n, [("OUT", c0), "EB", "OWN"], [wkey(0, b) for b in range(c0 // 128, c1 // 128)],
             lambda c0=c0, c1=c1, w=w, n=n: (T.W0[:, w:w + n], T.OUT[:, c0:c1], ACT.Exp, EB, 1.0 / STEP))
         if c0 == 0: send(0)
-    dma("Y", T.yp[:, :], T.OUT[:, :], [("OUT", 0), ("OUT", V)], ["yp"], 1500)
+    for (k, n) in (("RY", LY), ("R1", L1), ("R2", L2), ("R3", L3)):
+        op("G", gt(16 * n), lambda e, q, k=k, n=n: [q.affine_select(T[k][0:16, :], T.Z[0:16, 0:16 * n], [[8, 2], [1, 8], [0, n]], ALU.not_equal, KB * 1.0078125, 0, -1)],
+           ["Z", ("arr", 0)], [k])
+    dma("Y", T.yp[:, :], T.OUT[:, :], [("OUT", 0), ("OUT", V), ("arr", 0)], ["yp"], 1500)
 
     lk = ["LI0", "LI1", "LI2", "LI3"]
     vec("ts", 224, lk, ["LM"], lambda: (T.LM[:, :, :], T.LI[:, :, :], float(M), 16.0, ge, ALU.mult))
@@ -234,11 +242,11 @@ def plan(T, topo, rank, core):
         act(n, rd, wr, lambda: args() + (ACT.Ln, 0.0, UP), job, first_ln[0]); first_ln[0] = 0.0
 
     def gained(t, v0, v1):
-        n = (v1 - v0) // 16; o = v0 // 16; job = newjob("f"); pk = range(v0 // V, v1 // V)
+        n = (v1 - v0) // 16; o = v0 // 16; job = newjob("d"); pk = range(v0 // V, v1 // V)
         GL = T["GL%d" % t]; LO = T["LO%d" % t]
-        mm([(lambda p: p[:, 0:n // 16, 0:16], shift(2 + t, r - 9 - t), GL[:, v0 + r:v1:16], r == 0, r == 15, n) for r in range(16)],
+        mm([(lambda p: p[:, 0:n], shift(2 + t, r - 9 - t), GL[:, v0 + r:v1:16], r == 0, r == 15, n) for r in range(16)],
            [("GL", t, P) for P in pk] + [("PM", 2 + t)], job)
-        ln(n, [], [("LO", t, v0)], lambda: (LO[:, o:o + n], ps(job)[:, 0:n // 16, 0:16]), job)
+        ln(n, [], [("LO", t, v0)], lambda: (LO[:, o:o + n], ps(job)[:, 0:n]), job)
         vec("ts", n, [("LO", t, v0)], [("ON", t, P) for P in pk], lambda: (T["ON%d" % t][:, o:o + n], LO[:, o:o + n], STEP, float(M), ALU.mult, ALU.min))
 
     def named(buf, u, t, v0, v1):
@@ -246,66 +254,100 @@ def plan(T, topo, rank, core):
         gather(T[buf][:, v0:v1], win(t)[:, 0:EWIN], T["ON%d" % u][:, v0 // 16:v1 // 16], v1 - v0,
                objkeys(t) + [("ON", u, P) for P in pk], [(buf, P) for P in pk])
 
-    def whole(buf, b0, b1, at, k, key):
-        job = newjob("b"); bl = range(b0, b1)
-        turn([(lambda p, i=b - b0: p[:, i, :, :], T[buf][:, 128 * b:128 * b + 128]) for b in bl], ["ID"] + [(buf, b // 2) for b in bl], job, ID)
-        move(8 * k * len(bl), [], [(key, b) for b in bl], lambda: (T.SS[:, b0:b1, :, at:at + k], ps(job)[:, 0:b1 - b0, :, 0:k]), job, 0.5)
+    def tt(t, b0): return T.TT[0:16, 512 * t + 64 * b0:512 * t + 64 * b0 + 128]
 
-    def gains(u, b, items, rd):
-        job = newjob("f"); n = len(items)
-        mm([(lambda p, i=i: p[:, 0:8, i], a, T.ID[:, 26 + u:154:16], True, True, 8) for i, a in enumerate(items)], ["ID"] + rd, job)
-        out = T.SS[:, b, :, R0 + 10 + u:R0 + 12 * n:12]
-        move(8 * n, [], [("Sg1" if u else "Sg0", b)], lambda: (out, ps(job)[:, 0:8, 0:n]), job)
+    def tops(t, b0):
+        job = newjob("b")
+        turn([(lambda p: p[0:16, 0, :, :], T.TOP[:, 8 * b0:8 * b0 + 16])], ["ID", ("TOP", b0), ("TOP", b0 + 1)], job, ID)
+        move(128, [], [("TT", t, b0)], lambda: (tt(t, b0), ps(job)[0:16, 0, :, :]), job, 0.5)
+
+    def marked(t, b0, line, out, r, n, rd, wr):
+        job = newjob("d")
+        mm([(lambda p: p[:, 0:n], tt(t, b0), r, True, False, n), (lambda p: p[:, 0:n], T.NK[:, :], line, False, True, n)], rd + ["NK", ("TT", t, b0)], job)
+        vec("scan", n, rd, wr, lambda: (out, line, ps(job)[:, 0:n], 1.0, ALU.min, ALU.max), job)
 
     def stores(t):
         job = newjob("b"); GC = T["GC%d" % t]
-        turn([(lambda p, i=i: p[:, i, :, :], GC[:, 512 + 128 * i:640 + 128 * i]) for i in range(4)], ["ID", ("GC", t, 0)], job, ID)
-        move(192, [], ["Sy"], lambda: (T.SS[:, 0:2, :, 0:12], ps(job)[:, 2:4, :, 0:12]), job, 0.5)
+        turn([(lambda p, i=i: p[:, i, :, :], GC[:, 512 + 128 * i:640 + 128 * i]) for i in range(2)], ["ID", ("GC", t, 0)], job, ID)
         for b in range(2):
-            vec("ts", 48, ["OWN"], [("AX", b)], lambda b=b: (T.AX[:, 96 * b:96 * b + 96], ps(job)[:, b, :, 0:12], T.OWN[:, b:b + 1], None, ALU.not_equal), job)
-        vec("scan", 96, [("AX", 0), ("AX", 1), "P12"], ["SX"], lambda: (T.SX[:, :], T.P12[:, 0:192], T.AX[:, :], 0.0, ALU.max, ALU.min))
+            vec("ts", 48, ["OWN"], [("AX", b)], lambda b=b, job=job: (T.AX[:, 96 * b:96 * b + 96], ps(job)[:, b, :, 0:12], T.OWN[:, b:b + 1], None, ALU.not_equal), job)
+        vec("scan", 96, [("AX", 0), ("AX", 1), "P12"], ["SX"], lambda: (T.SX[:, :], T.P12[:, :], T.AX[:, :], 0.0, ALU.max, ALU.min))
+        job = newjob("a"); items = []
+        for b in range(2):
+            items += [(lambda p, b=b: p[:, :, 16 * b], ID, T.S3[:, b, :, 0], True, True, 8),
+                      (lambda p, b=b: p[:, :, 16 * b + 1:16 * b + LY], GC[:, 768 + 128 * b:896 + 128 * b], T.C12[:, :], True, True, 96)]
+        mm(items, ["ID", "C12", "reset", ("GC", t, 0)], job)
+        for b in range(2):
+            move(8 * LY, [], [("DY", b)], lambda b=b: (T.DY[:, 8 * LY * b:8 * LY * (b + 1)], ps(job)[:, :, 16 * b:16 * b + LY]), job)
+        marked(t, 0, T.DY[:, :], T.DZ[:, :], T.RY[0:16, :], 16 * LY, [("DY", 0), ("DY", 1), "RY"], ["DZ"])
+        vec("tt", 32, ["DZ", "SX"], ["PY"], lambda: (T.PY[:, :], T.DZ[:, LY - 1:16 * LY:LY], T.SX[:, 11:192:12], ALU.max))
+
+    def first(k, b0, b1):
+        bl = range(b0, b1)
+        for b in bl:
+            def thr(g, b=b): return T.S3[:, b, g, k:k + 1] if k else T.TOP[:, 8 * b + g:8 * b + g + 1]
+            def marks(e, q, b=b, thr=thr):
+                if e == "V": return [q.tensor_scalar(T.MK[:, b, g, :], T.SS[:, b, g, :], thr(g), None, ALU.is_le) for g in range(8)]
+                return [q.activation(T.MK[:, b, g, :], T.SS[:, b, g, :], ACT.Sign, bias=thr(g), scale=-0.995) for g in range(8)]
+            def scans(e, q, b=b):
+                return [q.tensor_tensor_scan(T.SO[:, 960 * b + 120 * g:960 * b + 120 * g + 120], T.SS[:, b, g, :], T.MK[:, b, g, :], 1.0, ALU.min, ALU.max) for g in range(8)]
+            rd = [("Sa", b), ("Sb", b)]
+            op("VS", {"V": 8 * vt(60), "S": 8 * st(120)}, marks, rd + [("S3", k - 1, b) if k else ("TOP", b)], [("MK", k, b), ("MK", b)]); ops[-1]["ni"] = 8
+            op("V", 8 * vt(60), scans, rd + [("MK", b)], [("SO", k, b), ("SO", b)]); ops[-1]["ni"] = 8
+        tk = [("TS", b) for b in bl]; ends = T.TS[:, 96 * b0 + 11:96 * b1:12]
+        vec("scan", 48 * (b1 - b0), [("SO", b) for b in bl] + ["P12"], [("TS", k, b0)] + tk,
+            lambda: (T.TS[:, 96 * b0:96 * b1], T.P12[:, 0:96 * (b1 - b0)], T.SO[:, 960 * b0 + 9:960 * b1:10], 0.0, ALU.max, ALU.min))
+        if k == 0: finish(0, b0, b1, ends, tk)
+        vec("cp", 8, tk, [("S3", k, b) for b in bl], lambda: (T.S3[:, b0:b1, :, k + 1], ends))
+
+    def later(k, b0, b1, u):
+        bl = range(b0, b1); L = (0, L1, L2, L3)[k]; DL = T["DL%d" % k]; n = 8 * L; t = min(k, 2)
+        for b in bl:
+            job = newjob("a"); c = slice(128 * b, 128 * b + 128); one = "GA" if u == 1 else "GB"
+            rd = ["ID", "reset", "C2", "C11", "C12"]
+            if k < 3:
+                items = [(lambda p: p[:, :, 0:4], ID, T.S3[:, b, :, :], True, True, 32)]; rd += [("S3", x, b) for x in range(3)]
+            else: items = [(lambda p, x=x: p[:, :, x], ID, T.S3[:, b, :, 0], True, True, 8) for x in range(2)]
+            for i in ((), range(12), range(10), range(10, 12))[k]:
+                a, x = source(u if i < 10 else t, b, i); rd += x
+                if k == 1: items.append((lambda p, i=i: p[:, :, 4 + i], a, T.ID[:, 26:154:16], True, True, 8))
+                else: items.append((lambda p, i=i - 11 * (k - 2): p[:, :, 4 + 2 * i:6 + 2 * i], a, T.C2[:, :], True, True, 16))
+            if k == 1:
+                items.append((lambda p: p[:, :, 16:27], T[one][:, c], T.C11[:, :], True, True, 88)); rd.append((one, b // 2))
+            if k == 3:
+                items += [(lambda p: p[:, :, 6:18], T.GB[:, c], T.C12[:, :], True, True, 96), (lambda p: p[:, :, 18:30], T.GN[:, c], T.C12[:, :], True, True, 96)]
+                rd += [("GN", b // 2), ("GB", b // 2)]
+            mm(items, rd, job)
+            move(n, [], [("DL", k, b)], lambda job=job, b=b: (DL[:, n * b:n * b + n], ps(job)[:, :, 0:L]), job)
+        ok = [("DO", k, b0)] + [("DO", b) for b in bl]; tk = [("DT", b) for b in bl]; c0 = 8 * L1 * b0; o = 8 * L3 * b0
+        marked(t, b0, DL[:, n * b0:n * b1], T.DO[:, o:o + 2 * n], T["R%d" % k][0:16, :], 2 * n, [("DL", k, b) for b in bl] + ["R%d" % k], ok)
+        K = L if k == 1 else L // 2; runs = T.DO[:, o:o + 2 * n] if k == 1 else T.DO[:, o + 1:o + 2 * n:2]
+        vec("scan", 8 * K, ok + ["P%d" % K], [("DT", k, b0)] + tk, lambda: (T.DT[:, c0:c0 + 16 * K], T["P%d" % K][:, 0:16 * K], runs, 0.0, ALU.max, ALU.min))
+        ends = T.DT[:, c0 + K - 1:c0 + 16 * K:K]; t3 = T.T3[:, 8 * b0:8 * b1]
+        if k == 1: finish(1, b0, b1, ends, tk)
+        elif k == 2: vec("cp", 16, tk, [("T3", b0)], lambda: (t3, ends))
+        else:
+            vec("tt", 32, tk + [("T3", b0)], [("T3", b0)], lambda: (t3, t3, ends, ALU.min))
+            finish(2, b0, b1, t3, [("T3", b0)])
 
     nout = [0]
-    def finish(t, b0, b1):
-        bl = range(b0, b1); n = 8 * (b1 - b0); K = 12 + t; end = R0 + 12 * K
-        s = 0 if b0 == 0 else R0; w = end - s
-        K += 2 if b0 == 0 else 0
-        line = 12 * K; so = 1536 * b0
+    def finish(t, b0, b1, ends, tk):
+        bl = range(b0, b1); n = 8 * (b1 - b0)
         def keys(s): return [(s, b) for b in bl]
-        for b in bl:
-            rd = [("Sa", b), ("Sb", b)] + (["Sy", "reset"] if b < 2 else []) + ([("Sg0", b), ("Sn1", b), "late"] if t else []) + ([("Sg1", b), ("Sn2", b)] if t == 2 else [])
-            def marks(e, q, b=b):
-                if e == "V": return [q.tensor_scalar(T.MK[:, b, g, s:end], T.SS[:, b, g, s:end], T.TOP[:, 8 * b + g:8 * b + g + 1], None, ALU.is_le) for g in range(8)]
-                return [q.activation(T.MK[:, b, g, s:end], T.SS[:, b, g, s:end], ACT.Sign, bias=T.TOP[:, 8 * b + g:8 * b + g + 1], scale=-0.995) for g in range(8)]
-            def scans(e, q, b=b):
-                return [q.tensor_tensor_scan(T.SO[:, c - w:c], T.SS[:, b, g, s:end], T.MK[:, b, g, s:end], 1.0, ALU.min, ALU.max)
-                        for g in range(8) for c in [so + line * (8 * (b - b0) + g + 1)]]
-            op("VS", {"V": 8 * vt(w / 2), "S": 8 * st(w)}, marks, rd + [("TOP", b)], [("MK", b)]); ops[-1]["ni"] = 8
-            op("V", 8 * vt(w / 2), scans, rd + [("MK", b)], [("SO", b)]); ops[-1]["ni"] = 8
-        c0 = 128 * b0; ends = T.TS[:, c0 + K - 1:c0 + n * K:K]; p0 = K - 1 if b0 == 0 else 0
-        vec("scan", n * K / 2, keys("SO") + ["P%d" % K], keys("TS"),
-            lambda: (T.TS[:, c0:c0 + n * K], T["P%d" % K][:, p0:p0 + n * K], T.SO[:, so + 11:so + n * line:12], 0.0, ALU.max, ALU.min))
         gain = T.A[:, b0:b1, :, 10 + t]; gk = keys("A")
-        if b0 == 0:
-            vec("tt", 32, keys("SO") + ["SX"], ["PY"], lambda: (T.PY[:, :], T.SO[:, 22:n * line:line], T.SX[:, 11:192:12], ALU.max))
-            if t == 1:
-                vec("tt", 32, keys("TS") + ["PY"], ["GXO"], lambda: (GXO, ends, T.PY[:, :], ALU.min))
-                send(2)
-                vec("cp", n, ["GXO"], gk, lambda: (gain, GXO))
-            else: vec("tt", 32, keys("TS") + ["PY"], gk, lambda: (gain, ends, T.PY[:, :], ALU.min))
-        elif t < 2: vec("cp", n, keys("TS"), gk, lambda: (gain, ends))
-        else: gain = ends; gk = keys("TS")
-        if t < 2:
-            if t == 0 or b0:
-                job = newjob("b"); wc = wcol(b0)
-                turn([(lambda p, i=b - b0: p[:, i, :, :], T.A[:, b, :, :]) for b in bl], ["ID"] + gk, job, ID)
-                move(16 * n, [], [wkey(t + 1, b) for b in bl], lambda: (win(t + 1)[:, wc:wc + 16 * n], ps(job)[:, 0:b1 - b0, :, :]), job, 0.5)
-                if b0 == 0: send(1)
-            c = slice(8 * b0, 8 * b1)
-            vec("ts", n, gk, keys("T1"), lambda: (T.T1[:, c], gain, THR, None, lt))
-            vec("tt", 2 * n, gk + keys("T1"), keys("T2"), lambda: (T.T2[:, c], T.T1[:, c], gain, ALU.mult))
-            vec("tt", 2 * n, keys("T2") + keys("TOP"), keys("TOP"), lambda: (T.TOP[:, c], T.TOP[:, c], T.T2[:, c], ALU.max))
-        if t == 2: output(2, b0, b1, gain, gk)
+        if b0 == 0: vec("tt", 32, tk + ["PY"], gk, lambda: (gain, ends, T.PY[:, :], ALU.min))
+        elif t < 2: vec("cp", n, tk, gk, lambda: (gain, ends))
+        else: gain = ends; gk = tk
+        if t == 2: return output(2, b0, b1, gain, gk)
+        job = newjob("b"); w = wcol(b0)
+        turn([(lambda p, i=b - b0: p[:, i, :, :], T.A[:, b, :, :]) for b in bl], ["ID"] + gk, job, ID)
+        move(16 * n, [], [wkey(t + 1, b) for b in bl], lambda: (win(t + 1)[:, w:w + 16 * n], ps(job)[:, 0:b1 - b0, :, :]), job, 0.5)
+        if b0 == 0: send(t + 1)
+        c = slice(8 * b0, 8 * b1)
+        vec("ts", n, gk, keys("T1"), lambda: (T.T1[:, c], gain, THR, None, lt))
+        vec("tt", 2 * n, gk + keys("T1"), keys("T2"), lambda: (T.T2[:, c], T.T1[:, c], gain, ALU.mult))
+        vec("tt", 2 * n, keys("T2") + keys("TOP"), keys("TOP"), lambda: (T.TOP[:, c], T.TOP[:, c], T.T2[:, c], ALU.max))
+        tops(t + 1, b0)
 
     def affine(n, rd, wr, args, scale, bias, job=None):
         def fn(e, q):
@@ -317,9 +359,9 @@ def plan(T, topo, rank, core):
         n = 8 * (b1 - b0); c = slice(64 * t + 8 * b0, 64 * t + 8 * b1); k = nout[0]; nout[0] += 1
         ln(n, gk, [("LG", k)], lambda: (T.LG[:, c], gain))
         affine(n, [("LG", k)], [("GF", k)], lambda: (T.GF[:, c], T.LG[:, c]), STEP, MAGIC)
-        job = newjob("f")
-        turn([(lambda p: p[0:n, 0:4, :], T.GF[:, c])], ["IDF", ("GF", k)], job, T.IDF[:, :], 4)
-        affine(128, [], [("FO", k)], lambda: (T.FO[0:n, 128 * k:128 * k + 128], ps(job)[0:n, 0:4, :]), 1.0, -MAGIC, job)
+        job = newjob("d")
+        turn([(lambda p: p[0:n, 0:128], T.GF[:, c])], ["IDF", ("GF", k)], job, T.IDF[:, :], 4)
+        affine(128, [], [("FO", k)], lambda: (T.FO[0:n, 128 * k:128 * k + 128], ps(job)[0:n, 0:128]), 1.0, -MAGIC, job)
         for b in range(b0, b1):
             dma("YS"[b % 2] if t == 2 else "Y", T.yp[10 + t:128:16, 128 * b:128 * b + 128], T.FO[8 * (b - b0):8 * (b - b0) + 8, 128 * k:128 * k + 128],
                 [("FO", k), "yp"], [], kind="fin")
@@ -327,12 +369,12 @@ def plan(T, topo, rank, core):
     rnd[0] = 1
     loads(0, 0, V); loads(0, V, X)
     for P in range(4):
-        job = newjob("f"); E = T.GL0; e = V * P
-        mm([(lambda p: p[:, 0:4, :], shift(0, 0), E[:, e:e + 128], True, False, 128), (lambda p: p[:, 0:4, :], shift(1, 10), E[:, e + 128:e + 256], False, True, 128)]
-           + [(lambda p: p[:, 4, :], shift(2, 4 * x - 6), E[:, e + 128 + x:e + 256:4], x == 0, x == 3, 32) for x in range(4)],
+        job = newjob("d"); E = T.GL0; e = V * P
+        mm([(lambda p: p[:, 0:128], shift(0, 0), E[:, e:e + 128], True, False, 128), (lambda p: p[:, 0:128], shift(1, 10), E[:, e + 128:e + 256], False, True, 128)]
+           + [(lambda p: p[:, 128:160], shift(2, 4 * x - 6), E[:, e + 128 + x:e + 256:4], x == 0, x == 3, 32) for x in range(4)],
            [("GL", 0, P), ("PM", 0), ("PM", 1), ("PM", 2)], job)
         c = slice(160 * P, 160 * P + 160)
-        ln(160, [], [("LN", P)], lambda job=job, c=c: (T.LN[:, c], ps(job)[:, 0:5, :]), job)
+        ln(160, [], [("LN", P)], lambda job=job, c=c: (T.LN[:, c], ps(job)[:, 0:160]), job)
         vec("ts", 160, [("LN", P)], [("O", P)], lambda c=c: (T.O[:, c], T.LN[:, c], STEP, float(M), ALU.mult, ALU.min))
         places(0, P); members(0, P)
     for b in range(8):
@@ -341,56 +383,32 @@ def plan(T, topo, rank, core):
             for i in range(i0, i1):
                 a, k = source(0, b, i); rd += k; items.append((lambda p, x=i - i0: p[:, :, x, :], a))
             turn(items, rd, job, ID)
-            move(96 * (i1 - i0), [], [(key, b), ("Sg0", b)], lambda job=job, b=b, i0=i0, i1=i1: (T.SS[:, b, :, R0 + 12 * i0:R0 + 12 * i1], ps(job)[:, :, 0:i1 - i0, 0:12]), job, 0.5)
-    stores(0)
-    for r in RANGES[0]: finish(0, *r)
+            move(80 * (i1 - i0), [], [(key, b)], lambda job=job, b=b, i0=i0, i1=i1: (T.SS[:, b, :, 10 * i0:10 * i1], ps(job)[:, :, 0:i1 - i0, 0:10]), job, 0.5)
+    tops(0, 0); stores(0)
+    for r in PAIRS: first(0, *r)
     output(0, 0, 8, T.A[:, :, :, 10], [("A", b) for b in range(8)])
 
     rnd[0] = 2
-    def first_gains(t, b):
-        items = []; rd = []
-        for i in range(12):
-            a, k = source(t if i < 10 else 1, b, i); items.append(a); rd += k
-        gains(0, b, items, rd)
+    first(1, 0, 2)
     for (v0, v1) in LOADS[1]:
         loads(1, v0, v1); gained(1, v0, v1)
     for P in range(4): places(1, P)
-    for P in range(EARLY // 2):
-        members(1, P); named("GA", 1, 1, V * P, V * P + V); whole("GA", 2 * P, 2 * P + 2, RN, 11, "Sn1")
-        for b in (2 * P, 2 * P + 1): first_gains(1, b)
-    stores(1)
-    for r in RANGES[1]:
-        if r[0] < EARLY: finish(1, *r)
-    for h in range(2):
-        job = newjob("b")
-        turn([(lambda p, i=i: p[:, i, :, :], T.W1[:, 1024 * h + 128 * i:1024 * h + 128 * i + 128]) for i in range(8)], ["ID"] + objkeys(1), job, ID)
-        move(1024, [], [("AT", h)], lambda job=job, h=h: (T.AT[:, 8 * h:8 * h + 8, :, :], ps(job)[:, :, :, :]), job, 0.5)
-    for h in range(2):
-        vec("cp", 64, [("arr", 2), "GXO"], [("AT", h)], lambda h=h: (T.AT[:, 8 * h:8 * h + 8, :, 11], T.GX[:, 64 * h:64 * h + 64]))
-        job = newjob("b")
-        turn([(lambda p, i=i: p[:, i, :, :], T.AT[:, 8 * h + i, :, :]) for i in range(8)], ["ID", ("AT", h)], job, ID)
-        move(1024, [], [("obj", h)], lambda job=job, h=h: (T.W2[:, 1024 * h:1024 * h + 1024], ps(job)[:, :, :, :]), job, 0.5)
-    for P in list(range(EARLY // 2, 4)) + list(range(EARLY // 2)):
+    members(1, 0); named("GA", 1, 1, 0, V)
+    stores(1); later(1, 0, 2, 1)
+    for r in PAIRS[1:]: first(1, *r)
+    for P in (1, 2, 3, 0):
         members(2, P); named("GB", 1, 2, V * P, V * P + V)
-        if P >= EARLY // 2:
-            whole("GB", 2 * P, 2 * P + 2, RN, 11, "Sn1")
-            for b in (2 * P, 2 * P + 1): first_gains(2, b)
-    for r in RANGES[1]:
-        if r[0] >= EARLY: finish(1, *r)
+    for r in PAIRS[1:]: later(1, r[0], r[1], 2)
+    for r in PAIRS: first(2, *r)
     output(1, 0, 8, T.A[:, :, :, 11], [("A", b) for b in range(8)])
 
     rnd[0] = 3
+    for r in PAIRS: later(2, r[0], r[1], 2)
     for (v0, v1) in LOADS[2]:
         loads(2, v0, v1); gained(2, v0, v1); named("GN", 2, 2, v0, v1)
-    for P in range(4):
-        places(2, P); whole("GN", 2 * P, 2 * P + 2, R2, 12, "Sn2")
-        for b in (2 * P, 2 * P + 1):
-            items = []; rd = [("GB", P)]
-            for i in range(12):
-                a, k = source(2, b, i); items.append(a); rd += k
-            gains(1, b, items + [T.GB[:, 128 * b:128 * b + 128]], rd)
+    for P in range(4): places(2, P)
     stores(2)
-    for r in RANGES[2]: finish(2, *r)
+    for r in PAIRS: later(3, r[0], r[1], 2)
     return ops
 
 
@@ -399,7 +417,7 @@ def order(ops):
         v = [SIGNS.index(ORDER[k]) * 62 + SIGNS.index(ORDER[k + 1]) for k in range(0, len(ORDER), 2)]
     else:
         v = [2 * i for i in range(len(ops))]
-    free = {"b": [[k, None] for k in range(NB16)], "f": [[k, None] for k in range(NF32)]}
+    free = {s: [[k, None] for k in range(BANKS[s])] for s in BANKS}
     seq = []
     for x in v:
         i = x // 2; o = ops[i]; job = o["job"]

import math
from concourse.bass import DstId, RemoteDMATransfer
from concourse.mybir import AluOpType as ALU, ActivationFunctionType as ACT

N, V, X, M, NONE = 8, 256, 1024, 2048, 2816
TMP = M + 16
WIN = TMP + (X - V) + 1
EWIN = M + 1
STEP, ZERO = 64.0, 2880.0
UP = math.exp(ZERO / STEP)
THR = math.exp(-5.0)
MAGIC = 12582912.0
KB = 2.0 ** 71
L1, L2, L3, LY = 27, 24, 30, 13
BANKS = {"b": 3, "a": 2, "d": 3}


def _sb(n, d): return ("sbuf", [128] + (n if isinstance(n, list) else [n]), d)


SCRATCH = {}
for _d, _l in (
    ("int32", dict(PI=X, LI=[14, 16], LM=[14, 16], CI=2)),
    ("uint16", dict(LU=224, O=640, ON1=64, ON2=64)),
    ("float32", dict(OUT=X, IDF=128, CF=8, OWF=4, LN=640, LO1=64, LO2=64, LG=192, GF=192, FO=1024)),
    ("bfloat16", dict(W0=2848, W1=2848, W2=2848, GE0=10240, GE1=2560, GE2=10240, GC0=2560, GC1=2560, GC2=2560,
                      GL0=X, GL1=X, GL2=X, GA=V, GB=X, GN=X, SS=[8, 8, 120], MK=[8, 8, 120], SO=7680, TS=768, S3=[8, 8, 4], A=[8, 8, 16],
                      DL1=64 * L1, DL2=64 * L2, DL3=64 * L3, DO=64 * L3, DT=64 * L1, T3=64, DY=16 * LY, DZ=16 * LY, TT=1536, TOP=64,
                      R1=16 * L1, R2=16 * L2, R3=16 * L3, RY=16 * LY, NK=128, I3=[8, 16], C12=96, C11=88, C2=16, Z=16 * L3,
                      ID=160, PM0=160, PM1=160, PM2=160, PM3=160, PM4=160, OWN=4, P10=320, P12=192, P15=240, P27=432,
                      AX=192, SX=192, PY=16, Y0=640, Y1=640, Y2=640, T1=64, T2=64)),
):
    for _k in _l: SCRATCH[_k] = _sb(_l[_k], _d)
for _k in range(BANKS["b"]): SCRATCH["Pb%d" % _k] = ("psum", [128, 8, 8, 16], "bfloat16")
for _k in range(BANKS["a"]): SCRATCH["Pa%d" % _k] = ("psum", [128, 8, 64], "float32")
for _k in range(BANKS["d"]): SCRATCH["Pd%d" % _k] = ("psum", [128, 512], "float32")

NDMA = 12
SEMAPHORES = ["cv", "cs", "cp", "cg", "fin"] + [s + str(t) for s in ("arr", "snt") for t in range(3)] + ["dm%d" % k for k in range(NDMA)]

CYC, PCYC, GATH, LAT = 0.95, 0.5, 1.56, 150.0
DMA_NS, NET_NS = 2300.0, 7000.0
PAIRS = [(0, 2), (2, 4), (4, 6), (6, 8)]
LOADS = [None, [(0, 256), (256, 1024)], [(0, 256), (256, 512), (512, 768), (768, 1024)]]
SIGNS = "0123456789abcdefghijklmnopqrstuvwxyzABCDEFGHIJKLMNOPQRSTUVWXYZ"
ORDER = "0k0m0e0p0016120g0q1e140c1w0s1z0U181k06040a02080i1A1C0u1o1a0y1F2i260Q0W1Q1u0w101S291O0C2l1m1g2a0E0O1U222c202e1i0G0I2g1c0Y0A1s240S2m4u4x1W1q1Y0K2o2q2s2v2y2T2B2w302M2E1K1I1M1G2P334y2C2H4A2Q2I3e4G3h2X4C2K4J2V373w2Y3y4E3s3u343A3E3C3G393b3d4K4S4W4M3I4U3K4Y4O3Q3M3S4Q503U3O3i523W543Y5m5a560M5q5o4a4c425s5c4640585u445e485w3p3n3l5O5g5i5S5y5A3r4e4i4m5Q5U4h5k5M4k4q5W4o5Y4s6g607b776k6i6m64626o665C6q786s6u6G8I7c7K8E7e7H7j7k7z7n7o6e7W6w7Y7g7O7J7M8c808V6J8R8K7Q8G8e88828a8g6y8M6K7S68846a7U8O8i866c8k6A5E8m968o6C7r7D7F8q8s7s6M7vbt925G5I6E8S988W8u948Y8w9abo9cbu90bq7w8y8AbE5K7BbR6PbNbAbGbC9f9tbcbI9A9g9i9l9n9r9o9v9K9O9M9Qbwae9Saiah9z9D9w9U8CaIakbKby9Wbg9YamaoaMaLaPcCaQcGa0a4bOa6bS9Ha8aqaScFascIaUcWaaaucSaybUa29FaWaAacaYcKbWawaCb2cYb0bicVdzaEb4aGcMdIdcd8dAe7bZdDdTd0b6b8dKbec0c2dEe5d2dedGbkbabmd4dUf2dbdNdOc5c6eYdgf4dXdYf0dpdRc86W6Q6Ye8cOe0cqf6cmctcofudqfwdi9IcQe3fqfScueadtd6dkduftf8fWdmcwfyfVdxfZeufaecfAeecyfCexeyg0eieBeleCegcAfcfEfHffg2emg4eEeoeqeGfJfhfiflfKg6esg9eIeKeNgagcgffpgjeOfMfReQeSfmcicecc6S6U72cg70ca74ggckfOeUeX"


def plan(T, topo, rank, core):
    ops, lastw, readers = [], {}, {}
    rnd, njob = [0], [0]

    def op(eng, dur, fn, rd=(), wr=(), job=None, kind="c", lat=0.0):
        deps = {}
        rd = list(rd); wr = list(wr)
        if job is not None:
            wr.append(("job", job[0])); rd.append(("job", job[0]))
        for k in rd:
            if k in lastw: deps[lastw[k]] = True
        for k in wr:
            if k in lastw: deps[lastw[k]] = True
            for r in readers.get(k, []): deps[r] = True
        i = len(ops)
        for k in rd: readers.setdefault(k, []).append(i)
        for k in wr: lastw[k] = i; readers[k] = []
        k = wr[0] if wr else "out"
        cls = "%s%d" % (k if isinstance(k, str) else k[0], rnd[0])
        ops.append({"eng": eng, "dur": dur, "fn": fn, "deps": deps, "job": job, "kind": kind, "lat": lat, "g": 0,
                    "cls": cls, "fine": cls if isinstance(k, str) else cls + "".join("." + str(x) for x in k[1:])})
        if job is not None: job[1].append(i)

    def newjob(kind):
        njob[0] += 1
        return [njob[0], [], None, kind]

    def ps(job): return T["P%s%d" % (job[3], job[2])]
    def gt(n): return 200 + 2 * n * CYC
    def vt(n): return max(64, n) * CYC + 10
    def st(n): return max(64, n) * CYC + 60

    calls = {"ts": lambda q, a: q.tensor_scalar(*a), "tt": lambda q, a: q.tensor_tensor(*a), "cp": lambda q, a: q.tensor_copy(*a),
             "ms": lambda q, a: q.memset(*a), "scan": lambda q, a: q.tensor_tensor_scan(*a)}

    def vec(name, n, rd, wr, args, job=None):
        op("V", vt(n), lambda e, q: [calls[name](q, args())], rd, wr, job)

    def act(n, rd, wr, args, job=None, extra=0.0):
        def fn(e, q):
            a = args()
            return [q.activation(a[0], a[1], a[2], bias=a[3], scale=a[4])]
        op("S", st(n) + extra, fn, rd, wr, job)

    def move(n, rd, wr, args, job=None, f=1.0):
        def fn(e, q):
            o, i = args()
            return [q.tensor_copy(o, i) if e == "V" else q.activation(o, i, ACT.Copy)]
        op("VS", {"V": vt(n * f), "S": st(n)}, fn, rd, wr, job)

    def gather(out, w, off, n, rd, wr):
        def fn(e, q):
            i = w.indirect(off)
            return [q.tensor_copy(out, i) if e == "V" else q.activation(out, i, ACT.Copy)]
        op("VS", {"V": n * GATH * CYC + 50, "S": n * GATH * CYC + 65}, fn, rd, wr)
        ops[-1]["g"] = 1

    def mm(items, rd, job):
        dur = sum(max(64, x[5]) for x in items) * PCYC + 60
        op("P", dur, lambda e, q: [q.matmul(c(ps(job)), l, r, a, b) for (c, l, r, a, b, _) in items], rd, [], job)

    def turn(items, rd, job, ident, f=1):
        op("P", 128 * f * len(items) * PCYC + 60, lambda e, q: [q.transpose(c(ps(job)), a, ident) for (c, a) in items], rd, [], job)

    def dma(eng, out, in_, rd, wr, extra=0.0, kind="dma"):
        op(eng, 60.0, lambda e, q: [q.dma_start(out, in_)], rd, wr, kind=kind, lat=DMA_NS + extra)

    own0 = rank * V
    ID = T.ID[:, 16:144]
    NN = T.OWN[:, 2:3]
    def wcol(b): return own0 + 128 * b if b < 2 else TMP + 128 * (b - 2)
    def win(t): return [T.W0, T.W1, T.W2][t]
    def wkey(t, b): return ("win", t, b)
    def objkeys(t): return [wkey(t, 0), wkey(t, 1), ("arr", t), ("none", t)]
    def allkeys(t): return objkeys(t) + [("pad", t)] + [wkey(t, b) for b in range(2, 8)]
    def shift(k, d): return T["PM%d" % k][:, 16 - d:144 - d]

    def send(t):
        src = win(t)[:, own0:own0 + V]
        def fn(e, q):
            trs = []
            at = 0
            for d in range(1, N):
                dst = T.cores[(rank + d) % N]
                eng = topo.engines(core, dst)
                k = len(eng) - (N - 2) if d == 1 else 1
                mask = sum(1 << x for x in eng[at:at + k]); at += k
                rid, pid = topo.addr(dst)[:2]
                trs.append(RemoteDMATransfer(dst_ids=[DstId(rid=rid, pnc=pid)], dma_engine_mask=mask, remote_sem=T.sem["arr%d" % t], src=src, dst=src))
            q.remote_dma_fused(trs, local_sem=T.sem["snt%d" % t])
            return []
        op("G", 300.0, fn, [wkey(t, 0), wkey(t, 1)], [("arr", t)], kind=("net", t), lat=NET_NS)

    dma("Y", T.PI[:, 0:V], T.pts[:, 0:V], [], ["PIo"])
    dma("Y", T.PI[:, V:X], T.pts[:, V:X], [], ["PIt"], 500)
    dma("Y", T.LI[:, 0:4, :], T.ld[:, :], [], ["LI0"])
    dma("Y", T.LI[:, 4:12, :], T.cp[:, :], [], ["LI1"])
    dma("Y", T.LI[:, 12, :], T.xs[:, :], [], ["LI2"])
    dma("Y", T.LI[:, 13, :], T.ys[:, :], [], ["LI3"])

    ge, lt = ALU.is_ge, ALU.is_lt
    CI, CF = T.CI, T.CF
    vec("ms", 240, [], ["Z"], lambda: (T.Z[:, :], 0.0))
    op("G", gt(2), lambda e, q: [q.iota(T.OWF[:, 0:2], [[128, 2]], own0, 1, allow_small_or_imprecise_dtypes=True)], [], ["OWF0"])
    op("G", gt(1), lambda e, q: [q.iota(CI[:, 0:1], [[0, 1]], 0, 1)], [], ["CI0"])
    op("G", gt(160), lambda e, q: [q.affine_select(T.ID[:, :], T.Z[:, 0:160], [[1, 160]], ALU.not_equal, 1.0, -16, -1)], ["Z"], ["ID"])
    vec("ms", 1, [], ["OWF1"], lambda: (T.OWF[:, 2:3], float(NONE)))
    vec("ms", 1, [], ["EB"], lambda: (T.OWF[:, 3:4], -ZERO / STEP))
    EB = T.OWF[:, 3:4]
    act(3, ["OWF0", "OWF1", "EB"], ["OWN"], lambda: (T.OWN[:, 0:3], T.OWF[:, 0:3], ACT.Exp, EB, 1.0 / STEP), extra=1300.0)
    vec("ts", 1, ["CI0"], ["CI1"], lambda: (CI[:, 1:2], CI[:, 0:1], 15, None, ALU.bitwise_and))
    vec("cp", 1, ["CI1"], ["CF5"], lambda: (CF[:, 5:6], CI[:, 1:2]))
    row = CF[:, 5:6]
    vec("ts", 1, ["CF5"], ["CF0"], lambda: (CF[:, 0:1], row, 10.0, None, lt))
    vec("ts", 1, ["CF5"], ["CF1"], lambda: (CF[:, 1:2], row, 6.0, None, lt))
    vec("ts", 1, ["CF5", "CF0"], ["CF2"], lambda: (CF[:, 2:3], row, 6.0, CF[:, 0:1], ge, ALU.mult))
    vec("ts", 1, ["CF5"], ["CF3"], lambda: (CF[:, 3:4], row, 10.0, None, ALU.is_equal))
    vec("ts", 1, ["CF5"], ["CF4"], lambda: (CF[:, 4:5], row, 11.0, None, ALU.is_equal))
    for k in range(5):
        vec("ts", 80, ["ID", "CF%d" % k], [("PM", k)], lambda k=k: (T["PM%d" % k][:, :], T.ID[:, :], CF[:, k:k + 1], None, ALU.mult))
    vec("cp", 128, ["ID"], ["IDF"], lambda: (T.IDF[:, :], ID))
    for t in range(3):
        vec("ts", 2, ["Z", "OWN"], [("none", t)], lambda t=t: (win(t)[:, M:WIN:WIN - 1 - M], T.Z[:, 0:2], NN, None, ALU.add))
        vec("ms", 8, [], [("pad", t)], lambda t=t: (win(t)[:, M + 1:TMP], 0.0))
    vec("ms", 160, [], ["P10"], lambda: (T.P10[:, :], 1.0))
    vec("ms", 32, ["P10"], ["P10"], lambda: (T.P10[:, 0:320:10], 0.0))
    for k in (12, 15, 27):
        p = T["P%d" % k]; key = "P%d" % k
        vec("ms", 8 * k, [], [key], lambda p=p: (p[:, :], 0.0))
        vec("ts", 16, ["Z", "OWN", key], [key], lambda p=p, k=k: (p[:, 0:16 * k:k], T.Z[:, 0:16], NN, None, ALU.add))
    vec("ms", 32, [], ["reset"], lambda: (T.S3[:, :, :, 0], -1.0))
    vec("ts", 32, ["Z", "OWN"], [("S3", 2, b) for b in range(8)], lambda: (T.S3[:, :, :, 3], T.Z[:, 0:64], NN, None, ALU.add))
    vec("ts", 64, ["ID"], ["NK"], lambda: (T.NK[:, :], ID, -KB, None, ALU.mult))
    vec("cp", 64, ["ID"], ["I3"], lambda: (T.I3[:, :, :], ID))
    for (k, r0, r1) in (("C12", 0, 12), ("C11", 0, 11), ("C2", 10, 12)):
        vec("cp", 48, ["I3"], [k], lambda k=k, r0=r0, r1=r1: (T[k][:, :], T.I3[:, :, r0:r1]))

    for (c0, c1, pk) in ((0, V, "PIo"), (V, X, "PIt")):
        n = c1 - c0; w = wcol(c0 // 128)
        vec("cp", n, [pk], [("OUT", c0)], lambda c0=c0, c1=c1: (T.OUT[:, c0:c1], T.PI[:, c0:c1]))
        act(n, [("OUT", c0), "EB", "OWN"], [wkey(0, b) for b in range(c0 // 128, c1 // 128)],
            lambda c0=c0, c1=c1, w=w, n=n: (T.W0[:, w:w + n], T.OUT[:, c0:c1], ACT.Exp, EB, 1.0 / STEP))
        if c0 == 0: send(0)
    for (k, n) in (("RY", LY), ("R1", L1), ("R2", L2), ("R3", L3)):
        op("G", gt(16 * n), lambda e, q, k=k, n=n: [q.affine_select(T[k][0:16, :], T.Z[0:16, 0:16 * n], [[8, 2], [1, 8], [0, n]], ALU.not_equal, KB * 1.0078125, 0, -1)],
           ["Z", ("arr", 0)], [k])
    dma("Y", T.yp[:, :], T.OUT[:, :], [("OUT", 0), ("OUT", V), ("arr", 0)], ["yp"], 1500)

    lk = ["LI0", "LI1", "LI2", "LI3"]
    vec("ts", 224, lk, ["LM"], lambda: (T.LM[:, :, :], T.LI[:, :, :], float(M), 16.0, ge, ALU.mult))
    vec("tt", 448, lk + ["LM"], ["LM"], lambda: (T.LM[:, :, :], T.LM[:, :, :], T.LI[:, :, :], ALU.add))
    vec("cp", 64, ["LM"], [("LU", 0)], lambda: (T.LU[:, 0:64], T.LM[:, 0:4, :]))
    vec("cp", 32, ["LM"], [("LU", 1)], lambda: (T.LU[:, 96:128], T.LM[:, 12:14, :]))
    def gb(P): return 512 + 512 * P if P else 0
    for P in range(4):
        o = 64 + gb(P) // 16
        vec("cp", 32, ["LM"], [("LU", 2 + P)], lambda P=P, o=o: (T.LU[:, o:o + 32], T.LM[:, 4 + P:12:4, :]))
    luk = [("LU", k) for k in range(6)]

    for h in range(2):
        job = newjob("b"); bl = range(4 * h, 4 * h + 4); ak = [("A", b) for b in bl]; c = slice(320 * h, 320 * h + 320)
        turn([(lambda p, i=i: p[:, i, :, :], T.W0[:, wcol(b):wcol(b) + 128]) for i, b in enumerate(bl)], ["ID"] + [wkey(0, b) for b in bl], job, ID)
        move(512, [], ak, lambda job=job, h=h: (T.A[:, 4 * h:4 * h + 4, :, :], ps(job)[:, 0:4, :, :]), job, 0.5)
        a = T.A[:, 4 * h:4 * h + 4, :, 0:10]
        vec("ts", 160, ak, [("Y0", h)], lambda a=a, c=c: (T.Y0[:, c], a, THR, None, lt))
        vec("tt", 640, ak + [("Y0", h)], [("Y1", h)], lambda a=a, c=c: (T.Y1[:, c], T.Y0[:, c], a, ALU.mult))
        vec("scan", 160, [("Y1", h), "P10"], [("Y2", h)], lambda c=c: (T.Y2[:, c], T.P10[:, 0:320], T.Y1[:, c], 0.0, ALU.mult, ALU.max))
        vec("cp", 32, [("Y2", h)], [("TOP", b) for b in bl], lambda h=h: (T.TOP[:, 32 * h:32 * h + 32], T.Y2[:, 320 * h + 9:320 * h + 320:10]))

    def source(t, b, i):
        P, odd = divmod(b, 2); base = 2560 * P
        if i >= 10:
            c = gb(P) + 256 * (i - 10) + 128 * odd
            return T["GC%d" % t][:, c:c + 128], [("GC", t, P)]
        GE = T["GE%d" % t]
        if odd and i >= 6: return GE[:, base + 2048 + i - 6:base + 2560:4], [("GE", t, P, 2)]
        return GE[:, base + 10 * odd + i:base + 2048:16], [("GE", t, P, 0), ("GE", t, P, 1)]

    def members(t, P):
        for x, (o, n) in enumerate(((0, 64), (64, 64), (128, 32))):
            o += 160 * P
            gather(T["GE%d" % t][:, 16 * o:16 * (o + n)], win(t)[:, 0:EWIN], T.O[:, o:o + n], 16 * n, objkeys(t) + [("O", P)], [("GE", t, P, x)])

    def places(t, P):
        n = 512 if P else 1024; c = gb(P)
        gather(T["GC%d" % t][:, c:c + n], win(t)[:, 0:WIN], T.LU[:, 64 + c // 16:64 + (c + n) // 16], n, allkeys(t) + luk, [("GC", t, P)])

    def loads(t, v0, v1):
        gather(T["GL%d" % t][:, v0:v1], win(t)[:, 0:WIN], T.LU[:, v0 // 16:v1 // 16], v1 - v0, allkeys(t) + luk,
               [("GL", t, P) for P in range(v0 // V, v1 // V)])

    first_ln = [1500.0]
    def ln(n, rd, wr, args, job=None):
        act(n, rd, wr, lambda: args() + (ACT.Ln, 0.0, UP), job, first_ln[0]); first_ln[0] = 0.0

    def gained(t, v0, v1):
        n = (v1 - v0) // 16; o = v0 // 16; job = newjob("d"); pk = range(v0 // V, v1 // V)
        GL = T["GL%d" % t]; LO = T["LO%d" % t]
        mm([(lambda p: p[:, 0:n], shift(2 + t, r - 9 - t), GL[:, v0 + r:v1:16], r == 0, r == 15, n) for r in range(16)],
           [("GL", t, P) for P in pk] + [("PM", 2 + t)], job)
        ln(n, [], [("LO", t, v0)], lambda: (LO[:, o:o + n], ps(job)[:, 0:n]), job)
        vec("ts", n, [("LO", t, v0)], [("ON", t, P) for P in pk], lambda: (T["ON%d" % t][:, o:o + n], LO[:, o:o + n], STEP, float(M), ALU.mult, ALU.min))

    def named(buf, u, t, v0, v1):
        pk = range(v0 // V, v1 // V)
        gather(T[buf][:, v0:v1], win(t)[:, 0:EWIN], T["ON%d" % u][:, v0 // 16:v1 // 16], v1 - v0,
               objkeys(t) + [("ON", u, P) for P in pk], [(buf, P) for P in pk])

    def tt(t, b0): return T.TT[0:16, 512 * t + 64 * b0:512 * t + 64 * b0 + 128]

    def tops(t, b0):
        job = newjob("b")
        turn([(lambda p: p[0:16, 0, :, :], T.TOP[:, 8 * b0:8 * b0 + 16])], ["ID", ("TOP", b0), ("TOP", b0 + 1)], job, ID)
        move(128, [], [("TT", t, b0)], lambda: (tt(t, b0), ps(job)[0:16, 0, :, :]), job, 0.5)

    def marked(t, b0, line, out, r, n, rd, wr):
        job = newjob("d")
        mm([(lambda p: p[:, 0:n], tt(t, b0), r, True, False, n), (lambda p: p[:, 0:n], T.NK[:, :], line, False, True, n)], rd + ["NK", ("TT", t, b0)], job)
        vec("scan", n, rd, wr, lambda: (out, line, ps(job)[:, 0:n], 1.0, ALU.min, ALU.max), job)

    def stores(t):
        job = newjob("b"); GC = T["GC%d" % t]
        turn([(lambda p, i=i: p[:, i, :, :], GC[:, 512 + 128 * i:640 + 128 * i]) for i in range(2)], ["ID", ("GC", t, 0)], job, ID)
        for b in range(2):
            vec("ts", 48, ["OWN"], [("AX", b)], lambda b=b, job=job: (T.AX[:, 96 * b:96 * b + 96], ps(job)[:, b, :, 0:12], T.OWN[:, b:b + 1], None, ALU.not_equal), job)
        vec("scan", 96, [("AX", 0), ("AX", 1), "P12"], ["SX"], lambda: (T.SX[:, :], T.P12[:, :], T.AX[:, :], 0.0, ALU.max, ALU.min))
        job = newjob("a"); items = []
        for b in range(2):
            items += [(lambda p, b=b: p[:, :, 16 * b], ID, T.S3[:, b, :, 0], True, True, 8),
                      (lambda p, b=b: p[:, :, 16 * b + 1:16 * b + LY], GC[:, 768 + 128 * b:896 + 128 * b], T.C12[:, :], True, True, 96)]
        mm(items, ["ID", "C12", "reset", ("GC", t, 0)], job)
        for b in range(2):
            move(8 * LY, [], [("DY", b)], lambda b=b: (T.DY[:, 8 * LY * b:8 * LY * (b + 1)], ps(job)[:, :, 16 * b:16 * b + LY]), job)
        marked(t, 0, T.DY[:, :], T.DZ[:, :], T.RY[0:16, :], 16 * LY, [("DY", 0), ("DY", 1), "RY"], ["DZ"])
        vec("tt", 32, ["DZ", "SX"], ["PY"], lambda: (T.PY[:, :], T.DZ[:, LY - 1:16 * LY:LY], T.SX[:, 11:192:12], ALU.max))

    def first(k, b0, b1):
        bl = range(b0, b1)
        for b in bl:
            def thr(g, b=b): return T.S3[:, b, g, k:k + 1] if k else T.TOP[:, 8 * b + g:8 * b + g + 1]
            def marks(e, q, b=b, thr=thr):
                if e == "V": return [q.tensor_scalar(T.MK[:, b, g, :], T.SS[:, b, g, :], thr(g), None, ALU.is_le) for g in range(8)]
                return [q.activation(T.MK[:, b, g, :], T.SS[:, b, g, :], ACT.Sign, bias=thr(g), scale=-0.995) for g in range(8)]
            def scans(e, q, b=b):
                return [q.tensor_tensor_scan(T.SO[:, 960 * b + 120 * g:960 * b + 120 * g + 120], T.SS[:, b, g, :], T.MK[:, b, g, :], 1.0, ALU.min, ALU.max) for g in range(8)]
            rd = [("Sa", b), ("Sb", b)]
            op("VS", {"V": 8 * vt(60), "S": 8 * st(120)}, marks, rd + [("S3", k - 1, b) if k else ("TOP", b)], [("MK", k, b), ("MK", b)]); ops[-1]["ni"] = 8
            op("V", 8 * vt(60), scans, rd + [("MK", b)], [("SO", k, b), ("SO", b)]); ops[-1]["ni"] = 8
        tk = [("TS", b) for b in bl]; ends = T.TS[:, 96 * b0 + 11:96 * b1:12]
        vec("scan", 48 * (b1 - b0), [("SO", b) for b in bl] + ["P12"], [("TS", k, b0)] + tk,
            lambda: (T.TS[:, 96 * b0:96 * b1], T.P12[:, 0:96 * (b1 - b0)], T.SO[:, 960 * b0 + 9:960 * b1:10], 0.0, ALU.max, ALU.min))
        if k == 0: finish(0, b0, b1, ends, tk)
        vec("cp", 8, tk, [("S3", k, b) for b in bl], lambda: (T.S3[:, b0:b1, :, k + 1], ends))

    def later(k, b0, b1, u):
        bl = range(b0, b1); L = (0, L1, L2, L3)[k]; DL = T["DL%d" % k]; n = 8 * L; t = min(k, 2)
        for b in bl:
            job = newjob("a"); c = slice(128 * b, 128 * b + 128); one = "GA" if u == 1 else "GB"
            rd = ["ID", "reset", "C2", "C11", "C12"]
            if k < 3:
                items = [(lambda p: p[:, :, 0:4], ID, T.S3[:, b, :, :], True, True, 32)]; rd += [("S3", x, b) for x in range(3)]
            else: items = [(lambda p, x=x: p[:, :, x], ID, T.S3[:, b, :, 0], True, True, 8) for x in range(2)]
            for i in ((), range(12), range(10), range(10, 12))[k]:
                a, x = source(u if i < 10 else t, b, i); rd += x
                if k == 1: items.append((lambda p, i=i: p[:, :, 4 + i], a, T.ID[:, 26:154:16], True, True, 8))
                else: items.append((lambda p, i=i - 11 * (k - 2): p[:, :, 4 + 2 * i:6 + 2 * i], a, T.C2[:, :], True, True, 16))
            if k == 1:
                items.append((lambda p: p[:, :, 16:27], T[one][:, c], T.C11[:, :], True, True, 88)); rd.append((one, b // 2))
            if k == 3:
                items += [(lambda p: p[:, :, 6:18], T.GB[:, c], T.C12[:, :], True, True, 96), (lambda p: p[:, :, 18:30], T.GN[:, c], T.C12[:, :], True, True, 96)]
                rd += [("GN", b // 2), ("GB", b // 2)]
            mm(items, rd, job)
            move(n, [], [("DL", k, b)], lambda job=job, b=b: (DL[:, n * b:n * b + n], ps(job)[:, :, 0:L]), job)
        ok = [("DO", k, b0)] + [("DO", b) for b in bl]; tk = [("DT", b) for b in bl]; c0 = 8 * L1 * b0; o = 8 * L3 * b0
        marked(t, b0, DL[:, n * b0:n * b1], T.DO[:, o:o + 2 * n], T["R%d" % k][0:16, :], 2 * n, [("DL", k, b) for b in bl] + ["R%d" % k], ok)
        K = L if k == 1 else L // 2; runs = T.DO[:, o:o + 2 * n] if k == 1 else T.DO[:, o + 1:o + 2 * n:2]
        vec("scan", 8 * K, ok + ["P%d" % K], [("DT", k, b0)] + tk, lambda: (T.DT[:, c0:c0 + 16 * K], T["P%d" % K][:, 0:16 * K], runs, 0.0, ALU.max, ALU.min))
        ends = T.DT[:, c0 + K - 1:c0 + 16 * K:K]; t3 = T.T3[:, 8 * b0:8 * b1]
        if k == 1: finish(1, b0, b1, ends, tk)
        elif k == 2: vec("cp", 16, tk, [("T3", b0)], lambda: (t3, ends))
        else:
            vec("tt", 32, tk + [("T3", b0)], [("T3", b0)], lambda: (t3, t3, ends, ALU.min))
            finish(2, b0, b1, t3, [("T3", b0)])

    nout = [0]
    def finish(t, b0, b1, ends, tk):
        bl = range(b0, b1); n = 8 * (b1 - b0)
        def keys(s): return [(s, b) for b in bl]
        gain = T.A[:, b0:b1, :, 10 + t]; gk = keys("A")
        if b0 == 0: vec("tt", 32, tk + ["PY"], gk, lambda: (gain, ends, T.PY[:, :], ALU.min))
        elif t < 2: vec("cp", n, tk, gk, lambda: (gain, ends))
        else: gain = ends; gk = tk
        if t == 2: return output(2, b0, b1, gain, gk)
        job = newjob("b"); w = wcol(b0)
        turn([(lambda p, i=b - b0: p[:, i, :, :], T.A[:, b, :, :]) for b in bl], ["ID"] + gk, job, ID)
        move(16 * n, [], [wkey(t + 1, b) for b in bl], lambda: (win(t + 1)[:, w:w + 16 * n], ps(job)[:, 0:b1 - b0, :, :]), job, 0.5)
        if b0 == 0: send(t + 1)
        c = slice(8 * b0, 8 * b1)
        vec("ts", n, gk, keys("T1"), lambda: (T.T1[:, c], gain, THR, None, lt))
        vec("tt", 2 * n, gk + keys("T1"), keys("T2"), lambda: (T.T2[:, c], T.T1[:, c], gain, ALU.mult))
        vec("tt", 2 * n, keys("T2") + keys("TOP"), keys("TOP"), lambda: (T.TOP[:, c], T.TOP[:, c], T.T2[:, c], ALU.max))
        tops(t + 1, b0)

    def affine(n, rd, wr, args, scale, bias, job=None):
        def fn(e, q):
            o, i = args()
            return [q.tensor_scalar(o, i, scale, bias, ALU.mult, ALU.add) if e == "V" else q.activation(o, i, ACT.Identity, bias=bias, scale=scale)]
        op("VS", {"V": vt(n), "S": st(n)}, fn, rd, wr, job)

    def output(t, b0, b1, gain, gk):
        n = 8 * (b1 - b0); c = slice(64 * t + 8 * b0, 64 * t + 8 * b1); k = nout[0]; nout[0] += 1
        ln(n, gk, [("LG", k)], lambda: (T.LG[:, c], gain))
        affine(n, [("LG", k)], [("GF", k)], lambda: (T.GF[:, c], T.LG[:, c]), STEP, MAGIC)
        job = newjob("d")
        turn([(lambda p: p[0:n, 0:128], T.GF[:, c])], ["IDF", ("GF", k)], job, T.IDF[:, :], 4)
        affine(128, [], [("FO", k)], lambda: (T.FO[0:n, 128 * k:128 * k + 128], ps(job)[0:n, 0:128]), 1.0, -MAGIC, job)
        for b in range(b0, b1):
            dma("YS"[b % 2] if t == 2 else "Y", T.yp[10 + t:128:16, 128 * b:128 * b + 128], T.FO[8 * (b - b0):8 * (b - b0) + 8, 128 * k:128 * k + 128],
                [("FO", k), "yp"], [], kind="fin")

    rnd[0] = 1
    loads(0, 0, V); loads(0, V, X)
    for P in range(4):
        job = newjob("d"); E = T.GL0; e = V * P
        mm([(lambda p: p[:, 0:128], shift(0, 0), E[:, e:e + 128], True, False, 128), (lambda p: p[:, 0:128], shift(1, 10), E[:, e + 128:e + 256], False, True, 128)]
           + [(lambda p: p[:, 128:160], shift(2, 4 * x - 6), E[:, e + 128 + x:e + 256:4], x == 0, x == 3, 32) for x in range(4)],
           [("GL", 0, P), ("PM", 0), ("PM", 1), ("PM", 2)], job)
        c = slice(160 * P, 160 * P + 160)
        ln(160, [], [("LN", P)], lambda job=job, c=c: (T.LN[:, c], ps(job)[:, 0:160]), job)
        vec("ts", 160, [("LN", P)], [("O", P)], lambda c=c: (T.O[:, c], T.LN[:, c], STEP, float(M), ALU.mult, ALU.min))
        places(0, P); members(0, P)
    for b in range(8):
        for (i0, i1, key) in ((0, 8, "Sa"), (8, 12, "Sb")):
            job = newjob("b"); rd = ["ID"]; items = []
            for i in range(i0, i1):
                a, k = source(0, b, i); rd += k; items.append((lambda p, x=i - i0: p[:, :, x, :], a))
            turn(items, rd, job, ID)
            move(80 * (i1 - i0), [], [(key, b)], lambda job=job, b=b, i0=i0, i1=i1: (T.SS[:, b, :, 10 * i0:10 * i1], ps(job)[:, :, 0:i1 - i0, 0:10]), job, 0.5)
    tops(0, 0); stores(0)
    for r in PAIRS: first(0, *r)
    output(0, 0, 8, T.A[:, :, :, 10], [("A", b) for b in range(8)])

    rnd[0] = 2
    first(1, 0, 2)
    for (v0, v1) in LOADS[1]:
        loads(1, v0, v1); gained(1, v0, v1)
    for P in range(4): places(1, P)
    members(1, 0); named("GA", 1, 1, 0, V)
    stores(1); later(1, 0, 2, 1)
    for r in PAIRS[1:]: first(1, *r)
    for P in (1, 2, 3, 0):
        members(2, P); named("GB", 1, 2, V * P, V * P + V)
    for r in PAIRS[1:]: later(1, r[0], r[1], 2)
    for r in PAIRS: first(2, *r)
    output(1, 0, 8, T.A[:, :, :, 11], [("A", b) for b in range(8)])

    rnd[0] = 3
    for r in PAIRS: later(2, r[0], r[1], 2)
    for (v0, v1) in LOADS[2]:
        loads(2, v0, v1); gained(2, v0, v1); named("GN", 2, 2, v0, v1)
    for P in range(4): places(2, P)
    stores(2)
    for r in PAIRS: later(3, r[0], r[1], 2)
    return ops


def order(ops):
    if ORDER:
        v = [SIGNS.index(ORDER[k]) * 62 + SIGNS.index(ORDER[k + 1]) for k in range(0, len(ORDER), 2)]
    else:
        v = [2 * i for i in range(len(ops))]
    free = {s: [[k, None] for k in range(BANKS[s])] for s in BANKS}
    seq = []
    for x in v:
        i = x // 2; o = ops[i]; job = o["job"]
        o["on"] = "VS"[x % 2] if o["eng"] == "VS" else o["eng"]
        if job is not None:
            if job[1][0] == i:
                job[2], last = free[job[3]].pop(0)
                if last is not None: o["deps"][last] = True
            if job[1][-1] == i: free[job[3]].append([job[2], i])
        seq.append(i)
    return seq


def rank_program(g, core, T, topo):
    rank = T.rank_of(core)
    if rank is None:
        return
    ops = plan(T, topo, rank, core)
    seq = order(ops)
    queue = {"V": g.vector, "S": g.scalar, "P": g.tensor, "G": g, "Y": g.sync}
    csem = {"V": "cv", "S": "cs", "P": "cp", "G": "cg"}
    count = {}
    waited = {e: {} for e in queue}
    ndma = 0
    nin = len(topo.engines(core, T.cores[(rank + 1) % N]))
    for i in seq:
        o = ops[i]; e = o["on"]; q = queue[e]
        need = {}
        for d in o["deps"]:
            p = ops[d]
            if e == "P" and p["on"] == "P": continue
            s, v = p["sig"]
            need[s] = max(need.get(s, 0), v)
        for s, v in need.items():
            if waited[e].get(s, 0) < v:
                q.wait_ge(T.sem[s], v); waited[e][s] = v
        ins = o["fn"](e, q)
        if o["kind"] == "c":
            s = csem[e]
            for x in ins:
                x.then_inc(T.sem[s], 1); count[s] = count.get(s, 0) + 1
            o["sig"] = (s, count[s])
        elif o["kind"] == "dma":
            s = "dm%d" % ndma; ndma += 1
            ins[0].then_inc(T.sem[s], 16); count[s] = 16; o["sig"] = (s, 16)
        elif o["kind"] == "fin":
            ins[0].then_inc(T.sem.fin, 16); count["fin"] = count.get("fin", 0) + 16
        else:
            t = o["kind"][1]
            o["sig"] = ("arr%d" % t, nin); count["arr%d" % t] = nin; count["snt%d" % t] = nin
    for s, v in count.items():
        if waited["G"].get(s, 0) < v: g.wait_ge(T.sem[s], v)
